import numpy as np
import ml_dtypes


def mxq(x, axis, fmt="e4m3"):
    dtype, down = {"e4m3": (ml_dtypes.float8_e4m3fn, 7), "e5m2": (ml_dtypes.float8_e5m2, 14)}[fmt]
    v = np.moveaxis(np.asarray(x, np.float32).astype(ml_dtypes.bfloat16).astype(np.float64), axis, -1)
    blocks = v.reshape(v.shape[:-1] + (-1, 32))
    amax = np.abs(blocks).max(-1, keepdims=True)
    byte = np.maximum(np.where(amax > 0, np.frexp(amax)[1] - 1 + 127, 0) - down, 1)
    scale = np.exp2(byte - 127.0)
    codes = (blocks / scale).astype(np.float32).astype(dtype).astype(np.float64)
    return np.moveaxis((codes * scale).reshape(v.shape), -1, axis)


WIDE = False


def mx_kscale(k):
    if not WIDE:
        return np.ones(k)
    levels = np.array([10, -10, 5, -5, 0])
    if k % 512:
        return np.exp2(np.random.permutation(np.resize(levels, k // 32))).repeat(32)
    a = np.empty((k // 512, 16))
    for p in range(k // 512):
        a[p, :8] = np.random.permutation(np.resize(levels, 8))
        for g in range(8):
            far = levels[np.abs(levels - a[p, g]) >= 10]
            a[p, g + 8] = far[np.random.randint(len(far))]
    return np.exp2(a.ravel()).repeat(32)


def f64(x):
    return np.asarray(x).astype(np.float64)


def striped(idx):
    return np.tile(idx.reshape(-1, 16).T, (8, 1)).astype(np.uint16)


def unstriped(offs):
    return offs[:16].T.reshape(-1).astype(np.int64)


E2M1 = np.array([0.0, 0.5, 1.0, 1.5, 2.0, 3.0, 4.0, 6.0, -0.0, -0.5, -1.0, -1.5, -2.0, -3.0, -4.0, -6.0])


def pack_weight(w, fmt):
    k, n = w.shape
    w = f64(np.asarray(w, np.float32).astype(ml_dtypes.bfloat16)).reshape(k // 32, 32, n)
    amax = np.abs(w).max(1)
    if fmt == "e4m3":
        byte = np.frexp(amax)[1] - 1 + 127 - 7
    else:
        mant, ex = np.frexp(amax / 6.0)
        byte = np.where(mant > 0.5, ex, ex - 1) + 127
    byte = np.clip(np.where(amax > 0, byte, 1), 1, 254)
    scaled = (w * np.exp2(127.0 - byte)[:, None, :]).reshape(k, n).astype(np.float32)
    by_word = np.ascontiguousarray(scaled.reshape(k // 512, 128, 4, n).transpose(0, 1, 3, 2))
    if fmt == "e4m3":
        words = by_word.astype(ml_dtypes.float8_e4m3fn).view(np.uint8)
    else:
        c = by_word.astype(ml_dtypes.float4_e2m1fn).view(np.uint8) & 0xF
        words = (c[..., 0::2] | (c[..., 1::2] << 4)).reshape(k // 512, 128, 2 * n)
    return np.ascontiguousarray(words), np.ascontiguousarray(byte.astype(np.uint8).reshape(k // 512, 16, n))


def unpack_weight(words, scales, fmt):
    g, _, n = scales.shape
    words = np.ascontiguousarray(words).reshape(g, 128, n, -1)
    if fmt == "e4m3":
        vals = words.view(ml_dtypes.float8_e4m3fn).astype(np.float64)
    else:
        nib = np.empty((g, 128, n, 4), np.uint8)
        nib[..., 0::2] = words & 0xF
        nib[..., 1::2] = words >> 4
        vals = E2M1[nib]
    vals = vals * np.repeat(np.exp2(scales.astype(np.float64) - 127.0), 8, axis=1)[..., None]
    return vals.transpose(0, 1, 3, 2).reshape(g * 512, n)


def gelu(v):
    return 0.5 * v * (1.0 + np.tanh(np.sqrt(2.0 / np.pi) * (v + 0.044715 * v**3)))


K, T, S, H, T2, N, P = 1024, 4096, 1024, 512, 2048, 512, 128

def setup_inputs():
    n = np.random.standard_normal
    s = mx_kscale(K)[:, None]
    u = mx_kscale(H)[:, None]
    tab_words, tab_scales = pack_weight(n((K, T)) * s, "e4m3")
    wp_words, wp_scales = pack_weight(n((H, N)) / np.sqrt(H) / u, "e2m1")
    return {
        "tab_words": tab_words,
        "tab_scales": tab_scales,
        "offs": striped(np.random.permutation(T)[:S]),
        "wx": (n((K, H)) / np.sqrt(K) / s * u.T).astype(np.float32),
        "wy": (n((K, H)) / np.sqrt(K) / s * u.T).astype(np.float32),
        "wgs": np.exp(0.3 * n((P, S))).astype(np.float32),
        "offs2": striped(np.random.permutation(T2)[:S]),
        "old": (np.abs(n((H, T2))) * u).astype(np.float32),
        "wp_words": wp_words,
        "wp_scales": wp_scales,
    }

def reference(tab_words, tab_scales, offs, wx, wy, wgs, offs2, old, wp_words, wp_scales):
    v = unpack_weight(tab_words, tab_scales, "e4m3")[:, unstriped(offs)]
    a = mxq(f64(wx), 0, "e4m3").T @ v
    b = mxq(f64(wy), 0, "e4m3").T @ v
    h = np.sqrt(a * a + b * b)
    page = np.zeros((H, T2))
    page[:, unstriped(offs2)] = np.tile(f64(wgs), (H // P, 1)) * h
    z = mxq(f64(old) - page, 0, "e4m3")
    wp = unpack_weight(wp_words, wp_scales, "e2m1")
    return wp.T @ z

@@ -1,0 +1,305 @@
+from contextlib import ExitStack
+
+import concourse.mybir as mybir
+from concourse.masks import make_identity
+
+K, T, S, H, T2, N, P = 1024, 4096, 1024, 512, 2048, 512, 128
+FLOPS = 2 * (2 * K * H * S + H * N * T2)
+
+F32 = mybir.dt.float32
+BF16 = mybir.dt.bfloat16
+I32 = mybir.dt.int32
+U32 = mybir.dt.uint32
+U16 = mybir.dt.uint16
+U8 = mybir.dt.uint8
+FP8X4 = mybir.dt.float8_e4m3fn_x4
+FP4X4 = mybir.dt.float4_e2m1fn_x4
+ACT = mybir.ActivationFunctionType
+MULT = mybir.AluOpType.mult
+
+PACK = 4
+PASSES = K // (P * PACK)
+SLICES = H // P
+BANK = 512
+HALVES = S // BANK
+CHUNKS = T2 // BANK
+LIST_COLS = BANK // 16
+
+
+def tile_list_particle_cell_pressure_kernel(
+    tc, tab_words, tab_scales, offs, wx, wy, wgs, offs2, old, wp_words, wp_scales, out
+):
+    nc = tc.nc
+    with ExitStack() as ctx:
+        keep = ctx.enter_context(tc.tile_pool(name="keep", bufs=1))
+        ring = ctx.enter_context(tc.tile_pool(name="ring", bufs=2))
+        psum = ctx.enter_context(tc.psum_pool(name="psum", bufs=1))
+
+        def bank(b):
+            return psum.tile([P, BANK], F32, name="bank%d" % b, tag="bank%d" % b)
+
+        one = keep.tile([P, 8], F32, name="one")
+        nc.gpsimd.memset(one[:], 1.0)
+        warm = keep.tile([P, 8], F32, name="warm")
+        nc.scalar.activation(warm[:], one[:], ACT.Sqrt)
+
+        tab_sc = keep.tile([P, T], U8, name="tab_sc", align_bytes=64)
+        nc.vector.memset(tab_sc[:].bitcast(I32), 0)
+        pages = [keep.tile([P, T2], F32, name="page%d" % t) for t in range(SLICES)]
+        ident = keep.tile([P, P], F32, name="ident")
+        make_identity(nc, ident[:])
+        for t in range(SLICES):
+            (nc.vector if t < 2 else nc.gpsimd).memset(pages[t][:], 0.0)
+
+        idx = keep.tile([P, S // 16], U16, name="idx")
+        nc.sync.dma_start(idx[:], offs)
+        for q in range(4):
+            nc.scalar.dma_start(
+                tab_sc[32 * q : 32 * q + 4 * PASSES, :].bitcast(I32),
+                tab_scales[:, 4 * q : 4 * q + 4, :].bitcast(I32),
+            )
+
+        w_raw = {}
+
+        def load_w(t, pool):
+            for a in range(PASSES):
+                for m, w in enumerate((wx, wy)):
+                    name = "w_raw%d_%d_%d" % (t, a, m)
+                    if (t, a, m) == (0, 0, 0):
+                        raw = keep.tile([P, PACK, P], F32, name=name, tag="tab1", align_bytes=64)
+                    else:
+                        raw = pool.tile([P, PACK, P], F32, name=name, tag=name)
+                    rows = w[a * P * PACK : (a + 1) * P * PACK, t * P : (t + 1) * P]
+                    nc.sync.dma_start(raw[:], rows.rearrange("(p i) c -> p i c", i=PACK))
+                    w_raw[t, a, m] = raw
+
+        wgs_sb = []
+
+        def load_wgs(h):
+            g = late.tile([P, BANK], F32, name="wgs%d" % h)
+            nc.sync.dma_start(g[:], wgs[:, h * BANK : (h + 1) * BANK])
+            wgs_sb.append(g)
+
+        old_sb = []
+
+        def load_old(t):
+            o = late.tile([P, T2], F32, name="old%d" % t)
+            nc.sync.dma_start(o[:], old[t * P : (t + 1) * P, :])
+            old_sb.append(o)
+
+        w_q = {}
+
+        def quantise_w(t):
+            for a in range(PASSES):
+                wb = ring.tile([P, 2 * P, PACK], BF16, name="w_bf", tag="w_bf", bufs=4, align_bytes=64)
+                for m in range(2):
+                    nc.scalar.copy(
+                        wb[:, m * P : (m + 1) * P, :].rearrange("p (g c) i -> p g i c", c=4),
+                        w_raw[t, a, m][:].rearrange("p i (g c) -> p g i c", c=4),
+                    )
+                codes = ring.tile([P, 2 * P], U32, name="w_codes", tag="w_codes", bufs=4, align_bytes=64)
+                scales = ring.tile([P, 2 * P], U8, name="w_scales", tag="w_scales", bufs=4, align_bytes=64)
+                nc.vector.quantize_mx(
+                    out=codes[:].bitcast(FP8X4), scales=scales[:], in_=wb[:].rearrange("p c i -> p (c i)")
+                )
+                w_q[t, a] = (codes, scales)
+
+        tab = []
+
+        def load_tab(a):
+            words = keep.tile([P, T], I32, name="tab%d" % a, tag="tab%d" % a, align_bytes=64)
+            nc.sync.dma_start(words[:], tab_words[a].rearrange("p t i -> p (t i)").bitcast(I32))
+            tab.append(words)
+
+        with tc.tile_pool(name="early", bufs=1) as early:
+            load_w(0, early)
+            load_tab(0)
+            idx2 = keep.tile([P, S // 16], U16, name="idx2")
+            nc.sync.dma_start(idx2[:], offs2)
+            quantise_w(0)
+        load_tab(1)
+        late = ctx.enter_context(tc.tile_pool(name="late", bufs=1))
+        load_wgs(0)
+        load_w(1, late)
+        load_wgs(1)
+        load_w(2, late)
+        load_old(0)
+        load_w(3, late)
+        for t in range(1, SLICES):
+            load_old(t)
+        wp_w = late.tile([P, 2 * N], U8, name="wp_w", align_bytes=64)
+        nc.sync.dma_start(wp_w[:].bitcast(I32), wp_words[0].bitcast(I32))
+        wp_sc = late.tile([P, N], U8, name="wp_sc", align_bytes=64)
+        nc.vector.memset(wp_sc[:].bitcast(I32), 0)
+        for q in range(4):
+            nc.sync.dma_start(
+                wp_sc[32 * q : 32 * q + 4, :].bitcast(I32),
+                wp_scales[0, 4 * q : 4 * q + 4, :].bitcast(I32),
+            )
+
+        v_sc = keep.tile([P, S], U8, name="v_sc", align_bytes=64)
+        nc.vector.tensor_copy(v_sc[:], tab_sc[:].indirect(idx[:]))
+        v_w = {}
+        for a in range(PASSES):
+            for h in range(HALVES):
+                g = keep.tile([P, BANK], U32, name="v%d_%d" % (a, h), align_bytes=64)
+                nc.vector.tensor_copy(
+                    g[:], tab[a][:].bitcast(U32).indirect(idx[:, h * LIST_COLS : (h + 1) * LIST_COLS])
+                )
+                v_w[a, h] = g
+
+        neg_wgs = []
+        for h in range(HALVES):
+            g = keep.tile([P, BANK], F32, name="neg_wgs%d" % h)
+            nc.scalar.activation(g[:], wgs_sb[h][:], ACT.Copy, scale=-1.0)
+            neg_wgs.append(g)
+
+        def speeds(t, h, pieces):
+            for sum_bank, tag, ds in pieces:
+                total = bank(sum_bank)
+                width = 2 * P * len(ds)
+                for d in ds:
+                    acc = bank(2 * h + d)
+                    for a in range(PASSES):
+                        codes, scales = w_q[t, a]
+                        for e in range(2):
+                            jb = 2 * d + e
+                            j0 = h * BANK + jb * P
+                            nc.tensor.matmul_mx(
+                                out=acc[:, e * 2 * P : (e + 1) * 2 * P],
+                                lhsT=v_w[a, h][:, jb * P : (jb + 1) * P].bitcast(FP8X4),
+                                lhsT_scale=v_sc[4 * a : P, j0 : j0 + P],
+                                rhs=codes[:].bitcast(FP8X4),
+                                rhs_scale=scales[:],
+                                start=(a == 0 and e == 0),
+                                stop=(a == PASSES - 1 and e == 1),
+                            )
+                    sq = ring.tile([P, BANK], F32, name="sq", tag="sq", bufs=4)
+                    nc.scalar.activation(sq[:], acc[:], ACT.Square)
+                    for e in range(2):
+                        o0 = (2 * (d - ds[0]) + e) * P
+                        for m in range(2):
+                            c0 = (2 * e + m) * P
+                            nc.tensor.matmul(
+                                total[:, o0 : o0 + P],
+                                sq[:, c0 : c0 + P],
+                                ident[:],
+                                start=(m == 0),
+                                stop=(m == 1),
+                                is_transpose=True,
+                            )
+                speed = late.tile([P, width], F32, name="speed", tag=tag)
+                nc.scalar.activation(speed[:], total[:, 0:width], ACT.Sqrt)
+                j0 = 2 * P * ds[0]
+                l0 = (h * BANK + j0) // 16
+                nc.vector.tensor_tensor(
+                    pages[t][:].indirect(idx2[:, l0 : l0 + width // 16]),
+                    speed[:],
+                    neg_wgs[h][:, j0 : j0 + width],
+                    MULT,
+                )
+
+        z_t = [keep.tile([P, 4, 2, P, 2], BF16, name="z_t%d" % q) for q in range(CHUNKS)]
+
+        def turn_into(acc, src, q, first, last):
+            for cb in range(4):
+                c0 = q * BANK + cb * P
+                nc.tensor.matmul(
+                    acc[:, cb * P : (cb + 1) * P],
+                    src[:, c0 : c0 + P],
+                    ident[:],
+                    start=(first and cb == 0),
+                    stop=(last and cb == 3),
+                    is_transpose=True,
+                )
+
+        def close_loss(acc, t, q, copy):
+            turn_into(acc, pages[t], q, False, True)
+            copy(
+                z_t[q][:, :, :, 32 * t : 32 * (t + 1), :],
+                acc[:].rearrange("c (cb p u e) -> c cb u p e", cb=4, u=2, e=2),
+            )
+
+        def loss(t):
+            for q in range(CHUNKS):
+                acc = bank(q)
+                turn_into(acc, old_sb[t], q, True, False)
+                close_loss(acc, t, q, nc.scalar.copy)
+
+        last = SLICES - 1
+        for t in range(SLICES):
+            if t == last:
+                loss(0)
+            if t == 0:
+                speeds(t, 0, [(4, "speed_first", [0]), (6, "speed0", [1])])
+            else:
+                speeds(t, 0, [(4, "speed%d" % t, [0, 1])])
+            if t < last:
+                quantise_w(t + 1)
+                speeds(t, 1, [(5, "w_raw%d_%d_%d" % (t + 1, PASSES - 1, 1), [0, 1])])
+            else:
+                speeds(t, 1, [(5, "speed_last", [0, 1])])
+        for t in range(1, last):
+            loss(t)
+        open_loss = []
+        for q in range(CHUNKS):
+            acc = bank(q)
+            turn_into(acc, old_sb[last], q, True, False)
+            open_loss.append(acc)
+
+        z_q = {}
+
+        def quantise_z(q):
+            words = z_t[q][:].rearrange("c cb u p e -> c (cb u p e)").bitcast(F32)
+            z_bf = ring.tile([P, BANK, PACK], BF16, name="z_bf", tag="z_bf", align_bytes=64)
+            z_words = z_bf[:].rearrange("p c i -> p (c i)").bitcast(F32)
+            for d in range(2):
+                turned = bank(4 + d)
+                for k in range(4):
+                    w0 = (4 * d + k) * P
+                    nc.tensor.transpose(turned[:, k * P : (k + 1) * P], words[:, w0 : w0 + P], ident[:])
+                dst = z_words[:, d * BANK : (d + 1) * BANK].rearrange("p (cb c u) -> p cb c u", cb=2, u=2)
+                src = turned[:].rearrange("p (cb u c) -> p cb c u", cb=2, u=2)
+                if d == 0:
+                    nc.scalar.copy(dst, src)
+                else:
+                    nc.vector.tensor_copy(dst, src)
+            z_codes = ring.tile([P, BANK], U32, name="z_codes", tag="z_codes", align_bytes=64)
+            z_scales = ring.tile([P, BANK], U8, name="z_scales", tag="z_scales", align_bytes=64)
+            nc.vector.quantize_mx(
+                out=z_codes[:].bitcast(FP8X4), scales=z_scales[:], in_=z_bf[:].rearrange("p c i -> p (c i)")
+            )
+            z_q[q] = (z_codes, z_scales)
+
+        out_banks = (6, 7, 0, 1, 2, 3)
+
+        def pressure(q):
+            z_codes, z_scales = z_q[q]
+            for nb in range(N // P):
+                acc = bank(out_banks[(4 * q + nb) % len(out_banks)])
+                nc.tensor.matmul_mx(
+                    out=acc[:],
+                    lhsT=wp_w[:, 2 * nb * P : 2 * (nb + 1) * P].bitcast(FP4X4),
+                    lhsT_scale=wp_sc[:, nb * P : (nb + 1) * P],
+                    rhs=z_codes[:].bitcast(FP8X4),
+                    rhs_scale=z_scales[:],
+                    start=True,
+                    stop=True,
+                )
+                res = ring.tile([P, BANK], F32, name="res", tag="res", bufs=8)
+                if nb % 2 == 0:
+                    nc.scalar.copy(res[:], acc[:])
+                else:
+                    nc.vector.tensor_copy(res[:], acc[:])
+                nc.sync.dma_start(out[nb * P : (nb + 1) * P, q * BANK : (q + 1) * BANK], res[:])
+
+        copies = (nc.scalar.copy, nc.vector.tensor_copy)
+        close_loss(open_loss[0], last, 0, copies[0])
+        close_loss(open_loss[1], last, 1, copies[1])
+        quantise_z(0)
+        close_loss(open_loss[2], last, 2, copies[0])
+        close_loss(open_loss[3], last, 3, copies[1])
+        for q in range(CHUNKS):
+            if q + 1 < CHUNKS:
+                quantise_z(q + 1)
+            pressure(q)

@@ -16,13 +16,16 @@ FP8X4 = mybir.dt.float8_e4m3fn_x4
 FP4X4 = mybir.dt.float4_e2m1fn_x4
 ACT = mybir.ActivationFunctionType
 MULT = mybir.AluOpType.mult
+ADD = mybir.AluOpType.add
 
 PACK = 4
 PASSES = K // (P * PACK)
 SLICES = H // P
 BANK = 512
 HALVES = S // BANK
-CHUNKS = T2 // BANK
+CHUNKS = ((0, 2), (2, 4), (6, 4), (10, 4), (14, 2))
+LOSS_BANKS = (0, 1, 2, 3, 7)
+OUT_BANKS = (6, 0, 1, 2, 3, 7)
 LIST_COLS = BANK // 16
 
 
@@ -43,35 +46,36 @@ def tile_list_particle_cell_pressure_kernel(
         warm = keep.tile([P, 8], F32, name="warm")
         nc.scalar.activation(warm[:], one[:], ACT.Sqrt)
 
-        tab_sc = keep.tile([P, T], U8, name="tab_sc", align_bytes=64)
+        tab_sc = keep.tile([P, T], U8, name="tab_sc", tag="tab_sc", align_bytes=64)
         nc.vector.memset(tab_sc[:].bitcast(I32), 0)
-        pages = [keep.tile([P, T2], F32, name="page%d" % t) for t in range(SLICES)]
+        pages = [keep.tile([P, T2], F32, name="page%d" % t) for t in range(2)]
         ident = keep.tile([P, P], F32, name="ident")
         make_identity(nc, ident[:])
-        for t in range(SLICES):
-            (nc.vector if t < 2 else nc.gpsimd).memset(pages[t][:], 0.0)
+        for t in range(2):
+            nc.vector.memset(pages[t][:], 0.0)
 
         idx = keep.tile([P, S // 16], U16, name="idx")
         nc.sync.dma_start(idx[:], offs)
         for q in range(4):
-            nc.scalar.dma_start(
+            nc.gpsimd.dma_start(
                 tab_sc[32 * q : 32 * q + 4 * PASSES, :].bitcast(I32),
                 tab_scales[:, 4 * q : 4 * q + 4, :].bitcast(I32),
             )
 
         w_raw = {}
 
-        def load_w(t, pool):
+        def load_w(t0, count, pool):
             for a in range(PASSES):
                 for m, w in enumerate((wx, wy)):
-                    name = "w_raw%d_%d_%d" % (t, a, m)
-                    if (t, a, m) == (0, 0, 0):
-                        raw = keep.tile([P, PACK, P], F32, name=name, tag="tab1", align_bytes=64)
+                    name = "w_raw%d_%d_%d" % (t0, a, m)
+                    if (t0, a, m) == (0, 0, 0):
+                        raw = keep.tile([P, PACK, count * P], F32, name=name, tag="tab1", align_bytes=64)
                     else:
-                        raw = pool.tile([P, PACK, P], F32, name=name, tag=name)
-                    rows = w[a * P * PACK : (a + 1) * P * PACK, t * P : (t + 1) * P]
+                        raw = pool.tile([P, PACK, count * P], F32, name=name, tag=name)
+                    rows = w[a * P * PACK : (a + 1) * P * PACK, t0 * P : (t0 + count) * P]
                     nc.sync.dma_start(raw[:], rows.rearrange("(p i) c -> p i c", i=PACK))
-                    w_raw[t, a, m] = raw
+                    for k in range(count):
+                        w_raw[t0 + k, a, m] = raw[:, :, k * P : (k + 1) * P]
 
         wgs_sb = []
 
@@ -80,29 +84,29 @@ def tile_list_particle_cell_pressure_kernel(
             nc.sync.dma_start(g[:], wgs[:, h * BANK : (h + 1) * BANK])
             wgs_sb.append(g)
 
-        old_sb = []
+        old_sb = {}
 
         def load_old(t):
             o = late.tile([P, T2], F32, name="old%d" % t)
             nc.sync.dma_start(o[:], old[t * P : (t + 1) * P, :])
-            old_sb.append(o)
+            old_sb[t] = o
 
         w_q = {}
 
         def quantise_w(t):
+            wb = ring.tile([P, PASSES, 2, P, PACK], BF16, name="w_bf", tag="w_bf", align_bytes=64)
             for a in range(PASSES):
-                wb = ring.tile([P, 2 * P, PACK], BF16, name="w_bf", tag="w_bf", bufs=4, align_bytes=64)
                 for m in range(2):
                     nc.scalar.copy(
-                        wb[:, m * P : (m + 1) * P, :].rearrange("p (g c) i -> p g i c", c=4),
-                        w_raw[t, a, m][:].rearrange("p i (g c) -> p g i c", c=4),
+                        wb[:, a, m].rearrange("p (g c) i -> p g i c", c=4),
+                        w_raw[t, a, m].rearrange("p i (g c) -> p g i c", c=4),
                     )
-                codes = ring.tile([P, 2 * P], U32, name="w_codes", tag="w_codes", bufs=4, align_bytes=64)
-                scales = ring.tile([P, 2 * P], U8, name="w_scales", tag="w_scales", bufs=4, align_bytes=64)
-                nc.vector.quantize_mx(
-                    out=codes[:].bitcast(FP8X4), scales=scales[:], in_=wb[:].rearrange("p c i -> p (c i)")
-                )
-                w_q[t, a] = (codes, scales)
+            codes = ring.tile([P, PASSES * 2 * P], U32, name="w_codes", tag="w_codes", bufs=SLICES, align_bytes=64)
+            scales = ring.tile([P, PASSES * 2 * P], U8, name="w_scales", tag="w_scales", bufs=SLICES, align_bytes=64)
+            nc.vector.quantize_mx(
+                out=codes[:].bitcast(FP8X4), scales=scales[:], in_=wb[:].rearrange("p a m c i -> p (a m c i)")
+            )
+            w_q[t] = (codes, scales)
 
         tab = []
 
@@ -112,20 +116,23 @@ def tile_list_particle_cell_pressure_kernel(
             tab.append(words)
 
         with tc.tile_pool(name="early", bufs=1) as early:
-            load_w(0, early)
+            load_w(0, 2, early)
             load_tab(0)
             idx2 = keep.tile([P, S // 16], U16, name="idx2")
             nc.sync.dma_start(idx2[:], offs2)
             quantise_w(0)
+            quantise_w(1)
         load_tab(1)
         late = ctx.enter_context(tc.tile_pool(name="late", bufs=1))
+        for t in range(2, SLICES):
+            page = late.tile([P, T2], F32, name="page%d" % t)
+            nc.gpsimd.memset(page[:], 0.0)
+            pages.append(page)
         load_wgs(0)
-        load_w(1, late)
         load_wgs(1)
-        load_w(2, late)
-        load_old(0)
-        load_w(3, late)
-        for t in range(1, SLICES):
+        load_w(2, 1, late)
+        load_w(3, 1, late)
+        for t in (1, 0, 2, 3):
             load_old(t)
         wp_w = late.tile([P, 2 * N], U8, name="wp_w", align_bytes=64)
         nc.sync.dma_start(wp_w[:].bitcast(I32), wp_words[0].bitcast(I32))
@@ -142,7 +149,9 @@ def tile_list_particle_cell_pressure_kernel(
         v_w = {}
         for a in range(PASSES):
             for h in range(HALVES):
-                g = keep.tile([P, BANK], U32, name="v%d_%d" % (a, h), align_bytes=64)
+                name = "v%d_%d" % (a, h)
+                tag = "tab_sc" if (a, h) == (1, 0) else name
+                g = keep.tile([P, BANK], U32, name=name, tag=tag, align_bytes=64)
                 nc.vector.tensor_copy(
                     g[:], tab[a][:].bitcast(U32).indirect(idx[:, h * LIST_COLS : (h + 1) * LIST_COLS])
                 )
@@ -154,152 +163,191 @@ def tile_list_particle_cell_pressure_kernel(
             nc.scalar.activation(g[:], wgs_sb[h][:], ACT.Copy, scale=-1.0)
             neg_wgs.append(g)
 
-        def speeds(t, h, pieces):
-            for sum_bank, tag, ds in pieces:
-                total = bank(sum_bank)
-                width = 2 * P * len(ds)
-                for d in ds:
-                    acc = bank(2 * h + d)
-                    for a in range(PASSES):
-                        codes, scales = w_q[t, a]
-                        for e in range(2):
-                            jb = 2 * d + e
-                            j0 = h * BANK + jb * P
-                            nc.tensor.matmul_mx(
-                                out=acc[:, e * 2 * P : (e + 1) * 2 * P],
-                                lhsT=v_w[a, h][:, jb * P : (jb + 1) * P].bitcast(FP8X4),
-                                lhsT_scale=v_sc[4 * a : P, j0 : j0 + P],
-                                rhs=codes[:].bitcast(FP8X4),
-                                rhs_scale=scales[:],
-                                start=(a == 0 and e == 0),
-                                stop=(a == PASSES - 1 and e == 1),
-                            )
-                    sq = ring.tile([P, BANK], F32, name="sq", tag="sq", bufs=4)
-                    nc.scalar.activation(sq[:], acc[:], ACT.Square)
+        def place(t, j0, speed):
+            width = speed.shape[1]
+            h, c0 = divmod(j0, BANK)
+            nc.vector.tensor_tensor(
+                pages[t][:].indirect(idx2[:, j0 // 16 : (j0 + width) // 16]),
+                speed[:],
+                neg_wgs[h][:, c0 : c0 + width],
+                MULT,
+            )
+
+        def first_speeds():
+            width = 2 * P
+            acc = bank(0)
+            codes, scales = w_q[0]
+            for a in range(PASSES):
+                for m in range(2):
+                    cols = slice((2 * a + m) * P, (2 * a + m + 1) * P)
+                    nc.tensor.matmul_mx(
+                        out=acc[:, m * width : (m + 1) * width],
+                        lhsT=codes[:, cols].bitcast(FP8X4),
+                        lhsT_scale=scales[:, cols],
+                        rhs=v_w[a, 0][:, 0:width].bitcast(FP8X4),
+                        rhs_scale=v_sc[4 * a : P, 0:width],
+                        start=(a == 0 and m == 0),
+                        stop=(a == PASSES - 1 and m == 1),
+                    )
+            sq = ring.tile([P, BANK], F32, name="sq", tag="sq", bufs=4)
+            nc.scalar.activation(sq[:], acc[:], ACT.Square)
+            total = late.tile([P, width], F32, name="total_first")
+            nc.vector.tensor_tensor(total[:], sq[:, 0:width], sq[:, width : 2 * width], ADD)
+            speed = late.tile([P, width], F32, name="speed_first")
+            nc.scalar.activation(speed[:], total[:], ACT.Sqrt)
+            place(0, 0, speed)
+
+        used = []
+
+        def speeds(t, blocks, tag):
+            total = bank(4 + len(used) % 3)
+            codes, scales = w_q[t]
+            for k, block in enumerate(blocks):
+                acc = bank(block)
+                for a in range(PASSES):
+                    cols = slice(a * 2 * P, (a + 1) * 2 * P)
                     for e in range(2):
-                        o0 = (2 * (d - ds[0]) + e) * P
-                        for m in range(2):
-                            c0 = (2 * e + m) * P
-                            nc.tensor.matmul(
-                                total[:, o0 : o0 + P],
-                                sq[:, c0 : c0 + P],
-                                ident[:],
-                                start=(m == 0),
-                                stop=(m == 1),
-                                is_transpose=True,
-                            )
-                speed = late.tile([P, width], F32, name="speed", tag=tag)
-                nc.scalar.activation(speed[:], total[:, 0:width], ACT.Sqrt)
-                j0 = 2 * P * ds[0]
-                l0 = (h * BANK + j0) // 16
-                nc.vector.tensor_tensor(
-                    pages[t][:].indirect(idx2[:, l0 : l0 + width // 16]),
-                    speed[:],
-                    neg_wgs[h][:, j0 : j0 + width],
-                    MULT,
-                )
+                        j0 = (2 * block + e) * P
+                        h, c0 = divmod(j0, BANK)
+                        nc.tensor.matmul_mx(
+                            out=acc[:, e * 2 * P : (e + 1) * 2 * P],
+                            lhsT=v_w[a, h][:, c0 : c0 + P].bitcast(FP8X4),
+                            lhsT_scale=v_sc[4 * a : P, j0 : j0 + P],
+                            rhs=codes[:, cols].bitcast(FP8X4),
+                            rhs_scale=scales[:, cols],
+                            start=(a == 0 and e == 0),
+                            stop=(a == PASSES - 1 and e == 1),
+                        )
+                sq = ring.tile([P, BANK], F32, name="sq", tag="sq", bufs=4)
+                nc.scalar.activation(sq[:], acc[:], ACT.Square)
+                for e in range(2):
+                    o0 = (2 * k + e) * P
+                    for m in range(2):
+                        c0 = (2 * e + m) * P
+                        nc.tensor.matmul(
+                            total[:, o0 : o0 + P],
+                            sq[:, c0 : c0 + P],
+                            ident[:],
+                            start=(m == 0),
+                            stop=(m == 1),
+                            is_transpose=True,
+                        )
+            width = 2 * P * len(blocks)
+            speed = late.tile([P, width], F32, name="speed", tag=tag)
+            nc.scalar.activation(speed[:], total[:, 0:width], ACT.Sqrt)
+            place(t, 2 * P * blocks[0], speed)
+            used.append(total)
 
-        z_t = [keep.tile([P, 4, 2, P, 2], BF16, name="z_t%d" % q) for q in range(CHUNKS)]
+        z_t = [keep.tile([P, nb, 2, P, 2], BF16, name="z_t%d" % q) for q, (b0, nb) in enumerate(CHUNKS)]
 
-        def turn_into(acc, src, q, first, last):
-            for cb in range(4):
-                c0 = q * BANK + cb * P
+        def turn_into(acc, src, q, first, final):
+            b0, nb = CHUNKS[q]
+            for cb in range(nb):
+                c0 = (b0 + cb) * P
                 nc.tensor.matmul(
                     acc[:, cb * P : (cb + 1) * P],
                     src[:, c0 : c0 + P],
                     ident[:],
                     start=(first and cb == 0),
-                    stop=(last and cb == 3),
+                    stop=(final and cb == nb - 1),
                     is_transpose=True,
                 )
 
         def close_loss(acc, t, q, copy):
+            nb = CHUNKS[q][1]
             turn_into(acc, pages[t], q, False, True)
             copy(
                 z_t[q][:, :, :, 32 * t : 32 * (t + 1), :],
-                acc[:].rearrange("c (cb p u e) -> c cb u p e", cb=4, u=2, e=2),
+                acc[:, 0 : nb * P].rearrange("c (cb p u e) -> c cb u p e", cb=nb, u=2, e=2),
             )
 
         def loss(t):
-            for q in range(CHUNKS):
-                acc = bank(q)
+            for q in range(len(CHUNKS)):
+                acc = bank(LOSS_BANKS[q])
                 turn_into(acc, old_sb[t], q, True, False)
                 close_loss(acc, t, q, nc.scalar.copy)
 
         last = SLICES - 1
-        for t in range(SLICES):
-            if t == last:
-                loss(0)
-            if t == 0:
-                speeds(t, 0, [(4, "speed_first", [0]), (6, "speed0", [1])])
-            else:
-                speeds(t, 0, [(4, "speed%d" % t, [0, 1])])
-            if t < last:
-                quantise_w(t + 1)
-                speeds(t, 1, [(5, "w_raw%d_%d_%d" % (t + 1, PASSES - 1, 1), [0, 1])])
-            else:
-                speeds(t, 1, [(5, "speed_last", [0, 1])])
-        for t in range(1, last):
-            loss(t)
+        first_speeds()
+        speeds(0, [1], "speed0_1")
+        speeds(1, [0, 1], "speed1_0")
+        speeds(0, [2], "speed0_2")
+        quantise_w(2)
+        speeds(1, [2, 3], "w_raw2_1_1")
+        quantise_w(3)
+        speeds(0, [3], "w_raw3_1_1")
+        speeds(2, [0, 1], "speed2_0")
+        speeds(2, [2, 3], "speed2_2")
+        speeds(3, [0, 1], "speed3_0")
+        loss(1)
+        speeds(3, [2, 3], "speed3_2")
+        loss(0)
+        loss(2)
         open_loss = []
-        for q in range(CHUNKS):
-            acc = bank(q)
+        for q in range(len(CHUNKS)):
+            acc = bank(LOSS_BANKS[q])
             turn_into(acc, old_sb[last], q, True, False)
             open_loss.append(acc)
 
         z_q = {}
+        copies = (nc.scalar.copy, nc.vector.tensor_copy)
 
         def quantise_z(q):
+            nb = CHUNKS[q][1]
+            half = nb // 2
             words = z_t[q][:].rearrange("c cb u p e -> c (cb u p e)").bitcast(F32)
-            z_bf = ring.tile([P, BANK, PACK], BF16, name="z_bf", tag="z_bf", align_bytes=64)
+            z_bf = ring.tile([P, nb * P, PACK], BF16, name="z_bf", tag="z_bf", align_bytes=64)
             z_words = z_bf[:].rearrange("p c i -> p (c i)").bitcast(F32)
             for d in range(2):
                 turned = bank(4 + d)
-                for k in range(4):
-                    w0 = (4 * d + k) * P
+                for k in range(nb):
+                    w0 = (nb * d + k) * P
                     nc.tensor.transpose(turned[:, k * P : (k + 1) * P], words[:, w0 : w0 + P], ident[:])
-                dst = z_words[:, d * BANK : (d + 1) * BANK].rearrange("p (cb c u) -> p cb c u", cb=2, u=2)
-                src = turned[:].rearrange("p (cb u c) -> p cb c u", cb=2, u=2)
-                if d == 0:
-                    nc.scalar.copy(dst, src)
-                else:
-                    nc.vector.tensor_copy(dst, src)
-            z_codes = ring.tile([P, BANK], U32, name="z_codes", tag="z_codes", align_bytes=64)
-            z_scales = ring.tile([P, BANK], U8, name="z_scales", tag="z_scales", align_bytes=64)
+                dst = z_words[:, d * nb * P : (d + 1) * nb * P].rearrange("p (cb c u) -> p cb c u", cb=half, u=2)
+                src = turned[:, 0 : nb * P].rearrange("p (cb u c) -> p cb c u", cb=half, u=2)
+                copies[1 - d](dst, src)
+            z_codes = ring.tile([P, nb * P], U32, name="z_codes", tag="z_codes", align_bytes=64)
+            z_scales = ring.tile([P, nb * P], U8, name="z_scales", tag="z_scales", align_bytes=64)
             nc.vector.quantize_mx(
                 out=z_codes[:].bitcast(FP8X4), scales=z_scales[:], in_=z_bf[:].rearrange("p c i -> p (c i)")
             )
             z_q[q] = (z_codes, z_scales)
 
-        out_banks = (6, 7, 0, 1, 2, 3)
+        filled = []
 
         def pressure(q):
+            b0, nb = CHUNKS[q]
+            width = nb * P
+            per_bank = BANK // width
             z_codes, z_scales = z_q[q]
-            for nb in range(N // P):
-                acc = bank(out_banks[(4 * q + nb) % len(out_banks)])
-                nc.tensor.matmul_mx(
-                    out=acc[:],
-                    lhsT=wp_w[:, 2 * nb * P : 2 * (nb + 1) * P].bitcast(FP4X4),
-                    lhsT_scale=wp_sc[:, nb * P : (nb + 1) * P],
-                    rhs=z_codes[:].bitcast(FP8X4),
-                    rhs_scale=z_scales[:],
-                    start=True,
-                    stop=True,
-                )
-                res = ring.tile([P, BANK], F32, name="res", tag="res", bufs=8)
-                if nb % 2 == 0:
-                    nc.scalar.copy(res[:], acc[:])
-                else:
-                    nc.vector.tensor_copy(res[:], acc[:])
-                nc.sync.dma_start(out[nb * P : (nb + 1) * P, q * BANK : (q + 1) * BANK], res[:])
+            for n0 in range(0, N // P, per_bank):
+                acc = bank(OUT_BANKS[len(filled) % len(OUT_BANKS)])
+                for k in range(per_bank):
+                    n = n0 + k
+                    nc.tensor.matmul_mx(
+                        out=acc[:, k * width : (k + 1) * width],
+                        lhsT=wp_w[:, 2 * n * P : 2 * (n + 1) * P].bitcast(FP4X4),
+                        lhsT_scale=wp_sc[:, n * P : (n + 1) * P],
+                        rhs=z_codes[:].bitcast(FP8X4),
+                        rhs_scale=z_scales[:],
+                        start=True,
+                        stop=True,
+                    )
+                res = ring.tile([P, per_bank, width], F32, name="res", tag="res", bufs=8)
+                copies[len(filled) % 2](res[:].rearrange("p k c -> p (k c)"), acc[:])
+                rows = out[n0 * P : (n0 + per_bank) * P, b0 * P : b0 * P + width]
+                nc.sync.dma_start(rows.rearrange("(k p) c -> p k c", p=P), res[:])
+                filled.append(acc)
 
-        copies = (nc.scalar.copy, nc.vector.tensor_copy)
         close_loss(open_loss[0], last, 0, copies[0])
         close_loss(open_loss[1], last, 1, copies[1])
         quantise_z(0)
         close_loss(open_loss[2], last, 2, copies[0])
-        close_loss(open_loss[3], last, 3, copies[1])
-        for q in range(CHUNKS):
-            if q + 1 < CHUNKS:
+        quantise_z(1)
+        pressure(0)
+        close_loss(open_loss[3], last, 3, copies[0])
+        close_loss(open_loss[4], last, 4, copies[0])
+        for q in range(1, len(CHUNKS)):
+            if q + 1 < len(CHUNKS):
                 quantise_z(q + 1)
             pressure(q)

@@ -24,8 +24,8 @@ SLICES = H // P
 BANK = 512
 HALVES = S // BANK
 CHUNKS = ((0, 2), (2, 4), (6, 4), (10, 4), (14, 2))
-LOSS_BANKS = (0, 1, 2, 3, 7)
-OUT_BANKS = (6, 0, 1, 2, 3, 7)
+LOSS_BANKS = (6, 4, 5, 7, 3)
+OUT_BANKS = (2, 6, 4, 5, 7, 3)
 LIST_COLS = BANK // 16
 
 
@@ -48,16 +48,16 @@ def tile_list_particle_cell_pressure_kernel(
 
         tab_sc = keep.tile([P, T], U8, name="tab_sc", tag="tab_sc", align_bytes=64)
         nc.vector.memset(tab_sc[:].bitcast(I32), 0)
-        pages = [keep.tile([P, T2], F32, name="page%d" % t) for t in range(2)]
+        pages = [keep.tile([P, T2], F32, name="page%d" % t) for t in range(SLICES)]
         ident = keep.tile([P, P], F32, name="ident")
         make_identity(nc, ident[:])
-        for t in range(2):
+        for t in range(SLICES):
             nc.vector.memset(pages[t][:], 0.0)
 
         idx = keep.tile([P, S // 16], U16, name="idx")
         nc.sync.dma_start(idx[:], offs)
         for q in range(4):
-            nc.gpsimd.dma_start(
+            nc.scalar.dma_start(
                 tab_sc[32 * q : 32 * q + 4 * PASSES, :].bitcast(I32),
                 tab_scales[:, 4 * q : 4 * q + 4, :].bitcast(I32),
             )
@@ -124,15 +124,11 @@ def tile_list_particle_cell_pressure_kernel(
             quantise_w(1)
         load_tab(1)
         late = ctx.enter_context(tc.tile_pool(name="late", bufs=1))
-        for t in range(2, SLICES):
-            page = late.tile([P, T2], F32, name="page%d" % t)
-            nc.gpsimd.memset(page[:], 0.0)
-            pages.append(page)
         load_wgs(0)
         load_wgs(1)
         load_w(2, 1, late)
         load_w(3, 1, late)
-        for t in (1, 0, 2, 3):
+        for t in range(SLICES):
             load_old(t)
         wp_w = late.tile([P, 2 * N], U8, name="wp_w", align_bytes=64)
         nc.sync.dma_start(wp_w[:].bitcast(I32), wp_words[0].bitcast(I32))
@@ -158,9 +154,13 @@ def tile_list_particle_cell_pressure_kernel(
                 v_w[a, h] = g
 
         neg_wgs = []
-        for h in range(HALVES):
-            g = keep.tile([P, BANK], F32, name="neg_wgs%d" % h)
-            nc.scalar.activation(g[:], wgs_sb[h][:], ACT.Copy, scale=-1.0)
+
+        def negate_wgs(h, tag):
+            g = late.tile([P, BANK], F32, name="neg_wgs%d" % h, tag=tag)
+            if h == 0:
+                nc.vector.tensor_scalar(g[:], wgs_sb[h][:], -1.0, None, MULT)
+            else:
+                nc.scalar.activation(g[:], wgs_sb[h][:], ACT.Copy, scale=-1.0)
             neg_wgs.append(g)
 
         def place(t, j0, speed):
@@ -189,7 +189,7 @@ def tile_list_particle_cell_pressure_kernel(
                         start=(a == 0 and m == 0),
                         stop=(a == PASSES - 1 and m == 1),
                     )
-            sq = ring.tile([P, BANK], F32, name="sq", tag="sq", bufs=4)
+            sq = keep.tile([P, BANK], F32, name="sq", tag="sq_first")
             nc.scalar.activation(sq[:], acc[:], ACT.Square)
             total = late.tile([P, width], F32, name="total_first")
             nc.vector.tensor_tensor(total[:], sq[:, 0:width], sq[:, width : 2 * width], ADD)
@@ -197,13 +197,11 @@ def tile_list_particle_cell_pressure_kernel(
             nc.scalar.activation(speed[:], total[:], ACT.Sqrt)
             place(0, 0, speed)
 
-        used = []
-
-        def speeds(t, blocks, tag):
-            total = bank(4 + len(used) % 3)
+        def speeds(t, blocks, tag, acc_banks, sum_bank):
+            total = bank(sum_bank)
             codes, scales = w_q[t]
             for k, block in enumerate(blocks):
-                acc = bank(block)
+                acc = bank(acc_banks[k])
                 for a in range(PASSES):
                     cols = slice(a * 2 * P, (a + 1) * 2 * P)
                     for e in range(2):
@@ -218,7 +216,10 @@ def tile_list_particle_cell_pressure_kernel(
                             start=(a == 0 and e == 0),
                             stop=(a == PASSES - 1 and e == 1),
                         )
-                sq = ring.tile([P, BANK], F32, name="sq", tag="sq", bufs=4)
+                if (t, block) == (1, 0):
+                    sq = keep.tile([P, BANK], F32, name="sq", tag="sq_first")
+                else:
+                    sq = ring.tile([P, BANK], F32, name="sq", tag="sq", bufs=3)
                 nc.scalar.activation(sq[:], acc[:], ACT.Square)
                 for e in range(2):
                     o0 = (2 * k + e) * P
@@ -235,8 +236,7 @@ def tile_list_particle_cell_pressure_kernel(
             width = 2 * P * len(blocks)
             speed = late.tile([P, width], F32, name="speed", tag=tag)
             nc.scalar.activation(speed[:], total[:, 0:width], ACT.Sqrt)
-            place(t, 2 * P * blocks[0], speed)
-            used.append(total)
+            return speed
 
         z_t = [keep.tile([P, nb, 2, P, 2], BF16, name="z_t%d" % q) for q, (b0, nb) in enumerate(CHUNKS)]
 
@@ -261,33 +261,41 @@ def tile_list_particle_cell_pressure_kernel(
                 acc[:, 0 : nb * P].rearrange("c (cb p u e) -> c cb u p e", cb=nb, u=2, e=2),
             )
 
-        def loss(t):
-            for q in range(len(CHUNKS)):
-                acc = bank(LOSS_BANKS[q])
-                turn_into(acc, old_sb[t], q, True, False)
-                close_loss(acc, t, q, nc.scalar.copy)
+        def loss(t, q, acc):
+            turn_into(acc, old_sb[t], q, True, False)
+            close_loss(acc, t, q, nc.scalar.copy)
 
         last = SLICES - 1
+        negate_wgs(0, "neg_wgs0")
         first_speeds()
-        speeds(0, [1], "speed0_1")
-        speeds(1, [0, 1], "speed1_0")
-        speeds(0, [2], "speed0_2")
+        place(0, 2 * P, speeds(0, [1], "speed0_1", [1], 6))
+        place(1, 0, speeds(1, [0, 1], "speed1_0", [2, 3], 7))
+        held = speeds(0, [2, 3], "speed0_2", [0, 1], 6)
         quantise_w(2)
-        speeds(1, [2, 3], "w_raw2_1_1")
+        negate_wgs(1, "w_raw2_1_1")
+        place(0, BANK, held)
+        place(1, BANK, speeds(1, [2, 3], "speed1_2", [4, 5], 7))
         quantise_w(3)
-        speeds(0, [3], "w_raw3_1_1")
-        speeds(2, [0, 1], "speed2_0")
-        speeds(2, [2, 3], "speed2_2")
-        speeds(3, [0, 1], "speed3_0")
-        loss(1)
-        speeds(3, [2, 3], "speed3_2")
-        loss(0)
-        loss(2)
+        place(2, 0, speeds(2, [0, 1], "w_raw3_1_1", [4, 5], 6))
+        place(2, BANK, speeds(2, [2, 3], "speed2_2", [4, 5], 7))
+        turns = [(t, q) for t in range(last) for q in range(len(CHUNKS))]
         open_loss = []
-        for q in range(len(CHUNKS)):
+
+        def open_last(q):
             acc = bank(LOSS_BANKS[q])
             turn_into(acc, old_sb[last], q, True, False)
             open_loss.append(acc)
+
+        for k, (t, q) in enumerate(turns):
+            loss(t, q, bank(k % 4))
+            if k == 2:
+                place(3, 0, speeds(3, [0, 1], "speed3_0", [4, 5], 6))
+            if k == 6:
+                place(3, BANK, speeds(3, [2, 3], "speed3_2", [4, 5], 7))
+            if k == 9:
+                for c in range(4):
+                    open_last(c)
+        open_last(4)
 
         z_q = {}
         copies = (nc.scalar.copy, nc.vector.tensor_copy)
@@ -299,13 +307,13 @@ def tile_list_particle_cell_pressure_kernel(
             z_bf = ring.tile([P, nb * P, PACK], BF16, name="z_bf", tag="z_bf", align_bytes=64)
             z_words = z_bf[:].rearrange("p c i -> p (c i)").bitcast(F32)
             for d in range(2):
-                turned = bank(4 + d)
+                turned = bank(d)
                 for k in range(nb):
                     w0 = (nb * d + k) * P
                     nc.tensor.transpose(turned[:, k * P : (k + 1) * P], words[:, w0 : w0 + P], ident[:])
                 dst = z_words[:, d * nb * P : (d + 1) * nb * P].rearrange("p (cb c u) -> p cb c u", cb=half, u=2)
                 src = turned[:, 0 : nb * P].rearrange("p (cb u c) -> p cb c u", cb=half, u=2)
-                copies[1 - d](dst, src)
+                copies[1](dst, src)
             z_codes = ring.tile([P, nb * P], U32, name="z_codes", tag="z_codes", align_bytes=64)
             z_scales = ring.tile([P, nb * P], U8, name="z_scales", tag="z_scales", align_bytes=64)
             nc.vector.quantize_mx(
@@ -334,7 +342,7 @@ def tile_list_particle_cell_pressure_kernel(
                         stop=True,
                     )
                 res = ring.tile([P, per_bank, width], F32, name="res", tag="res", bufs=8)
-                copies[len(filled) % 2](res[:].rearrange("p k c -> p (k c)"), acc[:])
+                copies[1 if len(filled) % 4 == 3 else 0](res[:].rearrange("p k c -> p (k c)"), acc[:])
                 rows = out[n0 * P : (n0 + per_bank) * P, b0 * P : b0 * P + width]
                 nc.sync.dma_start(rows.rearrange("(k p) c -> p k c", p=P), res[:])
                 filled.append(acc)

@@ -47,20 +47,29 @@ def tile_list_particle_cell_pressure_kernel(
         nc.scalar.activation(warm[:], one[:], ACT.Sqrt)
 
         tab_sc = keep.tile([P, T], U8, name="tab_sc", tag="tab_sc", align_bytes=64)
-        nc.vector.memset(tab_sc[:].bitcast(I32), 0)
+        rows = 16 * PASSES
+        nc.sync.dma_start(tab_sc[0:rows, :].bitcast(I32), tab_scales.rearrange("a q t -> (a q) t").bitcast(I32))
+        nc.vector.memset(tab_sc[rows:64, :].bitcast(I32), 0)
+        nc.vector.memset(tab_sc[64:P, :].bitcast(I32), 0)
+        v_sc = [keep.tile([P, S], U8, name="v_sc%d" % a, align_bytes=64) for a in range(PASSES)]
+        for a in range(PASSES):
+            nc.vector.memset(v_sc[a][:].bitcast(I32), 0)
         pages = [keep.tile([P, T2], F32, name="page%d" % t) for t in range(SLICES)]
         ident = keep.tile([P, P], F32, name="ident")
         make_identity(nc, ident[:])
-        for t in range(SLICES):
-            nc.vector.memset(pages[t][:], 0.0)
 
         idx = keep.tile([P, S // 16], U16, name="idx")
         nc.sync.dma_start(idx[:], offs)
-        for q in range(4):
-            nc.scalar.dma_start(
-                tab_sc[32 * q : 32 * q + 4 * PASSES, :].bitcast(I32),
-                tab_scales[:, 4 * q : 4 * q + 4, :].bitcast(I32),
-            )
+        picked_sc = keep.tile([P, S], U8, name="picked_sc", align_bytes=64)
+        nc.vector.tensor_copy(picked_sc[:], tab_sc[:].indirect(idx[:]))
+        for a in range(PASSES):
+            for q in range(4):
+                (nc.scalar, nc.gpsimd)[a].dma_start(
+                    v_sc[a][32 * q : 32 * q + 4, :].bitcast(I32),
+                    picked_sc[16 * a + 4 * q : 16 * a + 4 * q + 4, :].bitcast(I32),
+                )
+        for t in range(SLICES):
+            (nc.vector if t < 2 else nc.gpsimd).memset(pages[t][:], 0.0)
 
         w_raw = {}
 
@@ -68,7 +77,7 @@ def tile_list_particle_cell_pressure_kernel(
             for a in range(PASSES):
                 for m, w in enumerate((wx, wy)):
                     name = "w_raw%d_%d_%d" % (t0, a, m)
-                    if (t0, a, m) == (0, 0, 0):
+                    if (t0, a, m) == (0, 1, 0):
                         raw = keep.tile([P, PACK, count * P], F32, name=name, tag="tab1", align_bytes=64)
                     else:
                         raw = pool.tile([P, PACK, count * P], F32, name=name, tag=name)
@@ -77,17 +86,10 @@ def tile_list_particle_cell_pressure_kernel(
                     for k in range(count):
                         w_raw[t0 + k, a, m] = raw[:, :, k * P : (k + 1) * P]
 
-        wgs_sb = []
-
-        def load_wgs(h):
-            g = late.tile([P, BANK], F32, name="wgs%d" % h)
-            nc.sync.dma_start(g[:], wgs[:, h * BANK : (h + 1) * BANK])
-            wgs_sb.append(g)
-
         old_sb = {}
 
         def load_old(t):
-            o = late.tile([P, T2], F32, name="old%d" % t)
+            o = late.tile([P, T2], F32, name="old%d" % t, tag="old%d" % t, align_bytes=64)
             nc.sync.dma_start(o[:], old[t * P : (t + 1) * P, :])
             old_sb[t] = o
 
@@ -101,7 +103,7 @@ def tile_list_particle_cell_pressure_kernel(
                         wb[:, a, m].rearrange("p (g c) i -> p g i c", c=4),
                         w_raw[t, a, m].rearrange("p i (g c) -> p g i c", c=4),
                     )
-            codes = ring.tile([P, PASSES * 2 * P], U32, name="w_codes", tag="w_codes", bufs=SLICES, align_bytes=64)
+            codes = keep.tile([P, PASSES * 2 * P], U32, name="w_codes", tag="w_codes%d" % t, align_bytes=64)
             scales = ring.tile([P, PASSES * 2 * P], U8, name="w_scales", tag="w_scales", bufs=SLICES, align_bytes=64)
             nc.vector.quantize_mx(
                 out=codes[:].bitcast(FP8X4), scales=scales[:], in_=wb[:].rearrange("p a m c i -> p (a m c i)")
@@ -124,24 +126,11 @@ def tile_list_particle_cell_pressure_kernel(
             quantise_w(1)
         load_tab(1)
         late = ctx.enter_context(tc.tile_pool(name="late", bufs=1))
-        load_wgs(0)
-        load_wgs(1)
+        wgs_sb = late.tile([P, S], F32, name="wgs_sb")
+        nc.sync.dma_start(wgs_sb[:], wgs)
         load_w(2, 1, late)
         load_w(3, 1, late)
-        for t in range(SLICES):
-            load_old(t)
-        wp_w = late.tile([P, 2 * N], U8, name="wp_w", align_bytes=64)
-        nc.sync.dma_start(wp_w[:].bitcast(I32), wp_words[0].bitcast(I32))
-        wp_sc = late.tile([P, N], U8, name="wp_sc", align_bytes=64)
-        nc.vector.memset(wp_sc[:].bitcast(I32), 0)
-        for q in range(4):
-            nc.sync.dma_start(
-                wp_sc[32 * q : 32 * q + 4, :].bitcast(I32),
-                wp_scales[0, 4 * q : 4 * q + 4, :].bitcast(I32),
-            )
 
-        v_sc = keep.tile([P, S], U8, name="v_sc", align_bytes=64)
-        nc.vector.tensor_copy(v_sc[:], tab_sc[:].indirect(idx[:]))
         v_w = {}
         for a in range(PASSES):
             for h in range(HALVES):
@@ -153,23 +142,15 @@ def tile_list_particle_cell_pressure_kernel(
                 )
                 v_w[a, h] = g
 
-        neg_wgs = []
-
-        def negate_wgs(h, tag):
-            g = late.tile([P, BANK], F32, name="neg_wgs%d" % h, tag=tag)
-            if h == 0:
-                nc.vector.tensor_scalar(g[:], wgs_sb[h][:], -1.0, None, MULT)
-            else:
-                nc.scalar.activation(g[:], wgs_sb[h][:], ACT.Copy, scale=-1.0)
-            neg_wgs.append(g)
+        neg_wgs = late.tile([P, S], F32, name="neg_wgs")
+        nc.vector.tensor_scalar(neg_wgs[:], wgs_sb[:], -1.0, None, MULT)
 
         def place(t, j0, speed):
             width = speed.shape[1]
-            h, c0 = divmod(j0, BANK)
             nc.vector.tensor_tensor(
                 pages[t][:].indirect(idx2[:, j0 // 16 : (j0 + width) // 16]),
                 speed[:],
-                neg_wgs[h][:, c0 : c0 + width],
+                neg_wgs[:, j0 : j0 + width],
                 MULT,
             )
 
@@ -185,21 +166,21 @@ def tile_list_particle_cell_pressure_kernel(
                         lhsT=codes[:, cols].bitcast(FP8X4),
                         lhsT_scale=scales[:, cols],
                         rhs=v_w[a, 0][:, 0:width].bitcast(FP8X4),
-                        rhs_scale=v_sc[4 * a : P, 0:width],
+                        rhs_scale=v_sc[a][:, 0:width],
                         start=(a == 0 and m == 0),
                         stop=(a == PASSES - 1 and m == 1),
                     )
-            sq = keep.tile([P, BANK], F32, name="sq", tag="sq_first")
+            sq = keep.tile([P, BANK], F32, name="sq", tag="sq_first", align_bytes=64)
             nc.scalar.activation(sq[:], acc[:], ACT.Square)
-            total = late.tile([P, width], F32, name="total_first")
+            total = keep.tile([P, width], F32, name="total_first", tag="total_first", align_bytes=64)
             nc.vector.tensor_tensor(total[:], sq[:, 0:width], sq[:, width : 2 * width], ADD)
             speed = late.tile([P, width], F32, name="speed_first")
             nc.scalar.activation(speed[:], total[:], ACT.Sqrt)
             place(0, 0, speed)
 
-        def speeds(t, blocks, tag, acc_banks, sum_bank):
-            total = bank(sum_bank)
+        def square_sums(t, blocks, acc_banks, sum_bank, sq_tags):
             codes, scales = w_q[t]
+            total = bank(sum_bank)
             for k, block in enumerate(blocks):
                 acc = bank(acc_banks[k])
                 for a in range(PASSES):
@@ -210,16 +191,17 @@ def tile_list_particle_cell_pressure_kernel(
                         nc.tensor.matmul_mx(
                             out=acc[:, e * 2 * P : (e + 1) * 2 * P],
                             lhsT=v_w[a, h][:, c0 : c0 + P].bitcast(FP8X4),
-                            lhsT_scale=v_sc[4 * a : P, j0 : j0 + P],
+                            lhsT_scale=v_sc[a][:, j0 : j0 + P],
                             rhs=codes[:, cols].bitcast(FP8X4),
                             rhs_scale=scales[:, cols],
                             start=(a == 0 and e == 0),
                             stop=(a == PASSES - 1 and e == 1),
                         )
-                if (t, block) == (1, 0):
-                    sq = keep.tile([P, BANK], F32, name="sq", tag="sq_first")
-                else:
+                if sq_tags[k] == "sq":
                     sq = ring.tile([P, BANK], F32, name="sq", tag="sq", bufs=3)
+                else:
+                    pool = late if sq_tags[k] == "old0" else keep
+                    sq = pool.tile([P, BANK], F32, name="sq", tag=sq_tags[k], align_bytes=64)
                 nc.scalar.activation(sq[:], acc[:], ACT.Square)
                 for e in range(2):
                     o0 = (2 * k + e) * P
@@ -233,9 +215,14 @@ def tile_list_particle_cell_pressure_kernel(
                             stop=(m == 1),
                             is_transpose=True,
                         )
-            width = 2 * P * len(blocks)
-            speed = late.tile([P, width], F32, name="speed", tag=tag)
-            nc.scalar.activation(speed[:], total[:, 0:width], ACT.Sqrt)
+            return total[:, 0 : 2 * P * len(blocks)]
+
+        def roots(totals, tag):
+            speed = late.tile([P, sum(total.shape[1] for total in totals)], F32, name="speed", tag=tag)
+            c0 = 0
+            for total in totals:
+                nc.scalar.activation(speed[:, c0 : c0 + total.shape[1]], total, ACT.Sqrt)
+                c0 = c0 + total.shape[1]
             return speed
 
         z_t = [keep.tile([P, nb, 2, P, 2], BF16, name="z_t%d" % q) for q, (b0, nb) in enumerate(CHUNKS)]
@@ -266,18 +253,28 @@ def tile_list_particle_cell_pressure_kernel(
             close_loss(acc, t, q, nc.scalar.copy)
 
         last = SLICES - 1
-        negate_wgs(0, "neg_wgs0")
+        for t in range(SLICES):
+            load_old(t)
+        wp_w = late.tile([P, 2 * N], U8, name="wp_w", align_bytes=64)
+        nc.sync.dma_start(wp_w[:].bitcast(I32), wp_words[0].bitcast(I32))
+        wp_sc = late.tile([P, N], U8, name="wp_sc", align_bytes=64)
+        nc.vector.memset(wp_sc[:].bitcast(I32), 0)
+        for q in range(4):
+            nc.sync.dma_start(
+                wp_sc[32 * q : 32 * q + 4, :].bitcast(I32),
+                wp_scales[0, 4 * q : 4 * q + 4, :].bitcast(I32),
+            )
+
         first_speeds()
-        place(0, 2 * P, speeds(0, [1], "speed0_1", [1], 6))
-        place(1, 0, speeds(1, [0, 1], "speed1_0", [2, 3], 7))
-        held = speeds(0, [2, 3], "speed0_2", [0, 1], 6)
+        place(0, 2 * P, roots([square_sums(0, [1], [1], 6, ["sq"])], "speed0_1"))
+        place(1, 0, roots([square_sums(1, [0, 1], [4, 5], 7, ["sq_first", "total_first"])], "speed1_0"))
+        held = square_sums(0, [2, 3], [0, 1], 6, ["sq", "sq"])
         quantise_w(2)
-        negate_wgs(1, "w_raw2_1_1")
-        place(0, BANK, held)
-        place(1, BANK, speeds(1, [2, 3], "speed1_2", [4, 5], 7))
+        place(0, BANK, roots([held], "w_raw2_1_1"))
+        place(1, BANK, roots([square_sums(1, [2, 3], [4, 5], 7, ["sq", "sq"])], "speed1_2"))
         quantise_w(3)
-        place(2, 0, speeds(2, [0, 1], "w_raw3_1_1", [4, 5], 6))
-        place(2, BANK, speeds(2, [2, 3], "speed2_2", [4, 5], 7))
+        place(2, 0, roots([square_sums(2, [0, 1], [4, 5], 6, ["sq", "sq"])], "w_raw3_1_1"))
+        place(2, BANK, roots([square_sums(2, [2, 3], [4, 5], 7, ["sq", "sq"])], "speed2_2"))
         turns = [(t, q) for t in range(last) for q in range(len(CHUNKS))]
         open_loss = []
 
@@ -289,13 +286,25 @@ def tile_list_particle_cell_pressure_kernel(
         for k, (t, q) in enumerate(turns):
             loss(t, q, bank(k % 4))
             if k == 2:
-                place(3, 0, speeds(3, [0, 1], "speed3_0", [4, 5], 6))
+                place(3, 0, roots([square_sums(3, [0, 1], [4, 5], 6, ["sq", "sq"])], "speed3_0"))
             if k == 6:
-                place(3, BANK, speeds(3, [2, 3], "speed3_2", [4, 5], 7))
+                place(3, BANK, roots([square_sums(3, [2, 3], [4, 5], 7, ["sq", "sq"])], "speed3_2"))
             if k == 9:
                 for c in range(4):
                     open_last(c)
         open_last(4)
+        idle = bank(0)
+        codes, scales = w_q[last]
+        for k in range(3):
+            nc.tensor.matmul_mx(
+                out=idle[:],
+                lhsT=v_w[0, 0][:, 0:P].bitcast(FP8X4),
+                lhsT_scale=v_sc[0][:, 0:P],
+                rhs=codes[:].bitcast(FP8X4),
+                rhs_scale=scales[:],
+                start=True,
+                stop=True,
+            )
 
         z_q = {}
         copies = (nc.scalar.copy, nc.vector.tensor_copy)

@@ -24,8 +24,12 @@ SLICES = H // P
 BANK = 512
 HALVES = S // BANK
 CHUNKS = ((0, 2), (2, 4), (6, 4), (10, 4), (14, 2))
-LOSS_BANKS = (6, 4, 5, 7, 3)
-OUT_BANKS = (2, 6, 4, 5, 7, 3)
+GROUPS = ((0, 4), (1,), (2,), (3,))
+LOW_BANKS = (0, 1, 2, 3)
+HIGH_BANKS = (4, 6, 5, 7)
+WORD_BANKS = (4, 5)
+LAST_CHUNK_BANK = 6
+OUT_BANKS = (7, 0, 1, 2, 3, 6)
 LIST_COLS = BANK // 16
 
 
@@ -46,148 +50,177 @@ def tile_list_particle_cell_pressure_kernel(
         warm = keep.tile([P, 8], F32, name="warm")
         nc.scalar.activation(warm[:], one[:], ACT.Sqrt)
 
-        tab_sc = keep.tile([P, T], U8, name="tab_sc", tag="tab_sc", align_bytes=64)
-        rows = 16 * PASSES
-        nc.sync.dma_start(tab_sc[0:rows, :].bitcast(I32), tab_scales.rearrange("a q t -> (a q) t").bitcast(I32))
-        nc.vector.memset(tab_sc[rows:64, :].bitcast(I32), 0)
-        nc.vector.memset(tab_sc[64:P, :].bitcast(I32), 0)
+        idx = keep.tile([P, S // 16], U16, name="idx")
+        idx2 = keep.tile([P, S // 16], U16, name="idx2")
+        picked_sc = keep.tile([P, S], U8, name="picked_sc", align_bytes=64)
         v_sc = [keep.tile([P, S], U8, name="v_sc%d" % a, align_bytes=64) for a in range(PASSES)]
-        for a in range(PASSES):
-            nc.vector.memset(v_sc[a][:].bitcast(I32), 0)
+        wp_sc = keep.tile([P, N], U8, name="wp_sc", align_bytes=64)
         pages = [keep.tile([P, T2], F32, name="page%d" % t) for t in range(SLICES)]
         ident = keep.tile([P, P], F32, name="ident")
-        make_identity(nc, ident[:])
-
-        idx = keep.tile([P, S // 16], U16, name="idx")
-        nc.sync.dma_start(idx[:], offs)
-        picked_sc = keep.tile([P, S], U8, name="picked_sc", align_bytes=64)
-        nc.vector.tensor_copy(picked_sc[:], tab_sc[:].indirect(idx[:]))
+        tab = []
+        with tc.tile_pool(name="early", bufs=1) as early:
+            tab_sc = early.tile([P, T], U8, name="tab_sc", align_bytes=64)
+            rows = 16 * PASSES
+            nc.sync.dma_start(idx[:], offs)
+            nc.sync.dma_start(tab_sc[0:rows, :].bitcast(I32), tab_scales.rearrange("a q t -> (a q) t").bitcast(I32))
+            nc.sync.dma_start(idx2[:], offs2)
+            for a in range(PASSES):
+                words = keep.tile([P, T], I32, name="tab%d" % a, tag="tab%d" % a, align_bytes=64)
+                nc.sync.dma_start(words[:], tab_words[a].rearrange("p t i -> p (t i)").bitcast(I32))
+                tab.append(words)
+            nc.vector.memset(tab_sc[rows:64, :].bitcast(I32), 0)
+            nc.gpsimd.memset(tab_sc[64:P, :].bitcast(I32), 0)
+            for a in range(PASSES):
+                nc.gpsimd.memset(v_sc[a][:].bitcast(I32), 0)
+            nc.vector.tensor_copy(picked_sc[:], tab_sc[:].indirect(idx[:]))
         for a in range(PASSES):
             for q in range(4):
-                (nc.scalar, nc.gpsimd)[a].dma_start(
+                nc.scalar.dma_start(
                     v_sc[a][32 * q : 32 * q + 4, :].bitcast(I32),
                     picked_sc[16 * a + 4 * q : 16 * a + 4 * q + 4, :].bitcast(I32),
                 )
+        nc.gpsimd.memset(wp_sc[:].bitcast(I32), 0)
+        make_identity(nc, ident[:])
         for t in range(SLICES):
-            (nc.vector if t < 2 else nc.gpsimd).memset(pages[t][:], 0.0)
+            nc.gpsimd.memset(pages[t][:], 0.0)
+
+        late = ctx.enter_context(tc.tile_pool(name="late", bufs=1))
 
         w_raw = {}
 
-        def load_w(t0, count, pool):
-            for a in range(PASSES):
-                for m, w in enumerate((wx, wy)):
-                    name = "w_raw%d_%d_%d" % (t0, a, m)
-                    if (t0, a, m) == (0, 1, 0):
-                        raw = keep.tile([P, PACK, count * P], F32, name=name, tag="tab1", align_bytes=64)
-                    else:
-                        raw = pool.tile([P, PACK, count * P], F32, name=name, tag=name)
-                    rows = w[a * P * PACK : (a + 1) * P * PACK, t0 * P : (t0 + count) * P]
+        def load_w(t):
+            for m, w in enumerate((wx, wy)):
+                for a in range(PASSES):
+                    name = "w_raw%d_%d_%d" % (t, a, m)
+                    raw = late.tile([P, PACK, P], F32, name=name, tag=name)
+                    rows = w[a * P * PACK : (a + 1) * P * PACK, t * P : (t + 1) * P]
                     nc.sync.dma_start(raw[:], rows.rearrange("(p i) c -> p i c", i=PACK))
-                    for k in range(count):
-                        w_raw[t0 + k, a, m] = raw[:, :, k * P : (k + 1) * P]
+                    w_raw[t, a, m] = raw
 
         old_sb = {}
 
-        def load_old(t):
-            o = late.tile([P, T2], F32, name="old%d" % t, tag="old%d" % t, align_bytes=64)
+        def load_old(t, pool, tag):
+            o = pool.tile([P, T2], F32, name="old%d" % t, tag=tag, align_bytes=64)
             nc.sync.dma_start(o[:], old[t * P : (t + 1) * P, :])
             old_sb[t] = o
 
-        w_q = {}
-
-        def quantise_w(t):
-            wb = ring.tile([P, PASSES, 2, P, PACK], BF16, name="w_bf", tag="w_bf", align_bytes=64)
-            for a in range(PASSES):
-                for m in range(2):
-                    nc.scalar.copy(
-                        wb[:, a, m].rearrange("p (g c) i -> p g i c", c=4),
-                        w_raw[t, a, m].rearrange("p i (g c) -> p g i c", c=4),
-                    )
-            codes = keep.tile([P, PASSES * 2 * P], U32, name="w_codes", tag="w_codes%d" % t, align_bytes=64)
-            scales = ring.tile([P, PASSES * 2 * P], U8, name="w_scales", tag="w_scales", bufs=SLICES, align_bytes=64)
-            nc.vector.quantize_mx(
-                out=codes[:].bitcast(FP8X4), scales=scales[:], in_=wb[:].rearrange("p a m c i -> p (a m c i)")
-            )
-            w_q[t] = (codes, scales)
-
-        tab = []
-
-        def load_tab(a):
-            words = keep.tile([P, T], I32, name="tab%d" % a, tag="tab%d" % a, align_bytes=64)
-            nc.sync.dma_start(words[:], tab_words[a].rearrange("p t i -> p (t i)").bitcast(I32))
-            tab.append(words)
-
-        with tc.tile_pool(name="early", bufs=1) as early:
-            load_w(0, 2, early)
-            load_tab(0)
-            idx2 = keep.tile([P, S // 16], U16, name="idx2")
-            nc.sync.dma_start(idx2[:], offs2)
-            quantise_w(0)
-            quantise_w(1)
-        load_tab(1)
-        late = ctx.enter_context(tc.tile_pool(name="late", bufs=1))
-        wgs_sb = late.tile([P, S], F32, name="wgs_sb")
-        nc.sync.dma_start(wgs_sb[:], wgs)
-        load_w(2, 1, late)
-        load_w(3, 1, late)
+        load_w(0)
+        wgs_sb = [late.tile([P, BANK], F32, name="wgs_sb%d" % h) for h in range(HALVES)]
+        nc.sync.dma_start(wgs_sb[0][:], wgs[:, 0:BANK])
+        load_w(1)
+        nc.sync.dma_start(wgs_sb[1][:], wgs[:, BANK:S])
+        for t in range(2, SLICES):
+            load_w(t)
 
         v_w = {}
         for a in range(PASSES):
             for h in range(HALVES):
-                name = "v%d_%d" % (a, h)
-                tag = "tab_sc" if (a, h) == (1, 0) else name
-                g = keep.tile([P, BANK], U32, name=name, tag=tag, align_bytes=64)
+                g = keep.tile([P, BANK], U32, name="v%d_%d" % (a, h), align_bytes=64)
                 nc.vector.tensor_copy(
                     g[:], tab[a][:].bitcast(U32).indirect(idx[:, h * LIST_COLS : (h + 1) * LIST_COLS])
                 )
                 v_w[a, h] = g
 
-        neg_wgs = late.tile([P, S], F32, name="neg_wgs")
-        nc.vector.tensor_scalar(neg_wgs[:], wgs_sb[:], -1.0, None, MULT)
+        last = SLICES - 1
+        load_old(0, keep, "tab0")
+        load_old(last, keep, "tab1")
+        wp_w = late.tile([P, 2 * N], U8, name="wp_w", align_bytes=64)
+        nc.sync.dma_start(wp_w[:].bitcast(I32), wp_words[0].bitcast(I32))
+        for q in range(4):
+            nc.sync.dma_start(
+                wp_sc[32 * q : 32 * q + 4, :].bitcast(I32),
+                wp_scales[0, 4 * q : 4 * q + 4, :].bitcast(I32),
+            )
+
+        w_q = {}
+
+        def round_w(copy, dst, t, a, m):
+            copy(
+                dst.rearrange("p (g c) i -> p g i c", c=4),
+                w_raw[t, a, m][:].rearrange("p i (g c) -> p g i c", c=4),
+            )
+
+        def code_tiles(t):
+            codes = keep.tile([P, PASSES * 2 * P], U32, name="w_codes%d" % t, align_bytes=64)
+            scales = keep.tile([P, PASSES * 2 * P], U8, name="w_scales%d" % t, align_bytes=64)
+            w_q[t] = (codes, scales)
+            return codes, scales
+
+        def quantise_w(t):
+            wb = late.tile([P, PASSES, 2, P, PACK], BF16, name="w_bf", tag="w_bf%d" % t, align_bytes=64)
+            for m in range(2):
+                for a in range(PASSES):
+                    round_w(nc.scalar.copy, wb[:, a, m], t, a, m)
+            codes, scales = code_tiles(t)
+            nc.vector.quantize_mx(
+                out=codes[:].bitcast(FP8X4), scales=scales[:], in_=wb[:].rearrange("p a m c i -> p (a m c i)")
+            )
+
+        neg_wgs = [late.tile([P, BANK], F32, name="neg_wgs%d" % h) for h in range(HALVES)]
+
+        def negate_wgs(h):
+            nc.vector.tensor_scalar(neg_wgs[h][:], wgs_sb[h][:], -1.0, None, MULT)
 
         def place(t, j0, speed):
             width = speed.shape[1]
             nc.vector.tensor_tensor(
                 pages[t][:].indirect(idx2[:, j0 // 16 : (j0 + width) // 16]),
                 speed[:],
-                neg_wgs[:, j0 : j0 + width],
+                neg_wgs[j0 // BANK][:, j0 % BANK : j0 % BANK + width],
                 MULT,
             )
 
         def first_speeds():
-            width = 2 * P
-            acc = bank(0)
-            codes, scales = w_q[0]
-            for a in range(PASSES):
-                for m in range(2):
+            width = BANK // 2
+            codes, scales = code_tiles(0)
+            acc = [[bank(0)], [bank(1), bank(2)]]
+            for m in range(2):
+                for a in range(PASSES):
+                    wb = late.tile([P, P, PACK], BF16, name="w_bf_first%d_%d" % (a, m), align_bytes=64)
+                    round_w(nc.scalar.copy, wb[:], 0, a, m)
                     cols = slice((2 * a + m) * P, (2 * a + m + 1) * P)
-                    nc.tensor.matmul_mx(
-                        out=acc[:, m * width : (m + 1) * width],
-                        lhsT=codes[:, cols].bitcast(FP8X4),
-                        lhsT_scale=scales[:, cols],
-                        rhs=v_w[a, 0][:, 0:width].bitcast(FP8X4),
-                        rhs_scale=v_sc[a][:, 0:width],
-                        start=(a == 0 and m == 0),
-                        stop=(a == PASSES - 1 and m == 1),
+                    nc.vector.quantize_mx(
+                        out=codes[:, cols].bitcast(FP8X4),
+                        scales=scales[:, cols],
+                        in_=wb[:].rearrange("p c i -> p (c i)"),
                     )
-            sq = keep.tile([P, BANK], F32, name="sq", tag="sq_first", align_bytes=64)
-            nc.scalar.activation(sq[:], acc[:], ACT.Square)
-            total = keep.tile([P, width], F32, name="total_first", tag="total_first", align_bytes=64)
-            nc.vector.tensor_tensor(total[:], sq[:, 0:width], sq[:, width : 2 * width], ADD)
-            speed = late.tile([P, width], F32, name="speed_first")
-            nc.scalar.activation(speed[:], total[:], ACT.Sqrt)
-            place(0, 0, speed)
+                    n = BANK // len(acc[m])
+                    for k, dst in enumerate(acc[m]):
+                        nc.tensor.matmul_mx(
+                            out=dst[:, 0:n],
+                            lhsT=codes[:, cols].bitcast(FP8X4),
+                            lhsT_scale=scales[:, cols],
+                            rhs=v_w[a, 0][:, k * n : (k + 1) * n].bitcast(FP8X4),
+                            rhs_scale=v_sc[a][:, k * n : (k + 1) * n],
+                            start=(a == 0),
+                            stop=(a == PASSES - 1),
+                        )
+            negate_wgs(0)
+            sq_a = late.tile([P, BANK], F32, name="sq_a")
+            nc.scalar.activation(sq_a[:], acc[0][0][:], ACT.Square)
+            totals = []
+            for k in range(2):
+                sq_b = late.tile([P, width], F32, name="sq_b", tag=("w_bf2", "sq_b")[k], align_bytes=64)
+                nc.scalar.activation(sq_b[:], acc[1][k][:, 0:width], ACT.Square)
+                total = late.tile([P, width], F32, name="total", tag=("total", "w_bf1")[k], align_bytes=64)
+                nc.vector.tensor_tensor(total[:], sq_a[:, k * width : (k + 1) * width], sq_b[:], ADD)
+                totals.append(total)
+            for k in range(2):
+                speed = late.tile([P, width], F32, name="speed_first%d" % k)
+                nc.scalar.activation(speed[:], totals[k][:], ACT.Sqrt)
+                place(0, k * width, speed)
 
-        def square_sums(t, blocks, acc_banks, sum_bank, sq_tags):
+        def squares(t, h, sq_tags):
+            acc_banks = ((5, 7), (6, 5))[h]
             codes, scales = w_q[t]
-            total = bank(sum_bank)
-            for k, block in enumerate(blocks):
+            result = []
+            for k in range(2):
                 acc = bank(acc_banks[k])
                 for a in range(PASSES):
                     cols = slice(a * 2 * P, (a + 1) * 2 * P)
                     for e in range(2):
-                        j0 = (2 * block + e) * P
-                        h, c0 = divmod(j0, BANK)
+                        c0 = (2 * k + e) * P
+                        j0 = h * BANK + c0
                         nc.tensor.matmul_mx(
                             out=acc[:, e * 2 * P : (e + 1) * 2 * P],
                             lhsT=v_w[a, h][:, c0 : c0 + P].bitcast(FP8X4),
@@ -197,12 +230,17 @@ def tile_list_particle_cell_pressure_kernel(
                             start=(a == 0 and e == 0),
                             stop=(a == PASSES - 1 and e == 1),
                         )
-                if sq_tags[k] == "sq":
-                    sq = ring.tile([P, BANK], F32, name="sq", tag="sq", bufs=3)
+                if sq_tags[k]:
+                    sq = late.tile([P, BANK], F32, name="sq", tag=sq_tags[k], align_bytes=64)
                 else:
-                    pool = late if sq_tags[k] == "old0" else keep
-                    sq = pool.tile([P, BANK], F32, name="sq", tag=sq_tags[k], align_bytes=64)
+                    sq = ring.tile([P, BANK], F32, name="sq", tag="sq", bufs=3)
                 nc.scalar.activation(sq[:], acc[:], ACT.Square)
+                result.append(sq)
+            return result
+
+        def roots(t, j0, sqs, sum_bank, speed_tag):
+            total = bank(sum_bank)
+            for k, sq in enumerate(sqs):
                 for e in range(2):
                     o0 = (2 * k + e) * P
                     for m in range(2):
@@ -215,96 +253,69 @@ def tile_list_particle_cell_pressure_kernel(
                             stop=(m == 1),
                             is_transpose=True,
                         )
-            return total[:, 0 : 2 * P * len(blocks)]
-
-        def roots(totals, tag):
-            speed = late.tile([P, sum(total.shape[1] for total in totals)], F32, name="speed", tag=tag)
-            c0 = 0
-            for total in totals:
-                nc.scalar.activation(speed[:, c0 : c0 + total.shape[1]], total, ACT.Sqrt)
-                c0 = c0 + total.shape[1]
+            width = 2 * P * len(sqs)
+            speed = late.tile([P, width], F32, name="speed", tag=speed_tag)
+            nc.scalar.activation(speed[:], total[:, 0:width], ACT.Sqrt)
+            place(t, j0, speed)
             return speed
 
         z_t = [keep.tile([P, nb, 2, P, 2], BF16, name="z_t%d" % q) for q, (b0, nb) in enumerate(CHUNKS)]
 
-        def turn_into(acc, src, q, first, final):
-            b0, nb = CHUNKS[q]
-            for cb in range(nb):
-                c0 = (b0 + cb) * P
+        def turn_into(acc, src, group, first, final):
+            blocks = [b for q in group for b in range(CHUNKS[q][0], CHUNKS[q][0] + CHUNKS[q][1])]
+            for k, b in enumerate(blocks):
                 nc.tensor.matmul(
-                    acc[:, cb * P : (cb + 1) * P],
-                    src[:, c0 : c0 + P],
+                    acc[:, k * P : (k + 1) * P],
+                    src[:, b * P : (b + 1) * P],
                     ident[:],
-                    start=(first and cb == 0),
-                    stop=(final and cb == nb - 1),
+                    start=(first and k == 0),
+                    stop=(final and k == len(blocks) - 1),
                     is_transpose=True,
                 )
 
-        def close_loss(acc, t, q, copy):
-            nb = CHUNKS[q][1]
-            turn_into(acc, pages[t], q, False, True)
-            copy(
-                z_t[q][:, :, :, 32 * t : 32 * (t + 1), :],
-                acc[:, 0 : nb * P].rearrange("c (cb p u e) -> c cb u p e", cb=nb, u=2, e=2),
-            )
+        def close_loss(acc, t, group, copy):
+            turn_into(acc, pages[t], group, False, True)
+            c0 = 0
+            for q in group:
+                nb = CHUNKS[q][1]
+                copy(
+                    z_t[q][:, :, :, 32 * t : 32 * (t + 1), :],
+                    acc[:, c0 : c0 + nb * P].rearrange("c (cb p u e) -> c cb u p e", cb=nb, u=2, e=2),
+                )
+                c0 = c0 + nb * P
 
-        def loss(t, q, acc):
-            turn_into(acc, old_sb[t], q, True, False)
-            close_loss(acc, t, q, nc.scalar.copy)
-
-        last = SLICES - 1
-        for t in range(SLICES):
-            load_old(t)
-        wp_w = late.tile([P, 2 * N], U8, name="wp_w", align_bytes=64)
-        nc.sync.dma_start(wp_w[:].bitcast(I32), wp_words[0].bitcast(I32))
-        wp_sc = late.tile([P, N], U8, name="wp_sc", align_bytes=64)
-        nc.vector.memset(wp_sc[:].bitcast(I32), 0)
-        for q in range(4):
-            nc.sync.dma_start(
-                wp_sc[32 * q : 32 * q + 4, :].bitcast(I32),
-                wp_scales[0, 4 * q : 4 * q + 4, :].bitcast(I32),
-            )
+        def losses(t, banks):
+            for group, b in zip(GROUPS, banks):
+                acc = bank(b)
+                turn_into(acc, old_sb[t], group, True, False)
+                close_loss(acc, t, group, nc.scalar.copy)
 
         first_speeds()
-        place(0, 2 * P, roots([square_sums(0, [1], [1], 6, ["sq"])], "speed0_1"))
-        place(1, 0, roots([square_sums(1, [0, 1], [4, 5], 7, ["sq_first", "total_first"])], "speed1_0"))
-        held = square_sums(0, [2, 3], [0, 1], 6, ["sq", "sq"])
+        quantise_w(1)
+        negate_wgs(1)
+        roots(0, BANK, squares(0, 1, ("total", "w_bf2")), 7, "w_raw1_1_1")
+        sqs = squares(1, 0, (None, None))
+        roots(1, 0, sqs[0:1], 4, "speed1")
         quantise_w(2)
-        place(0, BANK, roots([held], "w_raw2_1_1"))
-        place(1, BANK, roots([square_sums(1, [2, 3], [4, 5], 7, ["sq", "sq"])], "speed1_2"))
+        roots(1, 2 * P, sqs[1:2], 3, "w_raw2_1_1")
+        roots(1, BANK, squares(1, 1, (None, "w_bf3")), 7, "speed2")
+        sqs = squares(2, 0, ("old1", None))
+        roots(2, 0, sqs[0:1], 4, "speed3")
+        load_old(1, late, "old1")
         quantise_w(3)
-        place(2, 0, roots([square_sums(2, [0, 1], [4, 5], 6, ["sq", "sq"])], "w_raw3_1_1"))
-        place(2, BANK, roots([square_sums(2, [2, 3], [4, 5], 7, ["sq", "sq"])], "speed2_2"))
-        turns = [(t, q) for t in range(last) for q in range(len(CHUNKS))]
+        roots(2, 2 * P, sqs[1:2], 3, "w_raw3_1_1")
+        roots(2, BANK, squares(2, 1, (None, None)), 7, "speed4")
+        losses(0, LOW_BANKS)
+        roots(3, 0, squares(3, 0, ("old2", None)), 4, "speed5")
+        load_old(2, late, "old2")
+        losses(1, LOW_BANKS)
+        roots(3, BANK, squares(3, 1, (None, None)), 7, "speed6")
         open_loss = []
-
-        def open_last(q):
-            acc = bank(LOSS_BANKS[q])
-            turn_into(acc, old_sb[last], q, True, False)
+        for q in range(len(CHUNKS) - 1):
+            acc = bank(LOW_BANKS[q])
+            turn_into(acc, old_sb[last], (q,), True, False)
             open_loss.append(acc)
-
-        for k, (t, q) in enumerate(turns):
-            loss(t, q, bank(k % 4))
-            if k == 2:
-                place(3, 0, roots([square_sums(3, [0, 1], [4, 5], 6, ["sq", "sq"])], "speed3_0"))
-            if k == 6:
-                place(3, BANK, roots([square_sums(3, [2, 3], [4, 5], 7, ["sq", "sq"])], "speed3_2"))
-            if k == 9:
-                for c in range(4):
-                    open_last(c)
-        open_last(4)
-        idle = bank(0)
-        codes, scales = w_q[last]
-        for k in range(3):
-            nc.tensor.matmul_mx(
-                out=idle[:],
-                lhsT=v_w[0, 0][:, 0:P].bitcast(FP8X4),
-                lhsT_scale=v_sc[0][:, 0:P],
-                rhs=codes[:].bitcast(FP8X4),
-                rhs_scale=scales[:],
-                start=True,
-                stop=True,
-            )
+        losses(2, HIGH_BANKS)
 
         z_q = {}
         copies = (nc.scalar.copy, nc.vector.tensor_copy)
@@ -315,13 +326,13 @@ def tile_list_particle_cell_pressure_kernel(
             words = z_t[q][:].rearrange("c cb u p e -> c (cb u p e)").bitcast(F32)
             z_bf = ring.tile([P, nb * P, PACK], BF16, name="z_bf", tag="z_bf", align_bytes=64)
             z_words = z_bf[:].rearrange("p c i -> p (c i)").bitcast(F32)
-            for d in range(2):
-                turned = bank(d)
-                for k in range(nb):
-                    w0 = (nb * d + k) * P
+            for d in range(half):
+                turned = bank(WORD_BANKS[(d + CHUNKS[q][0] // 2) % 2])
+                for k in range(4):
+                    w0 = (4 * d + k) * P
                     nc.tensor.transpose(turned[:, k * P : (k + 1) * P], words[:, w0 : w0 + P], ident[:])
-                dst = z_words[:, d * nb * P : (d + 1) * nb * P].rearrange("p (cb c u) -> p cb c u", cb=half, u=2)
-                src = turned[:, 0 : nb * P].rearrange("p (cb u c) -> p cb c u", cb=half, u=2)
+                dst = z_words[:, d * BANK : (d + 1) * BANK].rearrange("p (cb c u) -> p cb c u", cb=2, u=2)
+                src = turned[:].rearrange("p (cb u c) -> p cb c u", cb=2, u=2)
                 copies[1](dst, src)
             z_codes = ring.tile([P, nb * P], U32, name="z_codes", tag="z_codes", align_bytes=64)
             z_scales = ring.tile([P, nb * P], U8, name="z_scales", tag="z_scales", align_bytes=64)
@@ -356,14 +367,16 @@ def tile_list_particle_cell_pressure_kernel(
                 nc.sync.dma_start(rows.rearrange("(k p) c -> p k c", p=P), res[:])
                 filled.append(acc)
 
-        close_loss(open_loss[0], last, 0, copies[0])
-        close_loss(open_loss[1], last, 1, copies[1])
+        close_loss(open_loss[0], last, (0,), copies[0])
+        close_loss(open_loss[1], last, (1,), copies[1])
         quantise_z(0)
-        close_loss(open_loss[2], last, 2, copies[0])
+        close_loss(open_loss[2], last, (2,), copies[0])
         quantise_z(1)
         pressure(0)
-        close_loss(open_loss[3], last, 3, copies[0])
-        close_loss(open_loss[4], last, 4, copies[0])
+        close_loss(open_loss[3], last, (3,), copies[0])
+        acc = bank(LAST_CHUNK_BANK)
+        turn_into(acc, old_sb[last], (4,), True, False)
+        close_loss(acc, last, (4,), copies[0])
         for q in range(1, len(CHUNKS)):
             if q + 1 < len(CHUNKS):
                 quantise_z(q + 1)

@@ -21,16 +21,24 @@ ADD = mybir.AluOpType.add
 PACK = 4
 PASSES = K // (P * PACK)
 SLICES = H // P
+LAST = SLICES - 1
 BANK = 512
+PIECE = BANK // 2
 HALVES = S // BANK
-CHUNKS = ((0, 2), (2, 4), (6, 4), (10, 4), (14, 2))
-GROUPS = ((0, 4), (1,), (2,), (3,))
+QUADRANT = 32
+SCALE_ROWS = 16
+LIST_GROUP = 16
+NEIGHBOURS = 4
+CHUNKS = ((0, 2), (2, 2), (4, 4), (8, 4), (12, 4))
+GROUPS = ((0, 1), (2,), (3,), (4,))
 LOW_BANKS = (0, 1, 2, 3)
-HIGH_BANKS = (4, 6, 5, 7)
+HIGH_BANKS = (4, 5, 6, 7)
+SPARE_SUM, TURN_A, TURN_B, HALF_SUM = HIGH_BANKS
 WORD_BANKS = (4, 5)
-LAST_CHUNK_BANK = 6
-OUT_BANKS = (7, 0, 1, 2, 3, 6)
-LIST_COLS = BANK // 16
+OUT_BANKS = (6, 0, 1, 2, 3, 7)
+SHARED_FROM = 10
+SQUARE_BUFFERS = 3
+RESULT_BUFFERS = 8
 
 
 def tile_list_particle_cell_pressure_kernel(
@@ -47,97 +55,94 @@ def tile_list_particle_cell_pressure_kernel(
 
         one = keep.tile([P, 8], F32, name="one")
         nc.gpsimd.memset(one[:], 1.0)
-        warm = keep.tile([P, 8], F32, name="warm")
-        nc.scalar.activation(warm[:], one[:], ACT.Sqrt)
+        preload = keep.tile([P, 8], F32, name="preload")
+        nc.scalar.activation(preload[:], one[:], ACT.Sqrt)
 
-        idx = keep.tile([P, S // 16], U16, name="idx")
-        idx2 = keep.tile([P, S // 16], U16, name="idx2")
+        idx = keep.tile([P, S // LIST_GROUP], U16, name="idx")
+        idx2 = keep.tile([P, S // LIST_GROUP], U16, name="idx2")
         picked_sc = keep.tile([P, S], U8, name="picked_sc", align_bytes=64)
         v_sc = [keep.tile([P, S], U8, name="v_sc%d" % a, align_bytes=64) for a in range(PASSES)]
         wp_sc = keep.tile([P, N], U8, name="wp_sc", align_bytes=64)
-        pages = [keep.tile([P, T2], F32, name="page%d" % t) for t in range(SLICES)]
         ident = keep.tile([P, P], F32, name="ident")
-        tab = []
+        tab = [keep.tile([P, T], I32, name="tab%d" % a, align_bytes=64) for a in range(PASSES)]
         with tc.tile_pool(name="early", bufs=1) as early:
             tab_sc = early.tile([P, T], U8, name="tab_sc", align_bytes=64)
-            rows = 16 * PASSES
+            loaded = SCALE_ROWS * PASSES
             nc.sync.dma_start(idx[:], offs)
-            nc.sync.dma_start(tab_sc[0:rows, :].bitcast(I32), tab_scales.rearrange("a q t -> (a q) t").bitcast(I32))
+            nc.sync.dma_start(tab_sc[0:loaded, :].bitcast(I32), tab_scales.rearrange("a q t -> (a q) t").bitcast(I32))
             nc.sync.dma_start(idx2[:], offs2)
             for a in range(PASSES):
-                words = keep.tile([P, T], I32, name="tab%d" % a, tag="tab%d" % a, align_bytes=64)
-                nc.sync.dma_start(words[:], tab_words[a].rearrange("p t i -> p (t i)").bitcast(I32))
-                tab.append(words)
-            nc.vector.memset(tab_sc[rows:64, :].bitcast(I32), 0)
-            nc.gpsimd.memset(tab_sc[64:P, :].bitcast(I32), 0)
+                nc.sync.dma_start(tab[a][:], tab_words[a].rearrange("p t i -> p (t i)").bitcast(I32))
+            nc.vector.memset(tab_sc[loaded : P // 2, :].bitcast(I32), 0)
+            nc.gpsimd.memset(tab_sc[P // 2 : P, :].bitcast(I32), 0)
             for a in range(PASSES):
                 nc.gpsimd.memset(v_sc[a][:].bitcast(I32), 0)
             nc.vector.tensor_copy(picked_sc[:], tab_sc[:].indirect(idx[:]))
         for a in range(PASSES):
-            for q in range(4):
-                nc.scalar.dma_start(
-                    v_sc[a][32 * q : 32 * q + 4, :].bitcast(I32),
-                    picked_sc[16 * a + 4 * q : 16 * a + 4 * q + 4, :].bitcast(I32),
+            for q in range(P // QUADRANT):
+                row = SCALE_ROWS * a + 4 * q
+                (nc.scalar, nc.gpsimd)[a].dma_start(
+                    v_sc[a][QUADRANT * q : QUADRANT * q + 4, :].bitcast(I32),
+                    picked_sc[row : row + 4, :].bitcast(I32),
                 )
         nc.gpsimd.memset(wp_sc[:].bitcast(I32), 0)
         make_identity(nc, ident[:])
-        for t in range(SLICES):
-            nc.gpsimd.memset(pages[t][:], 0.0)
 
         late = ctx.enter_context(tc.tile_pool(name="late", bufs=1))
 
+        def tagged(shape, dtype, tag):
+            return late.tile(shape, dtype, name=tag, tag=tag, align_bytes=64)
+
+        pages = [late.tile([P, T2], F32, name="page%d" % t) for t in range(SLICES)]
+        for t in range(SLICES):
+            (nc.vector if t < SLICES // 2 else nc.gpsimd).memset(pages[t][:], 0.0)
+
         w_raw = {}
+
+        def raw_tag(t, a, m):
+            return "w_raw%d_%d_%d" % (t, a, m)
 
         def load_w(t):
             for m, w in enumerate((wx, wy)):
                 for a in range(PASSES):
-                    name = "w_raw%d_%d_%d" % (t, a, m)
-                    raw = late.tile([P, PACK, P], F32, name=name, tag=name)
+                    raw = tagged([P, PACK, P], F32, raw_tag(t, a, m))
                     rows = w[a * P * PACK : (a + 1) * P * PACK, t * P : (t + 1) * P]
                     nc.sync.dma_start(raw[:], rows.rearrange("(p i) c -> p i c", i=PACK))
                     w_raw[t, a, m] = raw
 
-        old_sb = {}
-
-        def load_old(t, pool, tag):
-            o = pool.tile([P, T2], F32, name="old%d" % t, tag=tag, align_bytes=64)
-            nc.sync.dma_start(o[:], old[t * P : (t + 1) * P, :])
-            old_sb[t] = o
-
-        load_w(0)
         wgs_sb = [late.tile([P, BANK], F32, name="wgs_sb%d" % h) for h in range(HALVES)]
-        nc.sync.dma_start(wgs_sb[0][:], wgs[:, 0:BANK])
-        load_w(1)
-        nc.sync.dma_start(wgs_sb[1][:], wgs[:, BANK:S])
-        for t in range(2, SLICES):
+        for t in range(SLICES):
             load_w(t)
+            if t < HALVES:
+                nc.sync.dma_start(wgs_sb[t][:], wgs[:, t * BANK : (t + 1) * BANK])
 
         v_w = {}
         for a in range(PASSES):
             for h in range(HALVES):
-                g = keep.tile([P, BANK], U32, name="v%d_%d" % (a, h), align_bytes=64)
-                nc.vector.tensor_copy(
-                    g[:], tab[a][:].bitcast(U32).indirect(idx[:, h * LIST_COLS : (h + 1) * LIST_COLS])
-                )
-                v_w[a, h] = g
+                v_w[a, h] = keep.tile([P, BANK], U32, name="v%d_%d" % (a, h), align_bytes=64)
+                entries = idx[:, h * BANK // LIST_GROUP : (h + 1) * BANK // LIST_GROUP]
+                nc.vector.tensor_copy(v_w[a, h][:], tab[a][:].bitcast(U32).indirect(entries))
 
-        last = SLICES - 1
-        load_old(0, keep, "tab0")
-        load_old(last, keep, "tab1")
         wp_w = late.tile([P, 2 * N], U8, name="wp_w", align_bytes=64)
         nc.sync.dma_start(wp_w[:].bitcast(I32), wp_words[0].bitcast(I32))
-        for q in range(4):
+        for q in range(P // QUADRANT):
             nc.sync.dma_start(
-                wp_sc[32 * q : 32 * q + 4, :].bitcast(I32),
+                wp_sc[QUADRANT * q : QUADRANT * q + 4, :].bitcast(I32),
                 wp_scales[0, 4 * q : 4 * q + 4, :].bitcast(I32),
             )
 
+        old_sb = {}
+
+        def load_old(t, tag):
+            old_sb[t] = tagged([P, T2], F32, tag)
+            nc.sync.dma_start(old_sb[t][:], old[t * P : (t + 1) * P, :])
+
         w_q = {}
 
-        def round_w(copy, dst, t, a, m):
-            copy(
-                dst.rearrange("p (g c) i -> p g i c", c=4),
-                w_raw[t, a, m][:].rearrange("p i (g c) -> p g i c", c=4),
+        def round_w(dst, t, a, m):
+            nc.scalar.copy(
+                dst.rearrange("p (g c) i -> p g i c", c=NEIGHBOURS),
+                w_raw[t, a, m][:].rearrange("p i (g c) -> p g i c", c=NEIGHBOURS),
             )
 
         def code_tiles(t):
@@ -147,10 +152,10 @@ def tile_list_particle_cell_pressure_kernel(
             return codes, scales
 
         def quantise_w(t):
-            wb = late.tile([P, PASSES, 2, P, PACK], BF16, name="w_bf", tag="w_bf%d" % t, align_bytes=64)
+            wb = tagged([P, PASSES, 2, P, PACK], BF16, "w_bf%d" % t)
             for m in range(2):
                 for a in range(PASSES):
-                    round_w(nc.scalar.copy, wb[:, a, m], t, a, m)
+                    round_w(wb[:, a, m], t, a, m)
             codes, scales = code_tiles(t)
             nc.vector.quantize_mx(
                 out=codes[:].bitcast(FP8X4), scales=scales[:], in_=wb[:].rearrange("p a m c i -> p (a m c i)")
@@ -161,37 +166,38 @@ def tile_list_particle_cell_pressure_kernel(
         def negate_wgs(h):
             nc.vector.tensor_scalar(neg_wgs[h][:], wgs_sb[h][:], -1.0, None, MULT)
 
-        def place(t, j0, speed):
-            width = speed.shape[1]
+        def place(t, j0, total, tag):
+            width = total.shape[1]
+            speed = tagged([P, width], F32, tag)
+            nc.scalar.activation(speed[:], total, ACT.Sqrt)
             nc.vector.tensor_tensor(
-                pages[t][:].indirect(idx2[:, j0 // 16 : (j0 + width) // 16]),
+                pages[t][:].indirect(idx2[:, j0 // LIST_GROUP : (j0 + width) // LIST_GROUP]),
                 speed[:],
                 neg_wgs[j0 // BANK][:, j0 % BANK : j0 % BANK + width],
                 MULT,
             )
 
-        def first_speeds():
-            width = BANK // 2
+        def first_half():
             codes, scales = code_tiles(0)
-            acc = [[bank(0)], [bank(1), bank(2)]]
+            acc = [[bank(LOW_BANKS[0])], [bank(TURN_B), bank(TURN_A)]]
             for m in range(2):
                 for a in range(PASSES):
                     wb = late.tile([P, P, PACK], BF16, name="w_bf_first%d_%d" % (a, m), align_bytes=64)
-                    round_w(nc.scalar.copy, wb[:], 0, a, m)
+                    round_w(wb[:], 0, a, m)
                     cols = slice((2 * a + m) * P, (2 * a + m + 1) * P)
                     nc.vector.quantize_mx(
                         out=codes[:, cols].bitcast(FP8X4),
                         scales=scales[:, cols],
                         in_=wb[:].rearrange("p c i -> p (c i)"),
                     )
-                    n = BANK // len(acc[m])
+                    width = BANK // len(acc[m])
                     for k, dst in enumerate(acc[m]):
                         nc.tensor.matmul_mx(
-                            out=dst[:, 0:n],
+                            out=dst[:, 0:width],
                             lhsT=codes[:, cols].bitcast(FP8X4),
                             lhsT_scale=scales[:, cols],
-                            rhs=v_w[a, 0][:, k * n : (k + 1) * n].bitcast(FP8X4),
-                            rhs_scale=v_sc[a][:, k * n : (k + 1) * n],
+                            rhs=v_w[a, 0][:, k * width : (k + 1) * width].bitcast(FP8X4),
+                            rhs_scale=v_sc[a][:, k * width : (k + 1) * width],
                             start=(a == 0),
                             stop=(a == PASSES - 1),
                         )
@@ -200,18 +206,15 @@ def tile_list_particle_cell_pressure_kernel(
             nc.scalar.activation(sq_a[:], acc[0][0][:], ACT.Square)
             totals = []
             for k in range(2):
-                sq_b = late.tile([P, width], F32, name="sq_b", tag=("w_bf2", "sq_b")[k], align_bytes=64)
-                nc.scalar.activation(sq_b[:], acc[1][k][:, 0:width], ACT.Square)
-                total = late.tile([P, width], F32, name="total", tag=("total", "w_bf1")[k], align_bytes=64)
-                nc.vector.tensor_tensor(total[:], sq_a[:, k * width : (k + 1) * width], sq_b[:], ADD)
+                sq_b = tagged([P, PIECE], F32, "sq_b%d" % k)
+                nc.scalar.activation(sq_b[:], acc[1][k][:, 0:PIECE], ACT.Square)
+                total = tagged([P, PIECE], F32, ("total", "w_bf1")[k])
+                nc.vector.tensor_tensor(total[:], sq_a[:, k * PIECE : (k + 1) * PIECE], sq_b[:], ADD)
                 totals.append(total)
             for k in range(2):
-                speed = late.tile([P, width], F32, name="speed_first%d" % k)
-                nc.scalar.activation(speed[:], totals[k][:], ACT.Sqrt)
-                place(0, k * width, speed)
+                place(0, k * PIECE, totals[k][:], "speed_first%d" % k)
 
-        def squares(t, h, sq_tags):
-            acc_banks = ((5, 7), (6, 5))[h]
+        def squares(t, h, acc_banks, second_tag):
             codes, scales = w_q[t]
             result = []
             for k in range(2):
@@ -219,7 +222,7 @@ def tile_list_particle_cell_pressure_kernel(
                 for a in range(PASSES):
                     cols = slice(a * 2 * P, (a + 1) * 2 * P)
                     for e in range(2):
-                        c0 = (2 * k + e) * P
+                        c0 = k * PIECE + e * P
                         j0 = h * BANK + c0
                         nc.tensor.matmul_mx(
                             out=acc[:, e * 2 * P : (e + 1) * 2 * P],
@@ -230,38 +233,34 @@ def tile_list_particle_cell_pressure_kernel(
                             start=(a == 0 and e == 0),
                             stop=(a == PASSES - 1 and e == 1),
                         )
-                if sq_tags[k]:
-                    sq = late.tile([P, BANK], F32, name="sq", tag=sq_tags[k], align_bytes=64)
+                if k == 1 and second_tag:
+                    sq = tagged([P, BANK], F32, second_tag)
                 else:
-                    sq = ring.tile([P, BANK], F32, name="sq", tag="sq", bufs=3)
+                    sq = ring.tile([P, BANK], F32, name="sq", tag="sq", bufs=SQUARE_BUFFERS)
                 nc.scalar.activation(sq[:], acc[:], ACT.Square)
                 result.append(sq)
             return result
 
-        def roots(t, j0, sqs, sum_bank, speed_tag):
+        def summed(sqs, sum_bank):
             total = bank(sum_bank)
             for k, sq in enumerate(sqs):
                 for e in range(2):
-                    o0 = (2 * k + e) * P
+                    j0 = k * PIECE + e * P
                     for m in range(2):
                         c0 = (2 * e + m) * P
                         nc.tensor.matmul(
-                            total[:, o0 : o0 + P],
+                            total[:, j0 : j0 + P],
                             sq[:, c0 : c0 + P],
                             ident[:],
                             start=(m == 0),
                             stop=(m == 1),
                             is_transpose=True,
                         )
-            width = 2 * P * len(sqs)
-            speed = late.tile([P, width], F32, name="speed", tag=speed_tag)
-            nc.scalar.activation(speed[:], total[:, 0:width], ACT.Sqrt)
-            place(t, j0, speed)
-            return speed
+            return total[:, 0 : PIECE * len(sqs)]
 
         z_t = [keep.tile([P, nb, 2, P, 2], BF16, name="z_t%d" % q) for q, (b0, nb) in enumerate(CHUNKS)]
 
-        def turn_into(acc, src, group, first, final):
+        def turn_into(acc, src, group, first):
             blocks = [b for q in group for b in range(CHUNKS[q][0], CHUNKS[q][0] + CHUNKS[q][1])]
             for k, b in enumerate(blocks):
                 nc.tensor.matmul(
@@ -269,71 +268,71 @@ def tile_list_particle_cell_pressure_kernel(
                     src[:, b * P : (b + 1) * P],
                     ident[:],
                     start=(first and k == 0),
-                    stop=(final and k == len(blocks) - 1),
+                    stop=(not first and k == len(blocks) - 1),
                     is_transpose=True,
                 )
 
+        def open_loss(t, group, b):
+            acc = bank(b)
+            turn_into(acc, old_sb[t], group, True)
+            return acc
+
         def close_loss(acc, t, group, copy):
-            turn_into(acc, pages[t], group, False, True)
+            turn_into(acc, pages[t], group, False)
+            words = P // PACK
             c0 = 0
             for q in group:
                 nb = CHUNKS[q][1]
                 copy(
-                    z_t[q][:, :, :, 32 * t : 32 * (t + 1), :],
+                    z_t[q][:, :, :, words * t : words * (t + 1), :],
                     acc[:, c0 : c0 + nb * P].rearrange("c (cb p u e) -> c cb u p e", cb=nb, u=2, e=2),
                 )
                 c0 = c0 + nb * P
 
-        def losses(t, banks):
+        def loss(t, banks):
             for group, b in zip(GROUPS, banks):
-                acc = bank(b)
-                turn_into(acc, old_sb[t], group, True, False)
-                close_loss(acc, t, group, nc.scalar.copy)
+                close_loss(open_loss(t, group, b), t, group, nc.scalar.copy)
 
-        first_speeds()
+        first_half()
+        sqs = squares(0, 1, (TURN_B, TURN_A), "w_bf2")
         quantise_w(1)
         negate_wgs(1)
-        roots(0, BANK, squares(0, 1, ("total", "w_bf2")), 7, "w_raw1_1_1")
-        sqs = squares(1, 0, (None, None))
-        roots(1, 0, sqs[0:1], 4, "speed1")
-        quantise_w(2)
-        roots(1, 2 * P, sqs[1:2], 3, "w_raw2_1_1")
-        roots(1, BANK, squares(1, 1, (None, "w_bf3")), 7, "speed2")
-        sqs = squares(2, 0, ("old1", None))
-        roots(2, 0, sqs[0:1], 4, "speed3")
-        load_old(1, late, "old1")
-        quantise_w(3)
-        roots(2, 2 * P, sqs[1:2], 3, "w_raw3_1_1")
-        roots(2, BANK, squares(2, 1, (None, None)), 7, "speed4")
-        losses(0, LOW_BANKS)
-        roots(3, 0, squares(3, 0, ("old2", None)), 4, "speed5")
-        load_old(2, late, "old2")
-        losses(1, LOW_BANKS)
-        roots(3, BANK, squares(3, 1, (None, None)), 7, "speed6")
-        open_loss = []
-        for q in range(len(CHUNKS) - 1):
-            acc = bank(LOW_BANKS[q])
-            turn_into(acc, old_sb[last], (q,), True, False)
-            open_loss.append(acc)
-        losses(2, HIGH_BANKS)
+        place(0, BANK, summed(sqs, HALF_SUM), raw_tag(1, 1, 1))
+        old_tags = {2: {0: (0, 0), 1: (1, 0), 2: (0, 1)}, LAST: {LAST: (0, 0)}}
+        for t in range(1, SLICES):
+            near, far = (TURN_A, TURN_B) if t % 2 else (TURN_B, TURN_A)
+            sqs = squares(t, 0, (near, HALF_SUM), None)
+            if t < LAST:
+                place(t, 0, summed(sqs[0:1], far), "speed%d_a" % t)
+                quantise_w(t + 1)
+                for s, (a, m) in old_tags[t + 1].items():
+                    load_old(s, raw_tag(t + 1, a, m))
+                place(t, PIECE, summed(sqs[1:2], SPARE_SUM), raw_tag(t + 1, 1, 1))
+            else:
+                place(t, 0, summed(sqs, far), "speed%d_a" % t)
+            sqs = squares(t, 1, (near, far), "w_bf%d" % (t + 2) if t + 2 <= LAST else None)
+            place(t, BANK, summed(sqs, HALF_SUM), "speed%d_b" % t)
+            if t >= 2:
+                loss(t - 2, LOW_BANKS)
+        loss(LAST - 1, HIGH_BANKS)
+        opened = [open_loss(LAST, group, b) for group, b in zip(GROUPS, LOW_BANKS)]
 
         z_q = {}
-        copies = (nc.scalar.copy, nc.vector.tensor_copy)
 
         def quantise_z(q):
-            nb = CHUNKS[q][1]
-            half = nb // 2
+            b0, nb = CHUNKS[q]
             words = z_t[q][:].rearrange("c cb u p e -> c (cb u p e)").bitcast(F32)
-            z_bf = ring.tile([P, nb * P, PACK], BF16, name="z_bf", tag="z_bf", align_bytes=64)
+            z_bf = ring.tile([P, nb * P, PACK], BF16, name="z_bf", tag="z_bf", bufs=1, align_bytes=64)
             z_words = z_bf[:].rearrange("p c i -> p (c i)").bitcast(F32)
-            for d in range(half):
-                turned = bank(WORD_BANKS[(d + CHUNKS[q][0] // 2) % 2])
-                for k in range(4):
-                    w0 = (4 * d + k) * P
+            for d in range(nb // 2):
+                turned = bank(WORD_BANKS[(b0 // 2 + d) % len(WORD_BANKS)])
+                for k in range(BANK // P):
+                    w0 = d * BANK + k * P
                     nc.tensor.transpose(turned[:, k * P : (k + 1) * P], words[:, w0 : w0 + P], ident[:])
-                dst = z_words[:, d * BANK : (d + 1) * BANK].rearrange("p (cb c u) -> p cb c u", cb=2, u=2)
-                src = turned[:].rearrange("p (cb u c) -> p cb c u", cb=2, u=2)
-                copies[1](dst, src)
+                nc.vector.tensor_copy(
+                    z_words[:, d * BANK : (d + 1) * BANK].rearrange("p (cb c u) -> p cb c u", cb=2, u=2),
+                    turned[:].rearrange("p (cb u c) -> p cb c u", cb=2, u=2),
+                )
             z_codes = ring.tile([P, nb * P], U32, name="z_codes", tag="z_codes", align_bytes=64)
             z_scales = ring.tile([P, nb * P], U8, name="z_scales", tag="z_scales", align_bytes=64)
             nc.vector.quantize_mx(
@@ -341,15 +340,13 @@ def tile_list_particle_cell_pressure_kernel(
             )
             z_q[q] = (z_codes, z_scales)
 
-        filled = []
-
-        def pressure(q):
+        def pressure(q, count):
             b0, nb = CHUNKS[q]
             width = nb * P
             per_bank = BANK // width
             z_codes, z_scales = z_q[q]
             for n0 in range(0, N // P, per_bank):
-                acc = bank(OUT_BANKS[len(filled) % len(OUT_BANKS)])
+                acc = bank(OUT_BANKS[count % len(OUT_BANKS)])
                 for k in range(per_bank):
                     n = n0 + k
                     nc.tensor.matmul_mx(
@@ -361,23 +358,21 @@ def tile_list_particle_cell_pressure_kernel(
                         start=True,
                         stop=True,
                     )
-                res = ring.tile([P, per_bank, width], F32, name="res", tag="res", bufs=8)
-                copies[1 if len(filled) % 4 == 3 else 0](res[:].rearrange("p k c -> p (k c)"), acc[:])
+                res = ring.tile([P, per_bank, width], F32, name="res", tag="res", bufs=RESULT_BUFFERS)
+                on_vector = count >= SHARED_FROM and count % 2 == 1
+                (nc.vector.tensor_copy if on_vector else nc.scalar.copy)(res[:].rearrange("p k c -> p (k c)"), acc[:])
                 rows = out[n0 * P : (n0 + per_bank) * P, b0 * P : b0 * P + width]
                 nc.sync.dma_start(rows.rearrange("(k p) c -> p k c", p=P), res[:])
-                filled.append(acc)
+                count = count + 1
+            return count
 
-        close_loss(open_loss[0], last, (0,), copies[0])
-        close_loss(open_loss[1], last, (1,), copies[1])
+        close_loss(opened[0], LAST, GROUPS[0], nc.vector.tensor_copy)
+        close_loss(opened[1], LAST, GROUPS[1], nc.scalar.copy)
         quantise_z(0)
-        close_loss(open_loss[2], last, (2,), copies[0])
-        quantise_z(1)
-        pressure(0)
-        close_loss(open_loss[3], last, (3,), copies[0])
-        acc = bank(LAST_CHUNK_BANK)
-        turn_into(acc, old_sb[last], (4,), True, False)
-        close_loss(acc, last, (4,), copies[0])
-        for q in range(1, len(CHUNKS)):
+        for g in range(2, len(GROUPS)):
+            close_loss(opened[g], LAST, GROUPS[g], nc.scalar.copy)
+        filled = 0
+        for q in range(len(CHUNKS)):
             if q + 1 < len(CHUNKS):
                 quantise_z(q + 1)
-            pressure(q)
+            filled = pressure(q, filled)

@@ -34,9 +34,16 @@ GROUPS = ((0, 1), (2,), (3,), (4,))
 LOW_BANKS = (0, 1, 2, 3)
 HIGH_BANKS = (4, 5, 6, 7)
 SPARE_SUM, TURN_A, TURN_B, HALF_SUM = HIGH_BANKS
-WORD_BANKS = (4, 5)
-OUT_BANKS = (6, 0, 1, 2, 3, 7)
+WORD_BANKS = (7,0,1,2,7,0,1,2)
+OUT_BANKS = (4,5,6,3)*2+(4,5,6,3,7,0,1,2)
 SHARED_FROM = 10
+Z_TAGS = ("z0","z1","z0","z3","z4")
+STORES = ((1,1),(1,1),(1,1,2),(2,2),(2,2))
+ON_VECTOR = (13,15)
+WARM = 0
+WORDS_ON_SCALAR = (1,)
+ROUND_ON_VECTOR = (0,1)
+TAIL = (("r",0),("r",1),("r",2),("r",3),("q",0),("q",1),("p",0),("q",2),("p",1),("q",3),("p",2),("q",4),("p",3),("p",4))
 SQUARE_BUFFERS = 3
 RESULT_BUFFERS = 8
 
@@ -62,67 +69,89 @@ def tile_list_particle_cell_pressure_kernel(
         idx2 = keep.tile([P, S // LIST_GROUP], U16, name="idx2")
         picked_sc = keep.tile([P, S], U8, name="picked_sc", align_bytes=64)
         v_sc = [keep.tile([P, S], U8, name="v_sc%d" % a, align_bytes=64) for a in range(PASSES)]
-        wp_sc = keep.tile([P, N], U8, name="wp_sc", align_bytes=64)
         ident = keep.tile([P, P], F32, name="ident")
-        tab = [keep.tile([P, T], I32, name="tab%d" % a, align_bytes=64) for a in range(PASSES)]
-        with tc.tile_pool(name="early", bufs=1) as early:
-            tab_sc = early.tile([P, T], U8, name="tab_sc", align_bytes=64)
-            loaded = SCALE_ROWS * PASSES
-            nc.sync.dma_start(idx[:], offs)
-            nc.sync.dma_start(tab_sc[0:loaded, :].bitcast(I32), tab_scales.rearrange("a q t -> (a q) t").bitcast(I32))
-            nc.sync.dma_start(idx2[:], offs2)
-            for a in range(PASSES):
-                nc.sync.dma_start(tab[a][:], tab_words[a].rearrange("p t i -> p (t i)").bitcast(I32))
-            nc.vector.memset(tab_sc[loaded : P // 2, :].bitcast(I32), 0)
-            nc.gpsimd.memset(tab_sc[P // 2 : P, :].bitcast(I32), 0)
-            for a in range(PASSES):
-                nc.gpsimd.memset(v_sc[a][:].bitcast(I32), 0)
-            nc.vector.tensor_copy(picked_sc[:], tab_sc[:].indirect(idx[:]))
-        for a in range(PASSES):
-            for q in range(P // QUADRANT):
-                row = SCALE_ROWS * a + 4 * q
-                (nc.scalar, nc.gpsimd)[a].dma_start(
-                    v_sc[a][QUADRANT * q : QUADRANT * q + 4, :].bitcast(I32),
-                    picked_sc[row : row + 4, :].bitcast(I32),
-                )
-        nc.gpsimd.memset(wp_sc[:].bitcast(I32), 0)
-        make_identity(nc, ident[:])
-
-        late = ctx.enter_context(tc.tile_pool(name="late", bufs=1))
-
-        def tagged(shape, dtype, tag):
-            return late.tile(shape, dtype, name=tag, tag=tag, align_bytes=64)
-
-        pages = [late.tile([P, T2], F32, name="page%d" % t) for t in range(SLICES)]
-        for t in range(SLICES):
-            (nc.vector if t < SLICES // 2 else nc.gpsimd).memset(pages[t][:], 0.0)
-
+        tab_last = keep.tile([P, T], I32, name="tab1", tag="tab1", align_bytes=64)
+        pages = [keep.tile([P, T2], F32, name="page%d" % t) for t in range(2)]
         w_raw = {}
+        v_w = {}
 
         def raw_tag(t, a, m):
             return "w_raw%d_%d_%d" % (t, a, m)
 
-        def load_w(t):
-            for m, w in enumerate((wx, wy)):
-                for a in range(PASSES):
-                    raw = tagged([P, PACK, P], F32, raw_tag(t, a, m))
+        def load_w(pool, t, which=((0, 0), (0, 1), (1, 0), (1, 1))):
+            for a, m in which:
+                w = (wx, wy)[m]
+                if True:
+                    raw = pool.tile([P, PACK, P], F32, name=raw_tag(t, a, m), tag=raw_tag(t, a, m), align_bytes=64)
                     rows = w[a * P * PACK : (a + 1) * P * PACK, t * P : (t + 1) * P]
                     nc.sync.dma_start(raw[:], rows.rearrange("(p i) c -> p i c", i=PACK))
                     w_raw[t, a, m] = raw
 
+        def gather_words(a, table, j0, width, tag):
+            words = keep.tile([P, width], U32, name=tag, tag=tag, align_bytes=64)
+            entries = idx[:, j0 // LIST_GROUP : (j0 + width) // LIST_GROUP]
+            nc.vector.tensor_copy(words[:], table[:].bitcast(U32).indirect(entries))
+            for j in range(j0, j0 + width, PIECE):
+                v_w[a, j // PIECE] = words[:, j - j0 : j - j0 + PIECE]
+            return words
+
+        with tc.tile_pool(name="early", bufs=1) as early:
+            tab_sc = early.tile([P, T], U8, name="tab_sc", align_bytes=64)
+            tab_first = early.tile([P, T], I32, name="tab0", align_bytes=64)
+            loaded = SCALE_ROWS * PASSES
+            nc.sync.dma_start(idx[:], offs)
+            nc.sync.dma_start(tab_sc[0:loaded, :].bitcast(I32), tab_scales.rearrange("a q t -> (a q) t").bitcast(I32))
+            for a, table in enumerate((tab_first, tab_last)):
+                nc.sync.dma_start(table[:], tab_words[a].rearrange("p t i -> p (t i)").bitcast(I32))
+                load_w(keep, 0, ((a, 0), (a, 1)))
+            nc.sync.dma_start(idx2[:], offs2)
+            nc.vector.memset(tab_sc[loaded : P // 2, :].bitcast(I32), 0)
+            nc.vector.memset(tab_sc[P // 2 : P, :].bitcast(I32), 0)
+            nc.vector.memset(pages[0][:], 0.0)
+            for a in range(PASSES):
+                nc.gpsimd.memset(v_sc[a][:].bitcast(I32), 0)
+            make_identity(nc, ident[:])
+            nc.gpsimd.memset(pages[1][:], 0.0)
+            nc.vector.tensor_copy(picked_sc[:], tab_sc[:].indirect(idx[:]))
+            for a in range(PASSES):
+                for q in range(P // QUADRANT):
+                    row = SCALE_ROWS * a + 4 * q
+                    (nc.scalar, nc.gpsimd)[a].dma_start(
+                        v_sc[a][QUADRANT * q : QUADRANT * q + 4, :].bitcast(I32),
+                        picked_sc[row : row + 4, :].bitcast(I32),
+                    )
+            first_words = [gather_words(0, tab_first, 0, BANK, "v0_0")]
+            gather_words(0, tab_first, BANK, BANK, "v0_1")
+
+        late = ctx.enter_context(tc.tile_pool(name="late", bufs=1))
+        pages.extend([late.tile([P, T2], F32, name="page%d" % t) for t in range(2, SLICES)])
+        nc.vector.memset(pages[3][:], 0.0)
+        nc.gpsimd.memset(pages[2][:], 0.0)
+        first_words.append(gather_words(1, tab_last, 0, BANK, "v1_0"))
+
+        def tagged(shape, dtype, tag):
+            return late.tile(shape, dtype, name=tag, tag=tag, align_bytes=64)
+
+        wp_sc = tagged([P, N], U8, "wp_sc")
+        nc.gpsimd.memset(wp_sc[:].bitcast(I32), 0)
+
+        old_sb = {}
+
+        def load_old(t):
+            old_sb[t] = tagged([P, T2], F32, "old%d" % t)
+            nc.sync.dma_start(old_sb[t][:], old[t * P : (t + 1) * P, :])
+
         wgs_sb = [late.tile([P, BANK], F32, name="wgs_sb%d" % h) for h in range(HALVES)]
-        for t in range(SLICES):
-            load_w(t)
-            if t < HALVES:
-                nc.sync.dma_start(wgs_sb[t][:], wgs[:, t * BANK : (t + 1) * BANK])
-
-        v_w = {}
-        for a in range(PASSES):
-            for h in range(HALVES):
-                v_w[a, h] = keep.tile([P, BANK], U32, name="v%d_%d" % (a, h), align_bytes=64)
-                entries = idx[:, h * BANK // LIST_GROUP : (h + 1) * BANK // LIST_GROUP]
-                nc.vector.tensor_copy(v_w[a, h][:], tab[a][:].bitcast(U32).indirect(entries))
-
+        load_w(late, 1, ((0, 0),))
+        nc.sync.dma_start(wgs_sb[0][:], wgs[:, 0:BANK])
+        load_w(late, 1, ((0, 1), (1, 0), (1, 1)))
+        nc.sync.dma_start(wgs_sb[1][:], wgs[:, BANK:S])
+        load_w(late, 2)
+        load_old(0)
+        load_w(late, 3)
+        load_old(1)
+        load_old(3)
+        load_old(2)
         wp_w = late.tile([P, 2 * N], U8, name="wp_w", align_bytes=64)
         nc.sync.dma_start(wp_w[:].bitcast(I32), wp_words[0].bitcast(I32))
         for q in range(P // QUADRANT):
@@ -131,16 +160,10 @@ def tile_list_particle_cell_pressure_kernel(
                 wp_scales[0, 4 * q : 4 * q + 4, :].bitcast(I32),
             )
 
-        old_sb = {}
-
-        def load_old(t, tag):
-            old_sb[t] = tagged([P, T2], F32, tag)
-            nc.sync.dma_start(old_sb[t][:], old[t * P : (t + 1) * P, :])
-
         w_q = {}
 
-        def round_w(dst, t, a, m):
-            nc.scalar.copy(
+        def round_into(dst, t, a, m, copy):
+            copy(
                 dst.rearrange("p (g c) i -> p g i c", c=NEIGHBOURS),
                 w_raw[t, a, m][:].rearrange("p i (g c) -> p g i c", c=NEIGHBOURS),
             )
@@ -151,112 +174,118 @@ def tile_list_particle_cell_pressure_kernel(
             w_q[t] = (codes, scales)
             return codes, scales
 
+        w_bf = {}
+
+        def round_w(t, pieces, tag=None):
+            if t not in w_bf:
+                w_bf[t] = tagged([P, PASSES, 2, P, PACK], BF16, tag)
+            for a, m in pieces:
+                round_into(w_bf[t][:, a, m], t, a, m, nc.scalar.copy)
+
         def quantise_w(t):
-            wb = tagged([P, PASSES, 2, P, PACK], BF16, "w_bf%d" % t)
-            for m in range(2):
-                for a in range(PASSES):
-                    round_w(wb[:, a, m], t, a, m)
             codes, scales = code_tiles(t)
             nc.vector.quantize_mx(
-                out=codes[:].bitcast(FP8X4), scales=scales[:], in_=wb[:].rearrange("p a m c i -> p (a m c i)")
+                out=codes[:].bitcast(FP8X4), scales=scales[:], in_=w_bf[t][:].rearrange("p a m c i -> p (a m c i)")
             )
 
-        neg_wgs = [late.tile([P, BANK], F32, name="neg_wgs%d" % h) for h in range(HALVES)]
+        neg_wgs = {}
 
-        def negate_wgs(h):
+        def negate_wgs(h, tag):
+            neg_wgs[h] = tagged([P, BANK], F32, tag)
             nc.vector.tensor_scalar(neg_wgs[h][:], wgs_sb[h][:], -1.0, None, MULT)
 
-        def place(t, j0, total, tag):
-            width = total.shape[1]
-            speed = tagged([P, width], F32, tag)
-            nc.scalar.activation(speed[:], total, ACT.Sqrt)
+        def prepare_w(t, a, ms, pool, tag):
+            wb = pool.tile([P, len(ms), P, PACK], BF16, name=tag, tag=tag, align_bytes=64)
+            for k, m in enumerate(ms):
+                round_into(wb[:, k], t, a, m, nc.scalar.copy)
+            codes, scales = w_q[t] if t in w_q else code_tiles(t)
+            cols = slice((2 * a + ms[0]) * P, (2 * a + ms[-1] + 1) * P)
+            nc.vector.quantize_mx(
+                out=codes[:, cols].bitcast(FP8X4), scales=scales[:, cols], in_=wb[:].rearrange("p m c i -> p (m c i)")
+            )
+
+        def scatter(t, j0, speed):
+            width = speed.shape[1]
             nc.vector.tensor_tensor(
                 pages[t][:].indirect(idx2[:, j0 // LIST_GROUP : (j0 + width) // LIST_GROUP]),
-                speed[:],
+                speed,
                 neg_wgs[j0 // BANK][:, j0 % BANK : j0 % BANK + width],
                 MULT,
             )
 
-        def first_half():
+        def first_products():
             codes, scales = code_tiles(0)
-            acc = [[bank(LOW_BANKS[0])], [bank(TURN_B), bank(TURN_A)]]
-            for m in range(2):
-                for a in range(PASSES):
-                    wb = late.tile([P, P, PACK], BF16, name="w_bf_first%d_%d" % (a, m), align_bytes=64)
-                    round_w(wb[:], 0, a, m)
+            acc = [[bank(7)], [bank(5), bank(6)]]
+            for a in range(PASSES):
+                for m in range(2):
+                    wb = keep.tile([P, P, PACK], BF16, name="w_bf_first%d_%d" % (a, m), tag="w_bf_first%d_%d" % (a, m), align_bytes=64)
+                    round_into(wb[:], 0, a, m, nc.scalar.copy)
                     cols = slice((2 * a + m) * P, (2 * a + m + 1) * P)
                     nc.vector.quantize_mx(
                         out=codes[:, cols].bitcast(FP8X4),
                         scales=scales[:, cols],
                         in_=wb[:].rearrange("p c i -> p (c i)"),
                     )
+                    if a == 1:
+                        gather_words(1, tab_last, BANK + m * PIECE, PIECE, "w_bf_first%d_%d" % (a, m))
                     width = BANK // len(acc[m])
                     for k, dst in enumerate(acc[m]):
                         nc.tensor.matmul_mx(
                             out=dst[:, 0:width],
                             lhsT=codes[:, cols].bitcast(FP8X4),
                             lhsT_scale=scales[:, cols],
-                            rhs=v_w[a, 0][:, k * width : (k + 1) * width].bitcast(FP8X4),
+                            rhs=first_words[a][:, k * width : (k + 1) * width].bitcast(FP8X4),
                             rhs_scale=v_sc[a][:, k * width : (k + 1) * width],
                             start=(a == 0),
                             stop=(a == PASSES - 1),
                         )
-            negate_wgs(0)
-            sq_a = late.tile([P, BANK], F32, name="sq_a")
-            nc.scalar.activation(sq_a[:], acc[0][0][:], ACT.Square)
-            totals = []
-            for k in range(2):
-                sq_b = tagged([P, PIECE], F32, "sq_b%d" % k)
-                nc.scalar.activation(sq_b[:], acc[1][k][:, 0:PIECE], ACT.Square)
-                total = tagged([P, PIECE], F32, ("total", "w_bf1")[k])
-                nc.vector.tensor_tensor(total[:], sq_a[:, k * PIECE : (k + 1) * PIECE], sq_b[:], ADD)
-                totals.append(total)
-            for k in range(2):
-                place(0, k * PIECE, totals[k][:], "speed_first%d" % k)
+            return acc
 
-        def squares(t, h, acc_banks, second_tag):
+        def products(n, k, b):
+            t, h = divmod(n, HALVES)
             codes, scales = w_q[t]
-            result = []
-            for k in range(2):
-                acc = bank(acc_banks[k])
-                for a in range(PASSES):
-                    cols = slice(a * 2 * P, (a + 1) * 2 * P)
-                    for e in range(2):
-                        c0 = k * PIECE + e * P
-                        j0 = h * BANK + c0
-                        nc.tensor.matmul_mx(
-                            out=acc[:, e * 2 * P : (e + 1) * 2 * P],
-                            lhsT=v_w[a, h][:, c0 : c0 + P].bitcast(FP8X4),
-                            lhsT_scale=v_sc[a][:, j0 : j0 + P],
-                            rhs=codes[:, cols].bitcast(FP8X4),
-                            rhs_scale=scales[:, cols],
-                            start=(a == 0 and e == 0),
-                            stop=(a == PASSES - 1 and e == 1),
-                        )
-                if k == 1 and second_tag:
-                    sq = tagged([P, BANK], F32, second_tag)
-                else:
-                    sq = ring.tile([P, BANK], F32, name="sq", tag="sq", bufs=SQUARE_BUFFERS)
-                nc.scalar.activation(sq[:], acc[:], ACT.Square)
-                result.append(sq)
-            return result
-
-        def summed(sqs, sum_bank):
-            total = bank(sum_bank)
-            for k, sq in enumerate(sqs):
+            acc = bank(b)
+            for a in range(PASSES):
+                cols = slice(a * 2 * P, (a + 1) * 2 * P)
                 for e in range(2):
-                    j0 = k * PIECE + e * P
-                    for m in range(2):
-                        c0 = (2 * e + m) * P
-                        nc.tensor.matmul(
-                            total[:, j0 : j0 + P],
-                            sq[:, c0 : c0 + P],
-                            ident[:],
-                            start=(m == 0),
-                            stop=(m == 1),
-                            is_transpose=True,
-                        )
-            return total[:, 0 : PIECE * len(sqs)]
+                    c0 = k * PIECE + e * P
+                    j0 = h * BANK + c0
+                    nc.tensor.matmul_mx(
+                        out=acc[:, e * 2 * P : (e + 1) * 2 * P],
+                        lhsT=v_w[a, 2 * h + k][:, e * P : (e + 1) * P].bitcast(FP8X4),
+                        lhsT_scale=v_sc[a][:, j0 : j0 + P],
+                        rhs=codes[:, cols].bitcast(FP8X4),
+                        rhs_scale=scales[:, cols],
+                        start=(a == 0 and e == 0),
+                        stop=(a == PASSES - 1 and e == 1),
+                    )
+            return acc
+
+        def square(acc, tag=None):
+            if tag:
+                sq = tagged([P, BANK], F32, tag)
+            else:
+                sq = ring.tile([P, BANK], F32, name="sq", tag="sq", bufs=SQUARE_BUFFERS)
+            nc.scalar.activation(sq[:], acc[:], ACT.Square)
+            return sq
+
+        def summed(sq, b):
+            total = bank(b)
+            for e in range(2):
+                for m in range(2):
+                    c0 = (2 * e + m) * P
+                    nc.tensor.matmul(
+                        total[:, e * P : (e + 1) * P],
+                        sq[:, c0 : c0 + P],
+                        ident[:],
+                        start=(m == 0),
+                        stop=(m == 1),
+                        is_transpose=True,
+                    )
+            return total[:, 0:PIECE]
+
+        def root(dst, total):
+            nc.scalar.activation(dst, total, ACT.Sqrt)
 
         z_t = [keep.tile([P, nb, 2, P, 2], BF16, name="z_t%d" % q) for q, (b0, nb) in enumerate(CHUNKS)]
 
@@ -277,8 +306,7 @@ def tile_list_particle_cell_pressure_kernel(
             turn_into(acc, old_sb[t], group, True)
             return acc
 
-        def close_loss(acc, t, group, copy):
-            turn_into(acc, pages[t], group, False)
+        def round_loss(acc, t, group, copy):
             words = P // PACK
             c0 = 0
             for q in group:
@@ -289,52 +317,99 @@ def tile_list_particle_cell_pressure_kernel(
                 )
                 c0 = c0 + nb * P
 
-        def loss(t, banks):
-            for group, b in zip(GROUPS, banks):
-                close_loss(open_loss(t, group, b), t, group, nc.scalar.copy)
+        def close_loss(acc, t, group, copy):
+            turn_into(acc, pages[t], group, False)
+            round_loss(acc, t, group, copy)
 
-        first_half()
-        sqs = squares(0, 1, (TURN_B, TURN_A), "w_bf2")
-        quantise_w(1)
-        negate_wgs(1)
-        place(0, BANK, summed(sqs, HALF_SUM), raw_tag(1, 1, 1))
-        old_tags = {2: {0: (0, 0), 1: (1, 0), 2: (0, 1)}, LAST: {LAST: (0, 0)}}
-        for t in range(1, SLICES):
-            near, far = (TURN_A, TURN_B) if t % 2 else (TURN_B, TURN_A)
-            sqs = squares(t, 0, (near, HALF_SUM), None)
-            if t < LAST:
-                place(t, 0, summed(sqs[0:1], far), "speed%d_a" % t)
-                quantise_w(t + 1)
-                for s, (a, m) in old_tags[t + 1].items():
-                    load_old(s, raw_tag(t + 1, a, m))
-                place(t, PIECE, summed(sqs[1:2], SPARE_SUM), raw_tag(t + 1, 1, 1))
+        def loss(t, g, b):
+            close_loss(open_loss(t, GROUPS[g], b), t, GROUPS[g], nc.scalar.copy)
+
+        QAT = {2: 1, 3: 1}
+        SPLIT = (1, 2, 4, 7)
+        ACC = (0, 1)
+        SUMS = (None, 2, 3, 4, 5, 6, 7, 2)
+        acc = first_products()
+        prepare_w(1, 0, (0,), late, "w_bf1")
+        negate_wgs(0, "neg_wgs0")
+        sq_a = late.tile([P, BANK], F32, name="sq_a")
+        nc.scalar.activation(sq_a[:], acc[0][0][:], ACT.Square)
+        totals = []
+        for k in range(2):
+            sq_b = tagged([P, PIECE], F32, "sq_b%d" % k)
+            nc.scalar.activation(sq_b[:], acc[1][k][:, 0:PIECE], ACT.Square)
+            total = tagged([P, PIECE], F32, "total%d" % k)
+            nc.vector.tensor_tensor(total[:], sq_a[:, k * PIECE : (k + 1) * PIECE], sq_b[:], ADD)
+            totals.append(total)
+        accs = [products(1, k, ACC[k]) for k in range(2)]
+        speed = tagged([P, PIECE], F32, "speed0_0")
+        root(speed[:], totals[0][:])
+        scatter(0, 0, speed[:])
+        prepare_w(1, 0, (1,), late, "sq_b0")
+        negate_wgs(1, "speed0_0")
+        prepare_w(1, 1, (0, 1), late, "total0")
+        speed = tagged([P, PIECE], F32, raw_tag(1, 0, 1))
+        root(speed[:], totals[1][:])
+        scatter(0, PIECE, speed[:])
+        for n in range(1, 2 * SLICES):
+            t, h = divmod(n, HALVES)
+            near, far = ACC if n % 2 else ACC[::-1]
+            sums = (3 if n == 6 else near, SUMS[n])
+            if n > 1:
+                accs = [products(n, 0, near), products(n, 1, far)]
+            tw, a = divmod(n + 3, PASSES)
+            held = raw_tag(1, 1, 1) if n == 1 else "sq_held%d" % n
+            sqs = [square(accs[0], raw_tag(1, 1, 0) if n == 1 else None), square(accs[1], held if n in (1, 3) else None)]
+            totals = [summed(sqs[k], sums[k]) for k in range(2)]
+            if n in SPLIT:
+                for k in range(2):
+                    late_w = h == 0 and tw <= LAST and k == QAT[tw]
+                    if late_w:
+                        round_w(tw, ((1, 0), (1, 1)))
+                        quantise_w(tw)
+                    speed = tagged([P, PIECE], F32, raw_tag(tw, a, 1) if late_w else "speed6" if (n, k) == (7, 1) else "speed%d_%d" % (n, k))
+                    root(speed[:], totals[k])
+                    scatter(t, h * BANK + k * PIECE, speed[:])
             else:
-                place(t, 0, summed(sqs, far), "speed%d_a" % t)
-            sqs = squares(t, 1, (near, far), "w_bf%d" % (t + 2) if t + 2 <= LAST else None)
-            place(t, BANK, summed(sqs, HALF_SUM), "speed%d_b" % t)
-            if t >= 2:
-                loss(t - 2, LOW_BANKS)
-        loss(LAST - 1, HIGH_BANKS)
-        opened = [open_loss(LAST, group, b) for group, b in zip(GROUPS, LOW_BANKS)]
+                late_w = h == 0 and t + 1 in QAT
+                if late_w:
+                    round_w(t + 1, ((1, 0), (1, 1)))
+                    quantise_w(t + 1)
+                speed = tagged([P, BANK], F32, raw_tag(t + 1, 1, 1) if late_w else "speed%d" % n)
+                for k in range(2):
+                    root(speed[:, k * PIECE : (k + 1) * PIECE], totals[k])
+                scatter(t, h * BANK, speed[:])
+            if h == 1 and tw <= LAST:
+                round_w(tw, ((0, 0), (0, 1)), held)
+            if n >= 3:
+                for g in range(2):
+                    loss((n - 3) // 2, 2 * (1 - h) + g, 3 if n == 7 and g == 0 else SUMS[n - 1])
+        for g in range(2):
+            loss(LAST - 1, 2 + g, g)
+        opened = [open_loss(LAST, group, b) for group, b in zip(GROUPS, (4, 5, 6, 3))]
 
         z_q = {}
+        used = []
+        spare_one = [raw_tag(t, a, m) for t in (2, 3) for a in range(PASSES) for m in range(2)]
+        spare_two = ["res_last", "sq_held3", raw_tag(1, 1, 1), "old1", "old0"]
 
         def quantise_z(q):
             b0, nb = CHUNKS[q]
             words = z_t[q][:].rearrange("c cb u p e -> c (cb u p e)").bitcast(F32)
-            z_bf = ring.tile([P, nb * P, PACK], BF16, name="z_bf", tag="z_bf", bufs=1, align_bytes=64)
+            z_bf = tagged([P, nb * P, PACK], BF16, Z_TAGS[q])
             z_words = z_bf[:].rearrange("p c i -> p (c i)").bitcast(F32)
-            for d in range(nb // 2):
-                turned = bank(WORD_BANKS[(b0 // 2 + d) % len(WORD_BANKS)])
-                for k in range(BANK // P):
+            for d in range(max(1, nb // 2)):
+                per = min(nb, 2)
+                turned = bank(WORD_BANKS[len(used)])
+                used.append(d)
+                for k in range(2 * per):
                     w0 = d * BANK + k * P
                     nc.tensor.transpose(turned[:, k * P : (k + 1) * P], words[:, w0 : w0 + P], ident[:])
-                nc.vector.tensor_copy(
-                    z_words[:, d * BANK : (d + 1) * BANK].rearrange("p (cb c u) -> p cb c u", cb=2, u=2),
-                    turned[:].rearrange("p (cb u c) -> p cb c u", cb=2, u=2),
+                (nc.scalar.copy if q in WORDS_ON_SCALAR else nc.vector.tensor_copy)(
+                    z_words[:, d * BANK : d * BANK + 2 * per * P].rearrange("p (cb c u) -> p cb c u", cb=per, u=2),
+                    turned[:, 0 : 2 * per * P].rearrange("p (cb u c) -> p cb c u", cb=per, u=2),
                 )
-            z_codes = ring.tile([P, nb * P], U32, name="z_codes", tag="z_codes", align_bytes=64)
-            z_scales = ring.tile([P, nb * P], U8, name="z_scales", tag="z_scales", align_bytes=64)
+            z_codes = tagged([P, nb * P], U32, "z_codes%d" % q)
+            z_scales = tagged([P, nb * P], U8, "z_scales%d" % q)
             nc.vector.quantize_mx(
                 out=z_codes[:].bitcast(FP8X4), scales=z_scales[:], in_=z_bf[:].rearrange("p c i -> p (c i)")
             )
@@ -345,34 +420,37 @@ def tile_list_particle_cell_pressure_kernel(
             width = nb * P
             per_bank = BANK // width
             z_codes, z_scales = z_q[q]
-            for n0 in range(0, N // P, per_bank):
-                acc = bank(OUT_BANKS[count % len(OUT_BANKS)])
-                for k in range(per_bank):
-                    n = n0 + k
-                    nc.tensor.matmul_mx(
-                        out=acc[:, k * width : (k + 1) * width],
-                        lhsT=wp_w[:, 2 * n * P : 2 * (n + 1) * P].bitcast(FP4X4),
-                        lhsT_scale=wp_sc[:, n * P : (n + 1) * P],
-                        rhs=z_codes[:].bitcast(FP8X4),
-                        rhs_scale=z_scales[:],
-                        start=True,
-                        stop=True,
-                    )
-                res = ring.tile([P, per_bank, width], F32, name="res", tag="res", bufs=RESULT_BUFFERS)
-                on_vector = count >= SHARED_FROM and count % 2 == 1
-                (nc.vector.tensor_copy if on_vector else nc.scalar.copy)(res[:].rearrange("p k c -> p (k c)"), acc[:])
-                rows = out[n0 * P : (n0 + per_bank) * P, b0 * P : b0 * P + width]
+            n0 = 0
+            for banks in STORES[q]:
+                res = tagged([P, banks * per_bank, width], F32, (spare_two if banks > 1 else spare_one).pop())
+                for s in range(banks):
+                    acc = bank(OUT_BANKS[count])
+                    for k in range(per_bank):
+                        n = n0 + s * per_bank + k
+                        nc.tensor.matmul_mx(
+                            out=acc[:, k * width : (k + 1) * width],
+                            lhsT=wp_w[:, 2 * n * P : 2 * (n + 1) * P].bitcast(FP4X4),
+                            lhsT_scale=wp_sc[:, n * P : (n + 1) * P],
+                            rhs=z_codes[:].bitcast(FP8X4),
+                            rhs_scale=z_scales[:],
+                            start=True,
+                            stop=True,
+                        )
+                    copy = nc.vector.tensor_copy if count in ON_VECTOR else nc.scalar.copy
+                    copy(res[:, s * per_bank : (s + 1) * per_bank, :].rearrange("p k c -> p (k c)"), acc[:])
+                    count = count + 1
+                rows = out[n0 * P : (n0 + banks * per_bank) * P, b0 * P : b0 * P + width]
                 nc.sync.dma_start(rows.rearrange("(k p) c -> p k c", p=P), res[:])
-                count = count + 1
+                n0 = n0 + banks * per_bank
             return count
 
-        close_loss(opened[0], LAST, GROUPS[0], nc.vector.tensor_copy)
-        close_loss(opened[1], LAST, GROUPS[1], nc.scalar.copy)
-        quantise_z(0)
-        for g in range(2, len(GROUPS)):
-            close_loss(opened[g], LAST, GROUPS[g], nc.scalar.copy)
+        for g in range(len(GROUPS)):
+            turn_into(opened[g], pages[LAST], GROUPS[g], False)
         filled = 0
-        for q in range(len(CHUNKS)):
-            if q + 1 < len(CHUNKS):
-                quantise_z(q + 1)
-            filled = pressure(q, filled)
+        for kind, k in TAIL:
+            if kind == "r":
+                round_loss(opened[k], LAST, GROUPS[k], nc.vector.tensor_copy if k in ROUND_ON_VECTOR else nc.scalar.copy)
+            elif kind == "q":
+                quantise_z(k)
+            else:
+                filled = pressure(k, filled)

@@ -40,7 +40,7 @@ SHARED_FROM = 10
 Z_TAGS = ("z0","z1","z0","z3","z4")
 STORES = ((1,1),(1,1),(1,1,2),(2,2),(2,2))
 ON_VECTOR = (13,15)
-WARM = 0
+WARM = 3
 WORDS_ON_SCALAR = (1,)
 ROUND_ON_VECTOR = (0,1)
 TAIL = (("r",0),("r",1),("r",2),("r",3),("q",0),("q",1),("p",0),("q",2),("p",1),("q",3),("p",2),("q",4),("p",3),("p",4))
@@ -386,6 +386,17 @@ def tile_list_particle_cell_pressure_kernel(
         for g in range(2):
             loss(LAST - 1, 2 + g, g)
         opened = [open_loss(LAST, group, b) for group, b in zip(GROUPS, (4, 5, 6, 3))]
+        warm = bank(SUMS[7])
+        for k in range(WARM):
+            nc.tensor.matmul_mx(
+                out=warm[:],
+                lhsT=w_q[LAST][0][:, 0:P].bitcast(FP8X4),
+                lhsT_scale=w_q[LAST][1][:, 0:P],
+                rhs=first_words[0][:].bitcast(FP8X4),
+                rhs_scale=v_sc[0][:, 0:BANK],
+                start=True,
+                stop=True,
+            )
 
         z_q = {}
         used = []

@@ -34,8 +34,8 @@ GROUPS = ((0, 1), (2,), (3,), (4,))
 LOW_BANKS = (0, 1, 2, 3)
 HIGH_BANKS = (4, 5, 6, 7)
 SPARE_SUM, TURN_A, TURN_B, HALF_SUM = HIGH_BANKS
-WORD_BANKS = (7,0,1,2,7,0,1,2)
-OUT_BANKS = (4,5,6,3)*2+(4,5,6,3,7,0,1,2)
+WORD_BANKS = (1,2,0,3)*2
+OUT_BANKS = (4,5,6,7)*3+(1,2,0,3)
 SHARED_FROM = 10
 Z_TAGS = ("z0","z1","z0","z3","z4")
 STORES = ((1,1),(1,1),(1,1,2),(2,2),(2,2))
@@ -44,7 +44,8 @@ WARM = 3
 WORDS_ON_SCALAR = (1,)
 ROUND_ON_VECTOR = (0,1)
 TAIL = (("r",0),("r",1),("r",2),("r",3),("q",0),("q",1),("p",0),("q",2),("p",1),("q",3),("p",2),("q",4),("p",3),("p",4))
-SQUARE_BUFFERS = 3
+WHOLE_FROM = 4
+SQUARE_BUFFERS = 4
 RESULT_BUFFERS = 8
 
 
@@ -190,10 +191,6 @@ def tile_list_particle_cell_pressure_kernel(
 
         neg_wgs = {}
 
-        def negate_wgs(h, tag):
-            neg_wgs[h] = tagged([P, BANK], F32, tag)
-            nc.vector.tensor_scalar(neg_wgs[h][:], wgs_sb[h][:], -1.0, None, MULT)
-
         def prepare_w(t, a, ms, pool, tag):
             wb = pool.tile([P, len(ms), P, PACK], BF16, name=tag, tag=tag, align_bytes=64)
             for k, m in enumerate(ms):
@@ -209,7 +206,7 @@ def tile_list_particle_cell_pressure_kernel(
             nc.vector.tensor_tensor(
                 pages[t][:].indirect(idx2[:, j0 // LIST_GROUP : (j0 + width) // LIST_GROUP]),
                 speed,
-                neg_wgs[j0 // BANK][:, j0 % BANK : j0 % BANK + width],
+                neg_wgs[j0 + width > BANK][:, j0 : j0 + width],
                 MULT,
             )
 
@@ -269,9 +266,9 @@ def tile_list_particle_cell_pressure_kernel(
             nc.scalar.activation(sq[:], acc[:], ACT.Square)
             return sq
 
-        def summed(sq, b):
-            total = bank(b)
-            for e in range(2):
+        def summed(sq, total, k, blocks=(0, 1)):
+            total = total[:, k * PIECE : (k + 1) * PIECE]
+            for e in blocks:
                 for m in range(2):
                     c0 = (2 * e + m) * P
                     nc.tensor.matmul(
@@ -282,7 +279,7 @@ def tile_list_particle_cell_pressure_kernel(
                         stop=(m == 1),
                         is_transpose=True,
                     )
-            return total[:, 0:PIECE]
+            return total
 
         def root(dst, total):
             nc.scalar.activation(dst, total, ACT.Sqrt)
@@ -327,11 +324,12 @@ def tile_list_particle_cell_pressure_kernel(
         QAT = {2: 1, 3: 1}
         SPLIT = (1, 2, 4, 7)
         ACC = (0, 1)
-        SUMS = (None, 2, 3, 4, 5, 6, 7, 2)
+        SPLIT_SUMS = {1: (0, 2), 2: (1, 3), 7: (0, 1)}
         acc = first_products()
         prepare_w(1, 0, (0,), late, "w_bf1")
-        negate_wgs(0, "neg_wgs0")
-        sq_a = late.tile([P, BANK], F32, name="sq_a")
+        neg_wgs[0] = tagged([P, BANK], F32, "neg_wgs0")
+        nc.vector.tensor_scalar(neg_wgs[0][:], wgs_sb[0][:], -1.0, None, MULT)
+        sq_a = tagged([P, BANK], F32, "sq_a")
         nc.scalar.activation(sq_a[:], acc[0][0][:], ACT.Square)
         totals = []
         for k in range(2):
@@ -345,48 +343,65 @@ def tile_list_particle_cell_pressure_kernel(
         root(speed[:], totals[0][:])
         scatter(0, 0, speed[:])
         prepare_w(1, 0, (1,), late, "sq_b0")
-        negate_wgs(1, "speed0_0")
-        prepare_w(1, 1, (0, 1), late, "total0")
-        speed = tagged([P, PIECE], F32, raw_tag(1, 0, 1))
+        prepare_w(1, 1, (0, 1), late, "sq_b1")
+        speed = tagged([P, PIECE], F32, raw_tag(1, 1, 1))
         root(speed[:], totals[1][:])
         scatter(0, PIECE, speed[:])
+        neg_wgs[1] = tagged([P, S], F32, "sq_b1")
+        nc.vector.tensor_scalar(neg_wgs[1][:, BANK:S], wgs_sb[1][:], -1.0, None, MULT)
+        ALL = ((0, 0), (0, 1), (1, 0), (1, 1))
         for n in range(1, 2 * SLICES):
             t, h = divmod(n, HALVES)
-            near, far = ACC if n % 2 else ACC[::-1]
-            sums = (3 if n == 6 else near, SUMS[n])
+            near, far = {2: (1, 0), 5: (2, 3), 7: (2, 3)}.get(n, ACC)
             if n > 1:
                 accs = [products(n, 0, near), products(n, 1, far)]
-            tw, a = divmod(n + 3, PASSES)
-            held = raw_tag(1, 1, 1) if n == 1 else "sq_held%d" % n
-            sqs = [square(accs[0], raw_tag(1, 1, 0) if n == 1 else None), square(accs[1], held if n in (1, 3) else None)]
-            totals = [summed(sqs[k], sums[k]) for k in range(2)]
-            if n in SPLIT:
-                for k in range(2):
-                    late_w = h == 0 and tw <= LAST and k == QAT[tw]
-                    if late_w:
-                        round_w(tw, ((1, 0), (1, 1)))
-                        quantise_w(tw)
-                    speed = tagged([P, PIECE], F32, raw_tag(tw, a, 1) if late_w else "speed6" if (n, k) == (7, 1) else "speed%d_%d" % (n, k))
-                    root(speed[:], totals[k])
-                    scatter(t, h * BANK + k * PIECE, speed[:])
+            if n == 2:
+                round_w(2, ALL[:2], "total1")
+            held = {1: "total1"}.get(n)
+            sqs = [square(accs[0], raw_tag(1, 1, 0) if n == 1 else None), square(accs[1], held)]
+            if n == 7:
+                break
+            if n in SPLIT_SUMS:
+                totals = [summed(sqs[k], bank(SPLIT_SUMS[n][k]), 0) for k in range(2)]
             else:
-                late_w = h == 0 and t + 1 in QAT
-                if late_w:
-                    round_w(t + 1, ((1, 0), (1, 1)))
-                    quantise_w(t + 1)
-                speed = tagged([P, BANK], F32, raw_tag(t + 1, 1, 1) if late_w else "speed%d" % n)
+                both = bank(1 + n)
                 for k in range(2):
-                    root(speed[:, k * PIECE : (k + 1) * PIECE], totals[k])
-                scatter(t, h * BANK, speed[:])
-            if h == 1 and tw <= LAST:
-                round_w(tw, ((0, 0), (0, 1)), held)
-            if n >= 3:
-                for g in range(2):
-                    loss((n - 3) // 2, 2 * (1 - h) + g, 3 if n == 7 and g == 0 else SUMS[n - 1])
-        for g in range(2):
-            loss(LAST - 1, 2 + g, g)
-        opened = [open_loss(LAST, group, b) for group, b in zip(GROUPS, (4, 5, 6, 3))]
-        warm = bank(SUMS[7])
+                    summed(sqs[k], both, k)
+                totals = [both[:]]
+            tag = "speed%d" % n
+            if n in (2, 3):
+                round_w(n, ALL[2:] if n == 2 else ALL, raw_tag(2, 1, 0))
+                quantise_w(n)
+                tag = raw_tag(n, 1, 1)
+            whole = t >= WHOLE_FROM
+            if not whole or h == 0:
+                speed = tagged([P, S if whole else BANK], F32, tag)
+            c0 = h * BANK if whole else 0
+            for total in totals:
+                root(speed[:, c0 : c0 + total.shape[1]], total)
+                c0 = c0 + total.shape[1]
+            if not whole or h == 1:
+                scatter(t, 0 if whole else h * BANK, speed[:])
+            if n == 3:
+                nc.scalar.copy(neg_wgs[1][:, 0:BANK], neg_wgs[0][:])
+            if 4 <= n <= 7:
+                loss(0, n - 4, n)
+        speed = tagged([P, PIECE], F32, "speed7")
+        root(speed[:], summed(sqs[0], bank(0), 0))
+        scatter(LAST, BANK, speed[:])
+        loss(0, 3, 7)
+        for g in range(4):
+            loss(1, g, (2, 3, 0, 1)[g])
+        opened = [open_loss(LAST, group, b) for group, b in zip(GROUPS, (4, 5, 6, 7))]
+        for g in range(3):
+            loss(2, g, (2, 3, 0)[g])
+        totals = [summed(sqs[1], bank(b), 0, (e,)) for e, b in enumerate((3, 0))]
+        speed = tagged([P, PIECE], F32, "speed6")
+        for e in range(2):
+            root(speed[:, e * P : (e + 1) * P], totals[e][:, e * P : (e + 1) * P])
+        scatter(LAST, BANK + PIECE, speed[:])
+        loss(2, 3, 3)
+        warm = bank(0)
         for k in range(WARM):
             nc.tensor.matmul_mx(
                 out=warm[:],
@@ -400,8 +415,8 @@ def tile_list_particle_cell_pressure_kernel(
 
         z_q = {}
         used = []
-        spare_one = [raw_tag(t, a, m) for t in (2, 3) for a in range(PASSES) for m in range(2)]
-        spare_two = ["res_last", "sq_held3", raw_tag(1, 1, 1), "old1", "old0"]
+        spare_one = [raw_tag(t, a, m) for t in (2, 3) for a in range(PASSES) for m in range(2) if (t, a, m) != (2, 1, 0)]
+        spare_two = ["res_last", "speed4", raw_tag(1, 1, 1), "old1", "old0"]
 
         def quantise_z(q):
             b0, nb = CHUNKS[q]

@@ -34,17 +34,17 @@ GROUPS = ((0, 1), (2,), (3,), (4,))
 LOW_BANKS = (0, 1, 2, 3)
 HIGH_BANKS = (4, 5, 6, 7)
 SPARE_SUM, TURN_A, TURN_B, HALF_SUM = HIGH_BANKS
-WORD_BANKS = (1,2,0,3)*2
-OUT_BANKS = (4,5,6,7)*3+(1,2,0,3)
+WORD_BANKS = (2,3,0,1)*2
+OUT_BANKS = (4,5,6,7)*3+(0,1,2,3)
 SHARED_FROM = 10
 Z_TAGS = ("z0","z1","z0","z3","z4")
 STORES = ((1,1),(1,1),(1,1,2),(2,2),(2,2))
 ON_VECTOR = (13,15)
-WARM = 3
+WARM = 0
 WORDS_ON_SCALAR = (1,)
 ROUND_ON_VECTOR = (0,1)
 TAIL = (("r",0),("r",1),("r",2),("r",3),("q",0),("q",1),("p",0),("q",2),("p",1),("q",3),("p",2),("q",4),("p",3),("p",4))
-WHOLE_FROM = 4
+WHOLE_FROM = 3
 SQUARE_BUFFERS = 4
 RESULT_BUFFERS = 8
 
@@ -266,9 +266,9 @@ def tile_list_particle_cell_pressure_kernel(
             nc.scalar.activation(sq[:], acc[:], ACT.Square)
             return sq
 
-        def summed(sq, total, k, blocks=(0, 1)):
+        def summed(sq, total, k):
             total = total[:, k * PIECE : (k + 1) * PIECE]
-            for e in blocks:
+            for e in range(2):
                 for m in range(2):
                     c0 = (2 * e + m) * P
                     nc.tensor.matmul(
@@ -359,8 +359,6 @@ def tile_list_particle_cell_pressure_kernel(
                 round_w(2, ALL[:2], "total1")
             held = {1: "total1"}.get(n)
             sqs = [square(accs[0], raw_tag(1, 1, 0) if n == 1 else None), square(accs[1], held)]
-            if n == 7:
-                break
             if n in SPLIT_SUMS:
                 totals = [summed(sqs[k], bank(SPLIT_SUMS[n][k]), 0) for k in range(2)]
             else:
@@ -386,32 +384,10 @@ def tile_list_particle_cell_pressure_kernel(
                 nc.scalar.copy(neg_wgs[1][:, 0:BANK], neg_wgs[0][:])
             if 4 <= n <= 7:
                 loss(0, n - 4, n)
-        speed = tagged([P, PIECE], F32, "speed7")
-        root(speed[:], summed(sqs[0], bank(0), 0))
-        scatter(LAST, BANK, speed[:])
-        loss(0, 3, 7)
-        for g in range(4):
-            loss(1, g, (2, 3, 0, 1)[g])
+        for t in (1, 2):
+            for g in range(4):
+                loss(t, g, (2, 3, 0, 1)[g])
         opened = [open_loss(LAST, group, b) for group, b in zip(GROUPS, (4, 5, 6, 7))]
-        for g in range(3):
-            loss(2, g, (2, 3, 0)[g])
-        totals = [summed(sqs[1], bank(b), 0, (e,)) for e, b in enumerate((3, 0))]
-        speed = tagged([P, PIECE], F32, "speed6")
-        for e in range(2):
-            root(speed[:, e * P : (e + 1) * P], totals[e][:, e * P : (e + 1) * P])
-        scatter(LAST, BANK + PIECE, speed[:])
-        loss(2, 3, 3)
-        warm = bank(0)
-        for k in range(WARM):
-            nc.tensor.matmul_mx(
-                out=warm[:],
-                lhsT=w_q[LAST][0][:, 0:P].bitcast(FP8X4),
-                lhsT_scale=w_q[LAST][1][:, 0:P],
-                rhs=first_words[0][:].bitcast(FP8X4),
-                rhs_scale=v_sc[0][:, 0:BANK],
-                start=True,
-                stop=True,
-            )
 
         z_q = {}
         used = []

@@ -34,17 +34,17 @@ GROUPS = ((0, 1), (2,), (3,), (4,))
 LOW_BANKS = (0, 1, 2, 3)
 HIGH_BANKS = (4, 5, 6, 7)
 SPARE_SUM, TURN_A, TURN_B, HALF_SUM = HIGH_BANKS
-WORD_BANKS = (2,3,0,1)*2
+WORD_BANKS = (3,2,0,1)*2
 OUT_BANKS = (4,5,6,7)*3+(0,1,2,3)
 SHARED_FROM = 10
-Z_TAGS = ("z0","z1","z0","z3","z4")
+Z_TAGS = ("z0","z1","z0","total1","total0")
 STORES = ((1,1),(1,1),(1,1,2),(2,2),(2,2))
 ON_VECTOR = (13,15)
 WARM = 0
 WORDS_ON_SCALAR = (1,)
 ROUND_ON_VECTOR = (0,1)
 TAIL = (("r",0),("r",1),("r",2),("r",3),("q",0),("q",1),("p",0),("q",2),("p",1),("q",3),("p",2),("q",4),("p",3),("p",4))
-WHOLE_FROM = 3
+WHOLE_FROM = 4
 SQUARE_BUFFERS = 4
 RESULT_BUFFERS = 8
 
@@ -71,8 +71,7 @@ def tile_list_particle_cell_pressure_kernel(
         picked_sc = keep.tile([P, S], U8, name="picked_sc", align_bytes=64)
         v_sc = [keep.tile([P, S], U8, name="v_sc%d" % a, align_bytes=64) for a in range(PASSES)]
         ident = keep.tile([P, P], F32, name="ident")
-        tab_last = keep.tile([P, T], I32, name="tab1", tag="tab1", align_bytes=64)
-        pages = [keep.tile([P, T2], F32, name="page%d" % t) for t in range(2)]
+        tab = [keep.tile([P, T], I32, name="tab%d" % a, align_bytes=64) for a in range(PASSES)]
         w_raw = {}
         v_w = {}
 
@@ -98,41 +97,39 @@ def tile_list_particle_cell_pressure_kernel(
 
         with tc.tile_pool(name="early", bufs=1) as early:
             tab_sc = early.tile([P, T], U8, name="tab_sc", align_bytes=64)
-            tab_first = early.tile([P, T], I32, name="tab0", align_bytes=64)
             loaded = SCALE_ROWS * PASSES
             nc.sync.dma_start(idx[:], offs)
             nc.sync.dma_start(tab_sc[0:loaded, :].bitcast(I32), tab_scales.rearrange("a q t -> (a q) t").bitcast(I32))
-            for a, table in enumerate((tab_first, tab_last)):
-                nc.sync.dma_start(table[:], tab_words[a].rearrange("p t i -> p (t i)").bitcast(I32))
-                load_w(keep, 0, ((a, 0), (a, 1)))
             nc.sync.dma_start(idx2[:], offs2)
+            for a in range(PASSES):
+                nc.sync.dma_start(tab[a][:], tab_words[a].rearrange("p t i -> p (t i)").bitcast(I32))
             nc.vector.memset(tab_sc[loaded : P // 2, :].bitcast(I32), 0)
-            nc.vector.memset(tab_sc[P // 2 : P, :].bitcast(I32), 0)
-            nc.vector.memset(pages[0][:], 0.0)
+            nc.gpsimd.memset(tab_sc[P // 2 : P, :].bitcast(I32), 0)
             for a in range(PASSES):
                 nc.gpsimd.memset(v_sc[a][:].bitcast(I32), 0)
-            make_identity(nc, ident[:])
-            nc.gpsimd.memset(pages[1][:], 0.0)
             nc.vector.tensor_copy(picked_sc[:], tab_sc[:].indirect(idx[:]))
-            for a in range(PASSES):
-                for q in range(P // QUADRANT):
-                    row = SCALE_ROWS * a + 4 * q
-                    (nc.scalar, nc.gpsimd)[a].dma_start(
-                        v_sc[a][QUADRANT * q : QUADRANT * q + 4, :].bitcast(I32),
-                        picked_sc[row : row + 4, :].bitcast(I32),
-                    )
-            first_words = [gather_words(0, tab_first, 0, BANK, "v0_0")]
-            gather_words(0, tab_first, BANK, BANK, "v0_1")
+        for a in range(PASSES):
+            for q in range(P // QUADRANT):
+                row = SCALE_ROWS * a + 4 * q
+                (nc.scalar, nc.gpsimd)[a].dma_start(
+                    v_sc[a][QUADRANT * q : QUADRANT * q + 4, :].bitcast(I32),
+                    picked_sc[row : row + 4, :].bitcast(I32),
+                )
+        make_identity(nc, ident[:])
 
         late = ctx.enter_context(tc.tile_pool(name="late", bufs=1))
-        pages.extend([late.tile([P, T2], F32, name="page%d" % t) for t in range(2, SLICES)])
-        nc.vector.memset(pages[3][:], 0.0)
-        nc.gpsimd.memset(pages[2][:], 0.0)
-        first_words.append(gather_words(1, tab_last, 0, BANK, "v1_0"))
 
         def tagged(shape, dtype, tag):
             return late.tile(shape, dtype, name=tag, tag=tag, align_bytes=64)
 
+        pages = [late.tile([P, T2], F32, name="page%d" % t) for t in range(SLICES)]
+        for t in range(SLICES):
+            (nc.vector if t < SLICES // 2 else nc.gpsimd).memset(pages[t][:], 0.0)
+        load_w(late, 0, ((0, 0), (1, 0), (0, 1), (1, 1)))
+        first_words = []
+        for a in range(PASSES):
+            first_words.append(gather_words(a, tab[a], 0, BANK, "v%d_0" % a))
+            gather_words(a, tab[a], BANK, BANK, "v%d_1" % a)
         wp_sc = tagged([P, N], U8, "wp_sc")
         nc.gpsimd.memset(wp_sc[:].bitcast(I32), 0)
 
@@ -142,11 +139,9 @@ def tile_list_particle_cell_pressure_kernel(
             old_sb[t] = tagged([P, T2], F32, "old%d" % t)
             nc.sync.dma_start(old_sb[t][:], old[t * P : (t + 1) * P, :])
 
-        wgs_sb = [late.tile([P, BANK], F32, name="wgs_sb%d" % h) for h in range(HALVES)]
-        load_w(late, 1, ((0, 0),))
-        nc.sync.dma_start(wgs_sb[0][:], wgs[:, 0:BANK])
-        load_w(late, 1, ((0, 1), (1, 0), (1, 1)))
-        nc.sync.dma_start(wgs_sb[1][:], wgs[:, BANK:S])
+        wgs_sb = late.tile([P, S], F32, name="wgs_sb")
+        nc.sync.dma_start(wgs_sb[:], wgs)
+        load_w(late, 1)
         load_w(late, 2)
         load_old(0)
         load_w(late, 3)
@@ -189,7 +184,6 @@ def tile_list_particle_cell_pressure_kernel(
                 out=codes[:].bitcast(FP8X4), scales=scales[:], in_=w_bf[t][:].rearrange("p a m c i -> p (a m c i)")
             )
 
-        neg_wgs = {}
 
         def prepare_w(t, a, ms, pool, tag):
             wb = pool.tile([P, len(ms), P, PACK], BF16, name=tag, tag=tag, align_bytes=64)
@@ -206,15 +200,15 @@ def tile_list_particle_cell_pressure_kernel(
             nc.vector.tensor_tensor(
                 pages[t][:].indirect(idx2[:, j0 // LIST_GROUP : (j0 + width) // LIST_GROUP]),
                 speed,
-                neg_wgs[j0 + width > BANK][:, j0 : j0 + width],
+                neg_wgs[:, j0 : j0 + width],
                 MULT,
             )
 
         def first_products():
             codes, scales = code_tiles(0)
-            acc = [[bank(7)], [bank(5), bank(6)]]
-            for a in range(PASSES):
-                for m in range(2):
+            acc = [[bank(7)], [bank(0), bank(1)]]
+            for m in range(2):
+                for a in range(PASSES):
                     wb = keep.tile([P, P, PACK], BF16, name="w_bf_first%d_%d" % (a, m), tag="w_bf_first%d_%d" % (a, m), align_bytes=64)
                     round_into(wb[:], 0, a, m, nc.scalar.copy)
                     cols = slice((2 * a + m) * P, (2 * a + m + 1) * P)
@@ -223,8 +217,6 @@ def tile_list_particle_cell_pressure_kernel(
                         scales=scales[:, cols],
                         in_=wb[:].rearrange("p c i -> p (c i)"),
                     )
-                    if a == 1:
-                        gather_words(1, tab_last, BANK + m * PIECE, PIECE, "w_bf_first%d_%d" % (a, m))
                     width = BANK // len(acc[m])
                     for k, dst in enumerate(acc[m]):
                         nc.tensor.matmul_mx(
@@ -323,12 +315,12 @@ def tile_list_particle_cell_pressure_kernel(
 
         QAT = {2: 1, 3: 1}
         SPLIT = (1, 2, 4, 7)
+        LOSSES = {4: ((0, 0),), 5: ((0, 1), (0, 2)), 6: ((0, 3), (1, 0)), 7: ((1, 1), (1, 2), (1, 3))}
         ACC = (0, 1)
-        SPLIT_SUMS = {1: (0, 2), 2: (1, 3), 7: (0, 1)}
+        SPLIT_SUMS = {1: (0, 2), 2: (1, 3), 4: (4, 5), 7: (0, 1)}
         acc = first_products()
-        prepare_w(1, 0, (0,), late, "w_bf1")
-        neg_wgs[0] = tagged([P, BANK], F32, "neg_wgs0")
-        nc.vector.tensor_scalar(neg_wgs[0][:], wgs_sb[0][:], -1.0, None, MULT)
+        neg_wgs = keep.tile([P, S], F32, name="neg_wgs", tag="w_bf_first1_1", align_bytes=64)
+        nc.vector.tensor_scalar(neg_wgs[:], wgs_sb[:], -1.0, None, MULT)
         sq_a = tagged([P, BANK], F32, "sq_a")
         nc.scalar.activation(sq_a[:], acc[0][0][:], ACT.Square)
         totals = []
@@ -342,35 +334,31 @@ def tile_list_particle_cell_pressure_kernel(
         speed = tagged([P, PIECE], F32, "speed0_0")
         root(speed[:], totals[0][:])
         scatter(0, 0, speed[:])
-        prepare_w(1, 0, (1,), late, "sq_b0")
-        prepare_w(1, 1, (0, 1), late, "sq_b1")
-        speed = tagged([P, PIECE], F32, raw_tag(1, 1, 1))
+        speed = tagged([P, PIECE], F32, "speed0_1")
         root(speed[:], totals[1][:])
         scatter(0, PIECE, speed[:])
-        neg_wgs[1] = tagged([P, S], F32, "sq_b1")
-        nc.vector.tensor_scalar(neg_wgs[1][:, BANK:S], wgs_sb[1][:], -1.0, None, MULT)
         ALL = ((0, 0), (0, 1), (1, 0), (1, 1))
         for n in range(1, 2 * SLICES):
             t, h = divmod(n, HALVES)
-            near, far = {2: (1, 0), 5: (2, 3), 7: (2, 3)}.get(n, ACC)
+            near, far = {2: (1, 0), 5: (3, 2), 7: (3, 2)}.get(n, ACC)
             if n > 1:
                 accs = [products(n, 0, near), products(n, 1, far)]
             if n == 2:
-                round_w(2, ALL[:2], "total1")
-            held = {1: "total1"}.get(n)
-            sqs = [square(accs[0], raw_tag(1, 1, 0) if n == 1 else None), square(accs[1], held)]
+                round_w(2, ALL[:3], "total0")
+            held = {1: "total0", 2: "sq_held"}.get(n)
+            sqs = [square(accs[0]), square(accs[1], held)]
             if n in SPLIT_SUMS:
                 totals = [summed(sqs[k], bank(SPLIT_SUMS[n][k]), 0) for k in range(2)]
             else:
-                both = bank(1 + n)
+                both = bank(2 if n == 3 else 1 + n)
                 for k in range(2):
                     summed(sqs[k], both, k)
                 totals = [both[:]]
             tag = "speed%d" % n
-            if n in (2, 3):
-                round_w(n, ALL[2:] if n == 2 else ALL, raw_tag(2, 1, 0))
+            if n in (1, 2, 3):
+                round_w(n, ALL[3:] if n == 2 else ALL, "total1" if n == 1 else "sq_held")
                 quantise_w(n)
-                tag = raw_tag(n, 1, 1)
+                tag = raw_tag(n, 1, 0)
             whole = t >= WHOLE_FROM
             if not whole or h == 0:
                 speed = tagged([P, S if whole else BANK], F32, tag)
@@ -380,19 +368,16 @@ def tile_list_particle_cell_pressure_kernel(
                 c0 = c0 + total.shape[1]
             if not whole or h == 1:
                 scatter(t, 0 if whole else h * BANK, speed[:])
-            if n == 3:
-                nc.scalar.copy(neg_wgs[1][:, 0:BANK], neg_wgs[0][:])
-            if 4 <= n <= 7:
-                loss(0, n - 4, n)
-        for t in (1, 2):
-            for g in range(4):
-                loss(t, g, (2, 3, 0, 1)[g])
+            for tl, g in LOSSES.get(n, ()):
+                loss(tl, g, 4 + g)
+        for g in range(4):
+            loss(2, g, (3, 2, 0, 1)[g])
         opened = [open_loss(LAST, group, b) for group, b in zip(GROUPS, (4, 5, 6, 7))]
 
         z_q = {}
         used = []
-        spare_one = [raw_tag(t, a, m) for t in (2, 3) for a in range(PASSES) for m in range(2) if (t, a, m) != (2, 1, 0)]
-        spare_two = ["res_last", "speed4", raw_tag(1, 1, 1), "old1", "old0"]
+        spare_one = [raw_tag(t, a, m) for t in (2, 3) for a in range(PASSES) for m in range(2)]
+        spare_two = ["res_last", "speed4", "sq_held", "old1", "old0"]
 
         def quantise_z(q):
             b0, nb = CHUNKS[q]

@@ -71,7 +71,7 @@ def tile_list_particle_cell_pressure_kernel(
         picked_sc = keep.tile([P, S], U8, name="picked_sc", align_bytes=64)
         v_sc = [keep.tile([P, S], U8, name="v_sc%d" % a, align_bytes=64) for a in range(PASSES)]
         ident = keep.tile([P, P], F32, name="ident")
-        tab = [keep.tile([P, T], I32, name="tab%d" % a, align_bytes=64) for a in range(PASSES)]
+        tab = [keep.tile([P, T], I32, name="tab%d" % a, tag="tab%d" % a, align_bytes=64) for a in range(PASSES)]
         w_raw = {}
         v_w = {}
 
@@ -111,7 +111,7 @@ def tile_list_particle_cell_pressure_kernel(
         for a in range(PASSES):
             for q in range(P // QUADRANT):
                 row = SCALE_ROWS * a + 4 * q
-                (nc.scalar, nc.gpsimd)[a].dma_start(
+                (nc.gpsimd, nc.scalar)[a].dma_start(
                     v_sc[a][QUADRANT * q : QUADRANT * q + 4, :].bitcast(I32),
                     picked_sc[row : row + 4, :].bitcast(I32),
                 )
@@ -122,16 +122,16 @@ def tile_list_particle_cell_pressure_kernel(
         def tagged(shape, dtype, tag):
             return late.tile(shape, dtype, name=tag, tag=tag, align_bytes=64)
 
-        pages = [late.tile([P, T2], F32, name="page%d" % t) for t in range(SLICES)]
-        for t in range(SLICES):
-            (nc.vector if t < SLICES // 2 else nc.gpsimd).memset(pages[t][:], 0.0)
+        second_page = late.tile([P, T2], F32, name="page1")
+        nc.vector.memset(second_page[:], 0.0)
         load_w(late, 0, ((0, 0), (1, 0), (0, 1), (1, 1)))
         first_words = []
         for a in range(PASSES):
             first_words.append(gather_words(a, tab[a], 0, BANK, "v%d_0" % a))
-            gather_words(a, tab[a], BANK, BANK, "v%d_1" % a)
-        wp_sc = tagged([P, N], U8, "wp_sc")
-        nc.gpsimd.memset(wp_sc[:].bitcast(I32), 0)
+            if a == 0:
+                gather_words(a, tab[a], BANK, BANK, "v0_1")
+                pages = [keep.tile([P, T2], F32, name="page0", tag="tab0", align_bytes=64), second_page]
+                nc.vector.memset(pages[0][:], 0.0)
 
         old_sb = {}
 
@@ -148,14 +148,6 @@ def tile_list_particle_cell_pressure_kernel(
         load_old(1)
         load_old(3)
         load_old(2)
-        wp_w = late.tile([P, 2 * N], U8, name="wp_w", align_bytes=64)
-        nc.sync.dma_start(wp_w[:].bitcast(I32), wp_words[0].bitcast(I32))
-        for q in range(P // QUADRANT):
-            nc.sync.dma_start(
-                wp_sc[QUADRANT * q : QUADRANT * q + 4, :].bitcast(I32),
-                wp_scales[0, 4 * q : 4 * q + 4, :].bitcast(I32),
-            )
-
         w_q = {}
 
         def round_into(dst, t, a, m, copy):
@@ -319,8 +311,7 @@ def tile_list_particle_cell_pressure_kernel(
         ACC = (0, 1)
         SPLIT_SUMS = {1: (0, 2), 2: (1, 3), 4: (4, 5), 7: (0, 1)}
         acc = first_products()
-        neg_wgs = keep.tile([P, S], F32, name="neg_wgs", tag="w_bf_first1_1", align_bytes=64)
-        nc.vector.tensor_scalar(neg_wgs[:], wgs_sb[:], -1.0, None, MULT)
+        gather_words(1, tab[1], BANK, BANK, "w_bf_first1_1")
         sq_a = tagged([P, BANK], F32, "sq_a")
         nc.scalar.activation(sq_a[:], acc[0][0][:], ACT.Square)
         totals = []
@@ -330,6 +321,9 @@ def tile_list_particle_cell_pressure_kernel(
             total = tagged([P, PIECE], F32, "total%d" % k)
             nc.vector.tensor_tensor(total[:], sq_a[:, k * PIECE : (k + 1) * PIECE], sq_b[:], ADD)
             totals.append(total)
+            if k == 0:
+                neg_wgs = tagged([P, S], F32, "sq_b0")
+                nc.vector.tensor_scalar(neg_wgs[:], wgs_sb[:], -1.0, None, MULT)
         accs = [products(1, k, ACC[k]) for k in range(2)]
         speed = tagged([P, PIECE], F32, "speed0_0")
         root(speed[:], totals[0][:])
@@ -337,6 +331,16 @@ def tile_list_particle_cell_pressure_kernel(
         speed = tagged([P, PIECE], F32, "speed0_1")
         root(speed[:], totals[1][:])
         scatter(0, PIECE, speed[:])
+        wp_sc = tagged([P, N], U8, "speed0_1")
+        nc.gpsimd.memset(wp_sc[:].bitcast(I32), 0)
+        wp_w = late.tile([P, 2 * N], U8, name="wp_w", align_bytes=64)
+        nc.sync.dma_start(wp_w[:].bitcast(I32), wp_words[0].bitcast(I32))
+        for q in range(P // QUADRANT):
+            nc.sync.dma_start(
+                wp_sc[QUADRANT * q : QUADRANT * q + 4, :].bitcast(I32),
+                wp_scales[0, 4 * q : 4 * q + 4, :].bitcast(I32),
+            )
+
         ALL = ((0, 0), (0, 1), (1, 0), (1, 1))
         for n in range(1, 2 * SLICES):
             t, h = divmod(n, HALVES)
@@ -358,6 +362,9 @@ def tile_list_particle_cell_pressure_kernel(
             if n in (1, 2, 3):
                 round_w(n, ALL[3:] if n == 2 else ALL, "total1" if n == 1 else "sq_held")
                 quantise_w(n)
+                if n < 3:
+                    pages.append(tagged([P, T2], F32, ("total1", "total0")[n - 1]))
+                    nc.gpsimd.memset(pages[n + 1][:], 0.0)
                 tag = raw_tag(n, 1, 0)
             whole = t >= WHOLE_FROM
             if not whole or h == 0:

@@ -34,8 +34,8 @@ GROUPS = ((0, 1), (2,), (3,), (4,))
 LOW_BANKS = (0, 1, 2, 3)
 HIGH_BANKS = (4, 5, 6, 7)
 SPARE_SUM, TURN_A, TURN_B, HALF_SUM = HIGH_BANKS
-WORD_BANKS = (3,2,0,1)*2
-OUT_BANKS = (4,5,6,7)*3+(0,1,2,3)
+WORD_BANKS = (6,7,0,1)*2
+OUT_BANKS = (2,3,4,5)*3+(6,7,0,1)
 SHARED_FROM = 10
 Z_TAGS = ("z0","z1","z0","total1","total0")
 STORES = ((1,1),(1,1),(1,1,2),(2,2),(2,2))
@@ -307,9 +307,9 @@ def tile_list_particle_cell_pressure_kernel(
 
         QAT = {2: 1, 3: 1}
         SPLIT = (1, 2, 4, 7)
-        LOSSES = {4: ((0, 0),), 5: ((0, 1), (0, 2)), 6: ((0, 3), (1, 0)), 7: ((1, 1), (1, 2), (1, 3))}
+        LOSSES = {3: ((0, 0),), 4: ((0, 1),), 5: ((0, 2), (0, 3)), 6: ((1, 0), (1, 1), (1, 2), (1, 3))}
         ACC = (0, 1)
-        SPLIT_SUMS = {1: (0, 2), 2: (1, 3), 4: (4, 5), 7: (0, 1)}
+        SPLIT_SUMS = {1: (0, 2), 2: (1, 6), 3: (2, 7), 4: (4, 5), 5: (6, 7), 7: (0, 1)}
         acc = first_products()
         gather_words(1, tab[1], BANK, BANK, "w_bf_first1_1")
         sq_a = tagged([P, BANK], F32, "sq_a")
@@ -344,7 +344,7 @@ def tile_list_particle_cell_pressure_kernel(
         ALL = ((0, 0), (0, 1), (1, 0), (1, 1))
         for n in range(1, 2 * SLICES):
             t, h = divmod(n, HALVES)
-            near, far = {2: (1, 0), 5: (3, 2), 7: (3, 2)}.get(n, ACC)
+            near, far = {2: (1, 0), 5: (3, 2), 7: (6, 7)}.get(n, ACC)
             if n > 1:
                 accs = [products(n, 0, near), products(n, 1, far)]
             if n == 2:
@@ -354,7 +354,7 @@ def tile_list_particle_cell_pressure_kernel(
             if n in SPLIT_SUMS:
                 totals = [summed(sqs[k], bank(SPLIT_SUMS[n][k]), 0) for k in range(2)]
             else:
-                both = bank(2 if n == 3 else 1 + n)
+                both = bank(3)
                 for k in range(2):
                     summed(sqs[k], both, k)
                 totals = [both[:]]
@@ -376,10 +376,11 @@ def tile_list_particle_cell_pressure_kernel(
             if not whole or h == 1:
                 scatter(t, 0 if whole else h * BANK, speed[:])
             for tl, g in LOSSES.get(n, ()):
-                loss(tl, g, 4 + g)
+                loss(tl, g, (6, 7, 4, 5)[g])
+        opened = [open_loss(LAST, group, b) for group, b in zip(GROUPS, (2, 3, 4, 5))]
+        waiting = [open_loss(LAST - 1, group, b) for group, b in zip(GROUPS, (6, 7, 0, 1))]
         for g in range(4):
-            loss(2, g, (3, 2, 0, 1)[g])
-        opened = [open_loss(LAST, group, b) for group, b in zip(GROUPS, (4, 5, 6, 7))]
+            close_loss(waiting[g], LAST - 1, GROUPS[g], nc.scalar.copy)
 
         z_q = {}
         used = []

@@ -21,32 +21,14 @@ ADD = mybir.AluOpType.add
 PACK = 4
 PASSES = K // (P * PACK)
 SLICES = H // P
-LAST = SLICES - 1
 BANK = 512
 PIECE = BANK // 2
-HALVES = S // BANK
 QUADRANT = 32
-SCALE_ROWS = 16
+PLANE_ROWS = 4
 LIST_GROUP = 16
 NEIGHBOURS = 4
 CHUNKS = ((0, 2), (2, 2), (4, 4), (8, 4), (12, 4))
 GROUPS = ((0, 1), (2,), (3,), (4,))
-LOW_BANKS = (0, 1, 2, 3)
-HIGH_BANKS = (4, 5, 6, 7)
-SPARE_SUM, TURN_A, TURN_B, HALF_SUM = HIGH_BANKS
-WORD_BANKS = (6,7,0,1)*2
-OUT_BANKS = (2,3,4,5)*3+(6,7,0,1)
-SHARED_FROM = 10
-Z_TAGS = ("z0","z1","z0","total1","total0")
-STORES = ((1,1),(1,1),(1,1,2),(2,2),(2,2))
-ON_VECTOR = (13,15)
-WARM = 0
-WORDS_ON_SCALAR = (1,)
-ROUND_ON_VECTOR = (0,1)
-TAIL = (("r",0),("r",1),("r",2),("r",3),("q",0),("q",1),("p",0),("q",2),("p",1),("q",3),("p",2),("q",4),("p",3),("p",4))
-WHOLE_FROM = 4
-SQUARE_BUFFERS = 4
-RESULT_BUFFERS = 8
 
 
 def tile_list_particle_cell_pressure_kernel(
@@ -55,140 +37,114 @@ def tile_list_particle_cell_pressure_kernel(
     nc = tc.nc
     with ExitStack() as ctx:
         keep = ctx.enter_context(tc.tile_pool(name="keep", bufs=1))
-        ring = ctx.enter_context(tc.tile_pool(name="ring", bufs=2))
         psum = ctx.enter_context(tc.psum_pool(name="psum", bufs=1))
 
         def bank(b):
             return psum.tile([P, BANK], F32, name="bank%d" % b, tag="bank%d" % b)
 
+        def tile(shape, dtype, tag):
+            return keep.tile(shape, dtype, name=tag, tag=tag, align_bytes=64)
+
+        idx = keep.tile([P, S // LIST_GROUP], U16, name="idx")
+        idx2 = keep.tile([P, S // LIST_GROUP], U16, name="idx2")
+        tab_sc = tile([P, T], U8, "tab_sc")
+        nc.vector.memset(tab_sc[:].bitcast(I32), 0)
+        tab = [tile([P, T], I32, "tab%d" % a) for a in range(PASSES)]
+        w_raw = {}
+        old_sb = {}
+
+        def load_table(a, c0, c1):
+            words = tab_words[a].rearrange("p t i -> p (t i)").bitcast(I32)
+            nc.sync.dma_start(tab[a][:, c0:c1], words[:, c0:c1])
+
+        def load_w(t, order):
+            for a, m in order:
+                raw = tile([P, PACK, P], F32, "w_raw%d_%d_%d" % (t, a, m))
+                rows = (wx, wy)[m][a * P * PACK : (a + 1) * P * PACK, t * P : (t + 1) * P]
+                nc.sync.dma_start(raw[:], rows.rearrange("(p i) c -> p i c", i=PACK))
+                w_raw[t, a, m] = raw
+
+        def load_old(t, c0=0, c1=T2):
+            if c0 == 0:
+                old_sb[t] = tile([P, T2], F32, "old%d" % t)
+            nc.sync.dma_start(old_sb[t][:, c0:c1], old[t * P : (t + 1) * P, c0:c1])
+
+        def load_wgs(h):
+            raw = tile([P, BANK], F32, "wgs%d" % h)
+            nc.sync.dma_start(raw[:], wgs[:, h * BANK : (h + 1) * BANK])
+            return raw
+
+        BY_PASS = ((0, 0), (0, 1), (1, 0), (1, 1))
+        nc.sync.dma_start(idx[:], offs)
+        load_w(0, BY_PASS)
+        nc.sync.dma_start(idx2[:], offs2)
+        load_table(0, 0, T // 2)
+        load_table(0, T // 2, T)
+        for q in (0, 2, 1, 3):
+            nc.sync.dma_start(
+                tab_sc[QUADRANT * q : QUADRANT * q + PASSES * PLANE_ROWS, :].bitcast(I32),
+                tab_scales[:, PLANE_ROWS * q : PLANE_ROWS * (q + 1), :].bitcast(I32),
+            )
+        load_table(1, 0, T)
+        wgs_raw = [load_wgs(0)]
+        load_w(1, BY_PASS)
+        wgs_raw.append(load_wgs(1))
+        load_w(2, BY_PASS)
+        load_old(0, 0, T2 // 2)
+        load_w(3, BY_PASS)
+        load_old(0, T2 // 2, T2)
+        load_old(1)
+        load_old(3)
+        load_old(2)
+
         one = keep.tile([P, 8], F32, name="one")
         nc.gpsimd.memset(one[:], 1.0)
         preload = keep.tile([P, 8], F32, name="preload")
         nc.scalar.activation(preload[:], one[:], ACT.Sqrt)
-
-        idx = keep.tile([P, S // LIST_GROUP], U16, name="idx")
-        idx2 = keep.tile([P, S // LIST_GROUP], U16, name="idx2")
-        picked_sc = keep.tile([P, S], U8, name="picked_sc", align_bytes=64)
-        v_sc = [keep.tile([P, S], U8, name="v_sc%d" % a, align_bytes=64) for a in range(PASSES)]
         ident = keep.tile([P, P], F32, name="ident")
-        tab = [keep.tile([P, T], I32, name="tab%d" % a, tag="tab%d" % a, align_bytes=64) for a in range(PASSES)]
-        w_raw = {}
-        v_w = {}
-
-        def raw_tag(t, a, m):
-            return "w_raw%d_%d_%d" % (t, a, m)
-
-        def load_w(pool, t, which=((0, 0), (0, 1), (1, 0), (1, 1))):
-            for a, m in which:
-                w = (wx, wy)[m]
-                if True:
-                    raw = pool.tile([P, PACK, P], F32, name=raw_tag(t, a, m), tag=raw_tag(t, a, m), align_bytes=64)
-                    rows = w[a * P * PACK : (a + 1) * P * PACK, t * P : (t + 1) * P]
-                    nc.sync.dma_start(raw[:], rows.rearrange("(p i) c -> p i c", i=PACK))
-                    w_raw[t, a, m] = raw
-
-        def gather_words(a, table, j0, width, tag):
-            words = keep.tile([P, width], U32, name=tag, tag=tag, align_bytes=64)
-            entries = idx[:, j0 // LIST_GROUP : (j0 + width) // LIST_GROUP]
-            nc.vector.tensor_copy(words[:], table[:].bitcast(U32).indirect(entries))
-            for j in range(j0, j0 + width, PIECE):
-                v_w[a, j // PIECE] = words[:, j - j0 : j - j0 + PIECE]
-            return words
-
-        with tc.tile_pool(name="early", bufs=1) as early:
-            tab_sc = early.tile([P, T], U8, name="tab_sc", align_bytes=64)
-            loaded = SCALE_ROWS * PASSES
-            nc.sync.dma_start(idx[:], offs)
-            nc.sync.dma_start(tab_sc[0:loaded, :].bitcast(I32), tab_scales.rearrange("a q t -> (a q) t").bitcast(I32))
-            nc.sync.dma_start(idx2[:], offs2)
-            for a in range(PASSES):
-                nc.sync.dma_start(tab[a][:], tab_words[a].rearrange("p t i -> p (t i)").bitcast(I32))
-            nc.vector.memset(tab_sc[loaded : P // 2, :].bitcast(I32), 0)
-            nc.gpsimd.memset(tab_sc[P // 2 : P, :].bitcast(I32), 0)
-            for a in range(PASSES):
-                nc.gpsimd.memset(v_sc[a][:].bitcast(I32), 0)
-            nc.vector.tensor_copy(picked_sc[:], tab_sc[:].indirect(idx[:]))
-        for a in range(PASSES):
-            for q in range(P // QUADRANT):
-                row = SCALE_ROWS * a + 4 * q
-                (nc.gpsimd, nc.scalar)[a].dma_start(
-                    v_sc[a][QUADRANT * q : QUADRANT * q + 4, :].bitcast(I32),
-                    picked_sc[row : row + 4, :].bitcast(I32),
-                )
         make_identity(nc, ident[:])
+        wp_sc = tile([P, N], U8, "wp_sc")
+        nc.gpsimd.memset(wp_sc[:].bitcast(I32), 0)
+        wp_w = tile([P, 2 * N], U8, "wp_w")
+        nc.sync.dma_start(wp_w[:].bitcast(I32), wp_words[0].bitcast(I32))
+        for q in range(P // QUADRANT):
+            nc.sync.dma_start(
+                wp_sc[QUADRANT * q : QUADRANT * q + PLANE_ROWS, :].bitcast(I32),
+                wp_scales[0, PLANE_ROWS * q : PLANE_ROWS * (q + 1), :].bitcast(I32),
+            )
 
-        late = ctx.enter_context(tc.tile_pool(name="late", bufs=1))
+        pages = [keep.tile([P, T2], F32, name="page%d" % t) for t in range(SLICES)]
+        for t in range(SLICES):
+            (nc.vector if t < 2 else nc.gpsimd).memset(pages[t][:], 0.0)
 
-        def tagged(shape, dtype, tag):
-            return late.tile(shape, dtype, name=tag, tag=tag, align_bytes=64)
+        v_w = [tile([P, S], U32, "v_w%d" % a) for a in range(PASSES)]
+        v_sc = tile([P, S], U8, "v_sc")
 
-        second_page = late.tile([P, T2], F32, name="page1")
-        nc.vector.memset(second_page[:], 0.0)
-        load_w(late, 0, ((0, 0), (1, 0), (0, 1), (1, 1)))
-        first_words = []
-        for a in range(PASSES):
-            first_words.append(gather_words(a, tab[a], 0, BANK, "v%d_0" % a))
-            if a == 0:
-                gather_words(a, tab[a], BANK, BANK, "v0_1")
-                pages = [keep.tile([P, T2], F32, name="page0", tag="tab0", align_bytes=64), second_page]
-                nc.vector.memset(pages[0][:], 0.0)
+        def gather(dst, table, j0, width):
+            entries = idx[:, j0 // LIST_GROUP : (j0 + width) // LIST_GROUP]
+            nc.vector.tensor_copy(dst[:, j0 : j0 + width], table.indirect(entries))
 
-        old_sb = {}
+        def plane(a, j0, width):
+            return v_sc[PLANE_ROWS * a : P, j0 : j0 + width]
 
-        def load_old(t):
-            old_sb[t] = tagged([P, T2], F32, "old%d" % t)
-            nc.sync.dma_start(old_sb[t][:], old[t * P : (t + 1) * P, :])
+        codes = [tile([P, PASSES * 2 * P], U32, "w_codes%d" % t) for t in range(SLICES)]
+        scales = [tile([P, PASSES * 2 * P], U8, "w_scales%d" % t) for t in range(SLICES)]
 
-        wgs_sb = late.tile([P, S], F32, name="wgs_sb")
-        nc.sync.dma_start(wgs_sb[:], wgs)
-        load_w(late, 1)
-        load_w(late, 2)
-        load_old(0)
-        load_w(late, 3)
-        load_old(1)
-        load_old(3)
-        load_old(2)
-        w_q = {}
-
-        def round_into(dst, t, a, m, copy):
+        def round_w(dst, t, a, m, copy):
             copy(
                 dst.rearrange("p (g c) i -> p g i c", c=NEIGHBOURS),
                 w_raw[t, a, m][:].rearrange("p i (g c) -> p g i c", c=NEIGHBOURS),
             )
 
-        def code_tiles(t):
-            codes = keep.tile([P, PASSES * 2 * P], U32, name="w_codes%d" % t, align_bytes=64)
-            scales = keep.tile([P, PASSES * 2 * P], U8, name="w_scales%d" % t, align_bytes=64)
-            w_q[t] = (codes, scales)
-            return codes, scales
-
-        w_bf = {}
-
-        def round_w(t, pieces, tag=None):
-            if t not in w_bf:
-                w_bf[t] = tagged([P, PASSES, 2, P, PACK], BF16, tag)
-            for a, m in pieces:
-                round_into(w_bf[t][:, a, m], t, a, m, nc.scalar.copy)
-
-        def quantise_w(t):
-            codes, scales = code_tiles(t)
+        def quantise_w(t, c0, src):
+            width = src.shape[1] // PACK
             nc.vector.quantize_mx(
-                out=codes[:].bitcast(FP8X4), scales=scales[:], in_=w_bf[t][:].rearrange("p a m c i -> p (a m c i)")
-            )
-
-
-        def prepare_w(t, a, ms, pool, tag):
-            wb = pool.tile([P, len(ms), P, PACK], BF16, name=tag, tag=tag, align_bytes=64)
-            for k, m in enumerate(ms):
-                round_into(wb[:, k], t, a, m, nc.scalar.copy)
-            codes, scales = w_q[t] if t in w_q else code_tiles(t)
-            cols = slice((2 * a + ms[0]) * P, (2 * a + ms[-1] + 1) * P)
-            nc.vector.quantize_mx(
-                out=codes[:, cols].bitcast(FP8X4), scales=scales[:, cols], in_=wb[:].rearrange("p m c i -> p (m c i)")
+                out=codes[t][:, c0 : c0 + width].bitcast(FP8X4), scales=scales[t][:, c0 : c0 + width], in_=src
             )
 
         def scatter(t, j0, speed):
             width = speed.shape[1]
+            h, c0 = divmod(j0, BANK)
             nc.vector.tensor_tensor(
                 pages[t][:].indirect(idx2[:, j0 // LIST_GROUP : (j0 + width) // LIST_GROUP]),
                 speed,
@@ -196,62 +152,28 @@ def tile_list_particle_cell_pressure_kernel(
                 MULT,
             )
 
-        def first_products():
-            codes, scales = code_tiles(0)
-            acc = [[bank(7)], [bank(0), bank(1)]]
-            for m in range(2):
-                for a in range(PASSES):
-                    wb = keep.tile([P, P, PACK], BF16, name="w_bf_first%d_%d" % (a, m), tag="w_bf_first%d_%d" % (a, m), align_bytes=64)
-                    round_into(wb[:], 0, a, m, nc.scalar.copy)
-                    cols = slice((2 * a + m) * P, (2 * a + m + 1) * P)
-                    nc.vector.quantize_mx(
-                        out=codes[:, cols].bitcast(FP8X4),
-                        scales=scales[:, cols],
-                        in_=wb[:].rearrange("p c i -> p (c i)"),
-                    )
-                    width = BANK // len(acc[m])
-                    for k, dst in enumerate(acc[m]):
-                        nc.tensor.matmul_mx(
-                            out=dst[:, 0:width],
-                            lhsT=codes[:, cols].bitcast(FP8X4),
-                            lhsT_scale=scales[:, cols],
-                            rhs=first_words[a][:, k * width : (k + 1) * width].bitcast(FP8X4),
-                            rhs_scale=v_sc[a][:, k * width : (k + 1) * width],
-                            start=(a == 0),
-                            stop=(a == PASSES - 1),
-                        )
-            return acc
-
-        def products(n, k, b):
-            t, h = divmod(n, HALVES)
-            codes, scales = w_q[t]
-            acc = bank(b)
-            for a in range(PASSES):
+        def products(t, k, acc, passes=range(PASSES)):
+            for a in passes:
                 cols = slice(a * 2 * P, (a + 1) * 2 * P)
                 for e in range(2):
-                    c0 = k * PIECE + e * P
-                    j0 = h * BANK + c0
+                    j0 = k * PIECE + e * P
                     nc.tensor.matmul_mx(
                         out=acc[:, e * 2 * P : (e + 1) * 2 * P],
-                        lhsT=v_w[a, 2 * h + k][:, e * P : (e + 1) * P].bitcast(FP8X4),
-                        lhsT_scale=v_sc[a][:, j0 : j0 + P],
-                        rhs=codes[:, cols].bitcast(FP8X4),
-                        rhs_scale=scales[:, cols],
+                        lhsT=v_w[a][:, j0 : j0 + P].bitcast(FP8X4),
+                        lhsT_scale=plane(a, j0, P),
+                        rhs=codes[t][:, cols].bitcast(FP8X4),
+                        rhs_scale=scales[t][:, cols],
                         start=(a == 0 and e == 0),
                         stop=(a == PASSES - 1 and e == 1),
                     )
             return acc
 
-        def square(acc, tag=None):
-            if tag:
-                sq = tagged([P, BANK], F32, tag)
-            else:
-                sq = ring.tile([P, BANK], F32, name="sq", tag="sq", bufs=SQUARE_BUFFERS)
-            nc.scalar.activation(sq[:], acc[:], ACT.Square)
+        def square(acc, tag):
+            sq = tile([P, acc.shape[1]], F32, tag)
+            nc.scalar.activation(sq[:], acc, ACT.Square)
             return sq
 
-        def summed(sq, total, k):
-            total = total[:, k * PIECE : (k + 1) * PIECE]
+        def summed(sq, total):
             for e in range(2):
                 for m in range(2):
                     c0 = (2 * e + m) * P
@@ -263,15 +185,14 @@ def tile_list_particle_cell_pressure_kernel(
                         stop=(m == 1),
                         is_transpose=True,
                     )
-            return total
 
         def root(dst, total):
             nc.scalar.activation(dst, total, ACT.Sqrt)
 
         z_t = [keep.tile([P, nb, 2, P, 2], BF16, name="z_t%d" % q) for q, (b0, nb) in enumerate(CHUNKS)]
 
-        def turn_into(acc, src, group, first):
-            blocks = [b for q in group for b in range(CHUNKS[q][0], CHUNKS[q][0] + CHUNKS[q][1])]
+        def turn_into(acc, src, g, first):
+            blocks = [b for q in GROUPS[g] for b in range(CHUNKS[q][0], CHUNKS[q][0] + CHUNKS[q][1])]
             for k, b in enumerate(blocks):
                 nc.tensor.matmul(
                     acc[:, k * P : (k + 1) * P],
@@ -282,15 +203,15 @@ def tile_list_particle_cell_pressure_kernel(
                     is_transpose=True,
                 )
 
-        def open_loss(t, group, b):
+        def open_loss(t, g, b):
             acc = bank(b)
-            turn_into(acc, old_sb[t], group, True)
+            turn_into(acc, old_sb[t], g, True)
             return acc
 
-        def round_loss(acc, t, group, copy):
+        def round_loss(acc, t, g, copy):
             words = P // PACK
             c0 = 0
-            for q in group:
+            for q in GROUPS[g]:
                 nb = CHUNKS[q][1]
                 copy(
                     z_t[q][:, :, :, words * t : words * (t + 1), :],
@@ -298,128 +219,168 @@ def tile_list_particle_cell_pressure_kernel(
                 )
                 c0 = c0 + nb * P
 
-        def close_loss(acc, t, group, copy):
-            turn_into(acc, pages[t], group, False)
-            round_loss(acc, t, group, copy)
-
         def loss(t, g, b):
-            close_loss(open_loss(t, GROUPS[g], b), t, GROUPS[g], nc.scalar.copy)
+            acc = open_loss(t, g, b)
+            turn_into(acc, pages[t], g, False)
+            round_loss(acc, t, g, nc.scalar.copy)
 
-        QAT = {2: 1, 3: 1}
-        SPLIT = (1, 2, 4, 7)
-        LOSSES = {3: ((0, 0),), 4: ((0, 1),), 5: ((0, 2), (0, 3)), 6: ((1, 0), (1, 1), (1, 2), (1, 3))}
-        ACC = (0, 1)
-        SPLIT_SUMS = {1: (0, 2), 2: (1, 6), 3: (2, 7), 4: (4, 5), 5: (6, 7), 7: (0, 1)}
-        acc = first_products()
-        gather_words(1, tab[1], BANK, BANK, "w_bf_first1_1")
-        sq_a = tagged([P, BANK], F32, "sq_a")
-        nc.scalar.activation(sq_a[:], acc[0][0][:], ACT.Square)
+        for a in range(PASSES):
+            wb = tile([P, 2, P, PACK], BF16, "w_first%d" % a)
+            for m in range(2):
+                round_w(wb[:, m], 0, a, m, nc.scalar.copy)
+            quantise_w(0, 2 * a * P, wb[:].rearrange("p m c i -> p (m c i)"))
+        for h in range(2):
+            gather(v_w[0], tab[0][:].bitcast(U32), h * BANK, BANK)
+            gather(v_sc, tab_sc[:], h * BANK, BANK)
+        for k in range(S // PIECE):
+            gather(v_w[1], tab[1][:].bitcast(U32), k * PIECE, PIECE)
+
+        def first_products(k, acc):
+            for a in range(PASSES):
+                for m in range(2):
+                    cols = slice((2 * a + m) * P, (2 * a + m + 1) * P)
+                    nc.tensor.matmul_mx(
+                        out=acc[:, m * PIECE : (m + 1) * PIECE],
+                        lhsT=codes[0][:, cols].bitcast(FP8X4),
+                        lhsT_scale=scales[0][:, cols],
+                        rhs=v_w[a][:, k * PIECE : (k + 1) * PIECE].bitcast(FP8X4),
+                        rhs_scale=plane(a, k * PIECE, PIECE),
+                        start=(a == 0 and m == 0),
+                        stop=(a == PASSES - 1 and m == 1),
+                    )
+            return acc
+
+        neg_wgs = tile([P, S], F32, "neg_wgs")
+        nc.scalar.activation(neg_wgs[:, 0:BANK], wgs_raw[0][:], ACT.Copy, scale=-1.0)
+        sq = [square(first_products(k, bank(k))[:], "sq%d" % k) for k in range(2)]
         totals = []
         for k in range(2):
-            sq_b = tagged([P, PIECE], F32, "sq_b%d" % k)
-            nc.scalar.activation(sq_b[:], acc[1][k][:, 0:PIECE], ACT.Square)
-            total = tagged([P, PIECE], F32, "total%d" % k)
-            nc.vector.tensor_tensor(total[:], sq_a[:, k * PIECE : (k + 1) * PIECE], sq_b[:], ADD)
-            totals.append(total)
-            if k == 0:
-                neg_wgs = tagged([P, S], F32, "sq_b0")
-                nc.vector.tensor_scalar(neg_wgs[:], wgs_sb[:], -1.0, None, MULT)
-        accs = [products(1, k, ACC[k]) for k in range(2)]
-        speed = tagged([P, PIECE], F32, "speed0_0")
-        root(speed[:], totals[0][:])
-        scatter(0, 0, speed[:])
-        speed = tagged([P, PIECE], F32, "speed0_1")
-        root(speed[:], totals[1][:])
-        scatter(0, PIECE, speed[:])
-        wp_sc = tagged([P, N], U8, "speed0_1")
-        nc.gpsimd.memset(wp_sc[:].bitcast(I32), 0)
-        wp_w = late.tile([P, 2 * N], U8, name="wp_w", align_bytes=64)
-        nc.sync.dma_start(wp_w[:].bitcast(I32), wp_words[0].bitcast(I32))
-        for q in range(P // QUADRANT):
-            nc.sync.dma_start(
-                wp_sc[QUADRANT * q : QUADRANT * q + 4, :].bitcast(I32),
-                wp_scales[0, 4 * q : 4 * q + 4, :].bitcast(I32),
-            )
+            totals.append(tile([P, PIECE], F32, "total%d" % k))
+            nc.vector.tensor_tensor(totals[k][:], sq[k][:, 0:PIECE], sq[k][:, PIECE:BANK], ADD)
+        acc = [products(0, 2, bank(2)), products(0, 3, bank(3))]
+        first = [tile([P, PIECE], F32, "first%d" % k) for k in range(2)]
+        root(first[0][:], totals[0][:])
 
-        ALL = ((0, 0), (0, 1), (1, 0), (1, 1))
-        for n in range(1, 2 * SLICES):
-            t, h = divmod(n, HALVES)
-            near, far = {2: (1, 0), 5: (3, 2), 7: (6, 7)}.get(n, ACC)
-            if n > 1:
-                accs = [products(n, 0, near), products(n, 1, far)]
-            if n == 2:
-                round_w(2, ALL[:3], "total0")
-            held = {1: "total0", 2: "sq_held"}.get(n)
-            sqs = [square(accs[0]), square(accs[1], held)]
-            if n in SPLIT_SUMS:
-                totals = [summed(sqs[k], bank(SPLIT_SUMS[n][k]), 0) for k in range(2)]
-            else:
-                both = bank(3)
-                for k in range(2):
-                    summed(sqs[k], both, k)
-                totals = [both[:]]
-            tag = "speed%d" % n
-            if n in (1, 2, 3):
-                round_w(n, ALL[3:] if n == 2 else ALL, "total1" if n == 1 else "sq_held")
-                quantise_w(n)
-                if n < 3:
-                    pages.append(tagged([P, T2], F32, ("total1", "total0")[n - 1]))
-                    nc.gpsimd.memset(pages[n + 1][:], 0.0)
-                tag = raw_tag(n, 1, 0)
-            whole = t >= WHOLE_FROM
-            if not whole or h == 0:
-                speed = tagged([P, S if whole else BANK], F32, tag)
-            c0 = h * BANK if whole else 0
-            for total in totals:
-                root(speed[:, c0 : c0 + total.shape[1]], total)
-                c0 = c0 + total.shape[1]
-            if not whole or h == 1:
-                scatter(t, 0 if whole else h * BANK, speed[:])
-            for tl, g in LOSSES.get(n, ()):
-                loss(tl, g, (6, 7, 4, 5)[g])
-        opened = [open_loss(LAST, group, b) for group, b in zip(GROUPS, (2, 3, 4, 5))]
-        waiting = [open_loss(LAST - 1, group, b) for group, b in zip(GROUPS, (6, 7, 0, 1))]
-        for g in range(4):
-            close_loss(waiting[g], LAST - 1, GROUPS[g], nc.scalar.copy)
+        w_bf = {}
+
+        def round_pieces(t, pieces, copy=nc.scalar.copy, tag=None):
+            if tag:
+                w_bf[t] = tile([P, PASSES, 2, P, PACK], BF16, tag)
+            for a, m in pieces:
+                round_w(w_bf[t][:, a, m], t, a, m, copy)
+
+        def quantise_slice(t):
+            quantise_w(t, 0, w_bf[t][:].rearrange("p a m c i -> p (a m c i)"))
+
+        def squares(acc, tags):
+            return [square(acc[k][:], tags[k]) for k in range(2)]
+
+        def sums(sq, b):
+            total = bank(b)
+            for k in range(2):
+                summed(sq[k], total[:, k * PIECE : (k + 1) * PIECE])
+            return total
+
+        def rooted(total, tag):
+            speed = tile([P, BANK], F32, tag)
+            root(speed[:], total[:])
+            return speed
+
+        def both(t, h, banks):
+            return [products(t, 2 * h + k, bank(banks[k])) for k in range(2)]
+
+        def closed(t, g, b):
+            acc = open_loss(t, g, b)
+            turn_into(acc, pages[t], g, False)
+            return acc
+
+        lone = tile([P, P, PACK], BF16, "sq1")
+        round_w(lone[:], 1, 0, 0, nc.vector.tensor_copy)
+        scatter(0, 0, first[0][:])
+        rest = tile([P, 3, P, PACK], BF16, "w_rest")
+        for k, (a, m) in enumerate(BY_PASS[1:]):
+            round_w(rest[:, k], 1, a, m, nc.scalar.copy)
+        quantise_w(1, 0, lone[:].rearrange("p c i -> p (c i)"))
+        quantise_w(1, P, rest[:].rearrange("p k c i -> p (k c i)"))
+        root(first[1][:], totals[1][:])
+        scatter(0, PIECE, first[1][:])
+        total = sums(squares(acc, ("total0", "sq0")), 4)
+        nc.scalar.activation(neg_wgs[:, BANK:S], wgs_raw[1][:], ACT.Copy, scale=-1.0)
+        acc = both(1, 0, (3, 4))
+        scatter(0, BANK, rooted(total, "speed1")[:])
+
+        total = sums(squares(acc, ("sq2", "sq3")), 5)
+        acc = both(1, 1, (3, 4))
+        round_pieces(2, BY_PASS, tag="w_first0")
+        quantise_slice(2)
+        scatter(1, 0, rooted(total, "speed2")[:])
+
+        total = sums(squares(acc, ("sq2", "sq3")), 2)
+        held = [closed(0, 0, 5), closed(0, 1, 3)]
+        acc = both(2, 0, (0, 1)) + both(2, 1, (6, 7))
+        round_pieces(3, BY_PASS, tag="w_first1")
+        quantise_slice(3)
+        scatter(1, BANK, rooted(total, "speed3")[:])
+
+        sq = squares(acc[:2], ("sq3", "sq4")) + squares(acc[2:], ("sq5", "sq6"))
+        totals = [sums(sq[:2], 4), sums(sq[2:], 0)]
+        speed = tile([P, S], F32, "speed45")
+        for h in range(2):
+            root(speed[:, h * BANK : (h + 1) * BANK], totals[h][:])
+        scatter(2, 0, speed[:])
+        for g in range(2):
+            round_loss(held[g], 0, g, nc.scalar.copy)
+        loss(0, 2, 2)
+        loss(0, 3, 1)
+        total = sums(squares(both(3, 0, (6, 7)), ("sq3", "sq4")), 4)
+        scatter(3, 0, rooted(total, "speed6")[:])
+        loss(1, 0, 0)
+        loss(1, 1, 6)
+        acc = both(3, 1, (0, 6))
+        loss(1, 2, 7)
+        loss(1, 3, 4)
+        total = sums(squares(acc, ("sq3", "sq4")), 7)
+        scatter(3, BANK, rooted(total, "speed7")[:])
+        opened = [open_loss(3, g, b) for g, b in enumerate((5, 3, 2, 1))]
+        for g, b in enumerate((4, 0, 6, 7)):
+            loss(2, g, b)
 
         z_q = {}
-        used = []
-        spare_one = [raw_tag(t, a, m) for t in (2, 3) for a in range(PASSES) for m in range(2)]
-        spare_two = ["res_last", "speed4", "sq_held", "old1", "old0"]
+        word_banks = [4, 0, 6, 7] * 2
+        out_banks = [5, 3, 2, 1] * 3 + [4, 0, 6, 7]
+        spare = ["old0", "old1", "tab0", "tab1", "w_raw3_1_1", "w_raw3_1_0", "w_raw3_0_1", "w_raw3_0_0", "w_raw2_1_1", "w_raw2_1_0", "old2"]
 
-        def quantise_z(q):
+        def quantise_z(q, copy):
             b0, nb = CHUNKS[q]
             words = z_t[q][:].rearrange("c cb u p e -> c (cb u p e)").bitcast(F32)
-            z_bf = tagged([P, nb * P, PACK], BF16, Z_TAGS[q])
+            z_bf = tile([P, nb * P, PACK], BF16, ("w_raw1_0_0", "w_raw1_0_1", "w_first0", "w_first1", "neg_wgs")[q])
             z_words = z_bf[:].rearrange("p c i -> p (c i)").bitcast(F32)
-            for d in range(max(1, nb // 2)):
-                per = min(nb, 2)
-                turned = bank(WORD_BANKS[len(used)])
-                used.append(d)
-                for k in range(2 * per):
+            for d in range(nb // 2):
+                turned = bank(word_banks.pop(0))
+                for k in range(4):
                     w0 = d * BANK + k * P
                     nc.tensor.transpose(turned[:, k * P : (k + 1) * P], words[:, w0 : w0 + P], ident[:])
-                (nc.scalar.copy if q in WORDS_ON_SCALAR else nc.vector.tensor_copy)(
-                    z_words[:, d * BANK : d * BANK + 2 * per * P].rearrange("p (cb c u) -> p cb c u", cb=per, u=2),
-                    turned[:, 0 : 2 * per * P].rearrange("p (cb u c) -> p cb c u", cb=per, u=2),
+                copy(
+                    z_words[:, d * BANK : (d + 1) * BANK].rearrange("p (cb c u) -> p cb c u", cb=2, u=2),
+                    turned[:].rearrange("p (cb u c) -> p cb c u", cb=2, u=2),
                 )
-            z_codes = tagged([P, nb * P], U32, "z_codes%d" % q)
-            z_scales = tagged([P, nb * P], U8, "z_scales%d" % q)
+            z_codes = tile([P, nb * P], U32, "z_codes%d" % q)
+            z_scales = tile([P, nb * P], U8, "z_scales%d" % q)
             nc.vector.quantize_mx(
                 out=z_codes[:].bitcast(FP8X4), scales=z_scales[:], in_=z_bf[:].rearrange("p c i -> p (c i)")
             )
             z_q[q] = (z_codes, z_scales)
 
-        def pressure(q, count):
+        def pressure(q, stores, on_vector=()):
             b0, nb = CHUNKS[q]
             width = nb * P
             per_bank = BANK // width
             z_codes, z_scales = z_q[q]
             n0 = 0
-            for banks in STORES[q]:
-                res = tagged([P, banks * per_bank, width], F32, (spare_two if banks > 1 else spare_one).pop())
+            for banks in stores:
+                res = tile([P, banks * per_bank, width], F32, spare.pop())
                 for s in range(banks):
-                    acc = bank(OUT_BANKS[count])
+                    acc = bank(out_banks.pop(0))
                     for k in range(per_bank):
                         n = n0 + s * per_bank + k
                         nc.tensor.matmul_mx(
@@ -431,21 +392,25 @@ def tile_list_particle_cell_pressure_kernel(
                             start=True,
                             stop=True,
                         )
-                    copy = nc.vector.tensor_copy if count in ON_VECTOR else nc.scalar.copy
+                    copy = nc.vector.tensor_copy if n0 + s in on_vector else nc.scalar.copy
                     copy(res[:, s * per_bank : (s + 1) * per_bank, :].rearrange("p k c -> p (k c)"), acc[:])
-                    count = count + 1
                 rows = out[n0 * P : (n0 + banks * per_bank) * P, b0 * P : b0 * P + width]
                 nc.sync.dma_start(rows.rearrange("(k p) c -> p k c", p=P), res[:])
                 n0 = n0 + banks * per_bank
-            return count
 
         for g in range(len(GROUPS)):
-            turn_into(opened[g], pages[LAST], GROUPS[g], False)
-        filled = 0
-        for kind, k in TAIL:
-            if kind == "r":
-                round_loss(opened[k], LAST, GROUPS[k], nc.vector.tensor_copy if k in ROUND_ON_VECTOR else nc.scalar.copy)
-            elif kind == "q":
-                quantise_z(k)
-            else:
-                filled = pressure(k, filled)
+            turn_into(opened[g], pages[3], g, False)
+        round_loss(opened[0], 3, 0, nc.vector.tensor_copy)
+        round_loss(opened[1], 3, 1, nc.scalar.copy)
+        round_loss(opened[2], 3, 2, nc.scalar.copy)
+        round_loss(opened[3], 3, 3, nc.scalar.copy)
+        quantise_z(0, nc.vector.tensor_copy)
+        quantise_z(1, nc.vector.tensor_copy)
+        pressure(0, (1, 1))
+        quantise_z(2, nc.vector.tensor_copy)
+        pressure(1, (1, 1))
+        quantise_z(3, nc.vector.tensor_copy)
+        pressure(2, (1, 1, 2))
+        quantise_z(4, nc.vector.tensor_copy)
+        pressure(3, (2, 2), (1, 3))
+        pressure(4, (2, 2), (1, 3))

@@ -43,12 +43,12 @@ def tile_list_particle_cell_pressure_kernel(
             return psum.tile([P, BANK], F32, name="bank%d" % b, tag="bank%d" % b)
 
         def tile(shape, dtype, tag):
-            return keep.tile(shape, dtype, name=tag, tag=tag, align_bytes=64)
+            return pools[-1].tile(shape, dtype, name=tag, tag=tag, align_bytes=64)
+
+        pools = [keep]
 
         idx = keep.tile([P, S // LIST_GROUP], U16, name="idx")
         idx2 = keep.tile([P, S // LIST_GROUP], U16, name="idx2")
-        tab_sc = tile([P, T], U8, "tab_sc")
-        nc.vector.memset(tab_sc[:].bitcast(I32), 0)
         tab = [tile([P, T], I32, "tab%d" % a) for a in range(PASSES)]
         w_raw = {}
         old_sb = {}
@@ -75,17 +75,33 @@ def tile_list_particle_cell_pressure_kernel(
             return raw
 
         BY_PASS = ((0, 0), (0, 1), (1, 0), (1, 1))
-        nc.sync.dma_start(idx[:], offs)
-        load_w(0, BY_PASS)
-        nc.sync.dma_start(idx2[:], offs2)
-        load_table(0, 0, T // 2)
-        load_table(0, T // 2, T)
-        for q in (0, 2, 1, 3):
+        picked_sc = tile([P, S], U8, "picked_sc")
+        v_sc = tile([P, S], U8, "v_sc")
+        both_planes = PASSES * PLANE_ROWS
+        with tc.tile_pool(name="early", bufs=1) as early:
+            tab_sc = early.tile([P, T], U8, name="tab_sc", align_bytes=64)
+            nc.sync.dma_start(idx[:], offs)
+            for r in range(PLANE_ROWS):
+                nc.sync.dma_start(
+                    tab_sc[r:QUADRANT:PLANE_ROWS, :].bitcast(I32),
+                    tab_scales.rearrange("a (q r) t -> r q a t", r=PLANE_ROWS)[r].bitcast(I32),
+                )
+            for a in range(PASSES):
+                load_table(a, 0, T)
+            nc.vector.memset(tab_sc[QUADRANT : P // 2, :].bitcast(I32), 0)
+            nc.vector.memset(tab_sc[P // 2 : P, :].bitcast(I32), 0)
+            nc.gpsimd.memset(v_sc[:].bitcast(I32), 0)
+            nc.vector.tensor_copy(picked_sc[:], tab_sc[:].indirect(idx[:]))
+        for q in range(P // QUADRANT):
             nc.sync.dma_start(
-                tab_sc[QUADRANT * q : QUADRANT * q + PASSES * PLANE_ROWS, :].bitcast(I32),
-                tab_scales[:, PLANE_ROWS * q : PLANE_ROWS * (q + 1), :].bitcast(I32),
+                v_sc[QUADRANT * q : QUADRANT * q + both_planes, :].bitcast(I32),
+                picked_sc[both_planes * q : both_planes * (q + 1), :].bitcast(I32),
             )
-        load_table(1, 0, T)
+        pages = [keep.tile([P, T2], F32, name="page%d" % t) for t in range(2)]
+        ident = keep.tile([P, P], F32, name="ident")
+        pools.append(ctx.enter_context(tc.tile_pool(name="late", bufs=1)))
+        load_w(0, ((0, 0), (1, 0), (0, 1), (1, 1)))
+        nc.sync.dma_start(idx2[:], offs2)
         wgs_raw = [load_wgs(0)]
         load_w(1, BY_PASS)
         wgs_raw.append(load_wgs(1))
@@ -101,7 +117,6 @@ def tile_list_particle_cell_pressure_kernel(
         nc.gpsimd.memset(one[:], 1.0)
         preload = keep.tile([P, 8], F32, name="preload")
         nc.scalar.activation(preload[:], one[:], ACT.Sqrt)
-        ident = keep.tile([P, P], F32, name="ident")
         make_identity(nc, ident[:])
         wp_sc = tile([P, N], U8, "wp_sc")
         nc.gpsimd.memset(wp_sc[:].bitcast(I32), 0)
@@ -113,12 +128,8 @@ def tile_list_particle_cell_pressure_kernel(
                 wp_scales[0, PLANE_ROWS * q : PLANE_ROWS * (q + 1), :].bitcast(I32),
             )
 
-        pages = [keep.tile([P, T2], F32, name="page%d" % t) for t in range(SLICES)]
-        for t in range(SLICES):
-            (nc.vector if t < 2 else nc.gpsimd).memset(pages[t][:], 0.0)
 
         v_w = [tile([P, S], U32, "v_w%d" % a) for a in range(PASSES)]
-        v_sc = tile([P, S], U8, "v_sc")
 
         def gather(dst, table, j0, width):
             entries = idx[:, j0 // LIST_GROUP : (j0 + width) // LIST_GROUP]
@@ -225,38 +236,36 @@ def tile_list_particle_cell_pressure_kernel(
             round_loss(acc, t, g, nc.scalar.copy)
 
         for a in range(PASSES):
-            wb = tile([P, 2, P, PACK], BF16, "w_first%d" % a)
-            for m in range(2):
-                round_w(wb[:, m], 0, a, m, nc.scalar.copy)
-            quantise_w(0, 2 * a * P, wb[:].rearrange("p m c i -> p (m c i)"))
-        for h in range(2):
-            gather(v_w[0], tab[0][:].bitcast(U32), h * BANK, BANK)
-            gather(v_sc, tab_sc[:], h * BANK, BANK)
-        for k in range(S // PIECE):
-            gather(v_w[1], tab[1][:].bitcast(U32), k * PIECE, PIECE)
-
-        def first_products(k, acc):
+            for h in range(2):
+                gather(v_w[a], tab[a][:].bitcast(U32), h * BANK, BANK)
+        for page in pages:
+            nc.vector.memset(page[:], 0.0)
+        acc_a, acc_b = bank(6), [bank(0), bank(1)]
+        for m in range(2):
             for a in range(PASSES):
-                for m in range(2):
-                    cols = slice((2 * a + m) * P, (2 * a + m + 1) * P)
+                wb = tile([P, P, PACK], BF16, "w_first%d" % (2 * m + a))
+                round_w(wb[:], 0, a, m, nc.vector.tensor_copy if (a, m) == (1, 1) else nc.scalar.copy)
+                cols = slice((2 * a + m) * P, (2 * a + m + 1) * P)
+                quantise_w(0, cols.start, wb[:].rearrange("p c i -> p (c i)"))
+                for j0, width, dst in ((0, BANK, acc_a),) if m == 0 else ((0, PIECE, acc_b[0]), (PIECE, PIECE, acc_b[1])):
                     nc.tensor.matmul_mx(
-                        out=acc[:, m * PIECE : (m + 1) * PIECE],
+                        out=dst[:, 0:width],
                         lhsT=codes[0][:, cols].bitcast(FP8X4),
                         lhsT_scale=scales[0][:, cols],
-                        rhs=v_w[a][:, k * PIECE : (k + 1) * PIECE].bitcast(FP8X4),
-                        rhs_scale=plane(a, k * PIECE, PIECE),
-                        start=(a == 0 and m == 0),
-                        stop=(a == PASSES - 1 and m == 1),
+                        rhs=v_w[a][:, j0 : j0 + width].bitcast(FP8X4),
+                        rhs_scale=plane(a, j0, width),
+                        start=(a == 0),
+                        stop=(a == PASSES - 1),
                     )
-            return acc
-
         neg_wgs = tile([P, S], F32, "neg_wgs")
+        sq_a = square(acc_a[:], "sq0")
         nc.scalar.activation(neg_wgs[:, 0:BANK], wgs_raw[0][:], ACT.Copy, scale=-1.0)
-        sq = [square(first_products(k, bank(k))[:], "sq%d" % k) for k in range(2)]
+        sq_b = [square(acc_b[k][:, 0:PIECE], ("sq_b", "sq1")[k]) for k in range(2)]
+
         totals = []
         for k in range(2):
             totals.append(tile([P, PIECE], F32, "total%d" % k))
-            nc.vector.tensor_tensor(totals[k][:], sq[k][:, 0:PIECE], sq[k][:, PIECE:BANK], ADD)
+            nc.vector.tensor_tensor(totals[k][:], sq_a[:, k * PIECE : (k + 1) * PIECE], sq_b[k][:], ADD)
         acc = [products(0, 2, bank(2)), products(0, 3, bank(3))]
         first = [tile([P, PIECE], F32, "first%d" % k) for k in range(2)]
         root(first[0][:], totals[0][:])
@@ -297,14 +306,16 @@ def tile_list_particle_cell_pressure_kernel(
         lone = tile([P, P, PACK], BF16, "sq1")
         round_w(lone[:], 1, 0, 0, nc.vector.tensor_copy)
         scatter(0, 0, first[0][:])
-        rest = tile([P, 3, P, PACK], BF16, "w_rest")
+        rest = tile([P, 3, P, PACK], BF16, "sq_b")
         for k, (a, m) in enumerate(BY_PASS[1:]):
             round_w(rest[:, k], 1, a, m, nc.scalar.copy)
         quantise_w(1, 0, lone[:].rearrange("p c i -> p (c i)"))
         quantise_w(1, P, rest[:].rearrange("p k c i -> p (k c i)"))
+        pages.append(tile([P, T2], F32, "sq_b"))
+        nc.gpsimd.memset(pages[2][:], 0.0)
         root(first[1][:], totals[1][:])
         scatter(0, PIECE, first[1][:])
-        total = sums(squares(acc, ("total0", "sq0")), 4)
+        total = sums(squares(acc, ("sq2", "total0")), 4)
         nc.scalar.activation(neg_wgs[:, BANK:S], wgs_raw[1][:], ACT.Copy, scale=-1.0)
         acc = both(1, 0, (3, 4))
         scatter(0, BANK, rooted(total, "speed1")[:])
@@ -313,6 +324,8 @@ def tile_list_particle_cell_pressure_kernel(
         acc = both(1, 1, (3, 4))
         round_pieces(2, BY_PASS, tag="w_first0")
         quantise_slice(2)
+        pages.append(tile([P, T2], F32, "w_first0"))
+        nc.gpsimd.memset(pages[3][:], 0.0)
         scatter(1, 0, rooted(total, "speed2")[:])
 
         total = sums(squares(acc, ("sq2", "sq3")), 2)
@@ -348,12 +361,12 @@ def tile_list_particle_cell_pressure_kernel(
         z_q = {}
         word_banks = [4, 0, 6, 7] * 2
         out_banks = [5, 3, 2, 1] * 3 + [4, 0, 6, 7]
-        spare = ["old0", "old1", "tab0", "tab1", "w_raw3_1_1", "w_raw3_1_0", "w_raw3_0_1", "w_raw3_0_0", "w_raw2_1_1", "w_raw2_1_0", "old2"]
+        spare = ["old0", "old1", "res_a", "res_b", "w_raw3_1_1", "w_raw3_1_0", "w_raw3_0_1", "w_raw3_0_0", "w_raw2_1_1", "w_raw2_1_0", "old2"]
 
         def quantise_z(q, copy):
             b0, nb = CHUNKS[q]
             words = z_t[q][:].rearrange("c cb u p e -> c (cb u p e)").bitcast(F32)
-            z_bf = tile([P, nb * P, PACK], BF16, ("w_raw1_0_0", "w_raw1_0_1", "w_first0", "w_first1", "neg_wgs")[q])
+            z_bf = tile([P, nb * P, PACK], BF16, ("w_raw1_0_0", "w_raw1_0_1", "speed45", "w_first1", "neg_wgs")[q])
             z_words = z_bf[:].rearrange("p c i -> p (c i)").bitcast(F32)
             for d in range(nb // 2):
                 turned = bank(word_banks.pop(0))

@@ -81,6 +81,7 @@ def tile_list_particle_cell_pressure_kernel(
         with tc.tile_pool(name="early", bufs=1) as early:
             tab_sc = early.tile([P, T], U8, name="tab_sc", align_bytes=64)
             nc.sync.dma_start(idx[:], offs)
+            nc.sync.dma_start(idx2[:], offs2)
             for r in range(PLANE_ROWS):
                 nc.sync.dma_start(
                     tab_sc[r:QUADRANT:PLANE_ROWS, :].bitcast(I32),
@@ -101,7 +102,6 @@ def tile_list_particle_cell_pressure_kernel(
         ident = keep.tile([P, P], F32, name="ident")
         pools.append(ctx.enter_context(tc.tile_pool(name="late", bufs=1)))
         load_w(0, ((0, 0), (1, 0), (0, 1), (1, 1)))
-        nc.sync.dma_start(idx2[:], offs2)
         wgs_raw = [load_wgs(0)]
         load_w(1, BY_PASS)
         wgs_raw.append(load_wgs(1))
@@ -129,11 +129,15 @@ def tile_list_particle_cell_pressure_kernel(
             )
 
 
-        v_w = [tile([P, S], U32, "v_w%d" % a) for a in range(PASSES)]
+        v_w = {}
 
-        def gather(dst, table, j0, width):
+        def gather_words(a, j0, width, tag):
+            words = tile([P, width], U32, tag)
             entries = idx[:, j0 // LIST_GROUP : (j0 + width) // LIST_GROUP]
-            nc.vector.tensor_copy(dst[:, j0 : j0 + width], table.indirect(entries))
+            nc.vector.tensor_copy(words[:], tab[a][:].bitcast(U32).indirect(entries))
+            for j in range(j0, j0 + width, PIECE):
+                v_w[a, j // PIECE] = words[:, j - j0 : j - j0 + PIECE]
+            return words
 
         def plane(a, j0, width):
             return v_sc[PLANE_ROWS * a : P, j0 : j0 + width]
@@ -170,7 +174,7 @@ def tile_list_particle_cell_pressure_kernel(
                     j0 = k * PIECE + e * P
                     nc.tensor.matmul_mx(
                         out=acc[:, e * 2 * P : (e + 1) * 2 * P],
-                        lhsT=v_w[a][:, j0 : j0 + P].bitcast(FP8X4),
+                        lhsT=v_w[a, k][:, e * P : (e + 1) * P].bitcast(FP8X4),
                         lhsT_scale=plane(a, j0, P),
                         rhs=codes[t][:, cols].bitcast(FP8X4),
                         rhs_scale=scales[t][:, cols],
@@ -235,9 +239,8 @@ def tile_list_particle_cell_pressure_kernel(
             turn_into(acc, pages[t], g, False)
             round_loss(acc, t, g, nc.scalar.copy)
 
-        for a in range(PASSES):
-            for h in range(2):
-                gather(v_w[a], tab[a][:].bitcast(U32), h * BANK, BANK)
+        first_words = [gather_words(0, 0, S, "v0"), gather_words(1, 0, BANK, "v1_0")]
+        gather_words(1, BANK, PIECE, "v1_2")
         for page in pages:
             nc.vector.memset(page[:], 0.0)
         acc_a, acc_b = bank(6), [bank(0), bank(1)]
@@ -252,11 +255,12 @@ def tile_list_particle_cell_pressure_kernel(
                         out=dst[:, 0:width],
                         lhsT=codes[0][:, cols].bitcast(FP8X4),
                         lhsT_scale=scales[0][:, cols],
-                        rhs=v_w[a][:, j0 : j0 + width].bitcast(FP8X4),
+                        rhs=first_words[a][:, j0 : j0 + width].bitcast(FP8X4),
                         rhs_scale=plane(a, j0, width),
                         start=(a == 0),
                         stop=(a == PASSES - 1),
                     )
+        gather_words(1, BANK + PIECE, PIECE, "w_first3")
         neg_wgs = tile([P, S], F32, "neg_wgs")
         sq_a = square(acc_a[:], "sq0")
         nc.scalar.activation(neg_wgs[:, 0:BANK], wgs_raw[0][:], ACT.Copy, scale=-1.0)
@@ -329,7 +333,6 @@ def tile_list_particle_cell_pressure_kernel(
         scatter(1, 0, rooted(total, "speed2")[:])
 
         total = sums(squares(acc, ("sq2", "sq3")), 2)
-        held = [closed(0, 0, 5), closed(0, 1, 3)]
         acc = both(2, 0, (0, 1)) + both(2, 1, (6, 7))
         round_pieces(3, BY_PASS, tag="w_first1")
         quantise_slice(3)
@@ -341,8 +344,8 @@ def tile_list_particle_cell_pressure_kernel(
         for h in range(2):
             root(speed[:, h * BANK : (h + 1) * BANK], totals[h][:])
         scatter(2, 0, speed[:])
-        for g in range(2):
-            round_loss(held[g], 0, g, nc.scalar.copy)
+        loss(0, 0, 5)
+        loss(0, 1, 3)
         loss(0, 2, 2)
         loss(0, 3, 1)
         total = sums(squares(both(3, 0, (6, 7)), ("sq3", "sq4")), 4)
@@ -359,16 +362,16 @@ def tile_list_particle_cell_pressure_kernel(
             loss(2, g, b)
 
         z_q = {}
-        word_banks = [4, 0, 6, 7] * 2
-        out_banks = [5, 3, 2, 1] * 3 + [4, 0, 6, 7]
-        spare = ["old0", "old1", "res_a", "res_b", "w_raw3_1_1", "w_raw3_1_0", "w_raw3_0_1", "w_raw3_0_0", "w_raw2_1_1", "w_raw2_1_0", "old2"]
+        word_banks = [4, 0, 6, 7, 5, 3, 2, 1]
+        out_banks = [4, 0, 6, 7, 5, 3, 4, 0, 2, 1, 6, 7, 5, 3, 4, 0]
+        spare = [("w_raw%d_%d_%d" % (t, a, m)) for t in (0, 2, 3) for a, m in BY_PASS] + ["old0", "old1", "old2", "sq3"]
 
-        def quantise_z(q, copy):
+        def quantise_z(q, copies):
             b0, nb = CHUNKS[q]
             words = z_t[q][:].rearrange("c cb u p e -> c (cb u p e)").bitcast(F32)
             z_bf = tile([P, nb * P, PACK], BF16, ("w_raw1_0_0", "w_raw1_0_1", "speed45", "w_first1", "neg_wgs")[q])
             z_words = z_bf[:].rearrange("p c i -> p (c i)").bitcast(F32)
-            for d in range(nb // 2):
+            for d, copy in enumerate(copies):
                 turned = bank(word_banks.pop(0))
                 for k in range(4):
                     w0 = d * BANK + k * P
@@ -411,19 +414,21 @@ def tile_list_particle_cell_pressure_kernel(
                 nc.sync.dma_start(rows.rearrange("(k p) c -> p k c", p=P), res[:])
                 n0 = n0 + banks * per_bank
 
-        for g in range(len(GROUPS)):
+        def last_loss(g, copy):
             turn_into(opened[g], pages[3], g, False)
-        round_loss(opened[0], 3, 0, nc.vector.tensor_copy)
-        round_loss(opened[1], 3, 1, nc.scalar.copy)
-        round_loss(opened[2], 3, 2, nc.scalar.copy)
-        round_loss(opened[3], 3, 3, nc.scalar.copy)
-        quantise_z(0, nc.vector.tensor_copy)
-        quantise_z(1, nc.vector.tensor_copy)
+            round_loss(opened[g], 3, g, copy)
+
+        on_vector, on_scalar = nc.vector.tensor_copy, nc.scalar.copy
+        last_loss(0, on_vector)
+        quantise_z(0, (on_vector,))
+        quantise_z(1, (on_scalar,))
+        for g in range(1, len(GROUPS)):
+            last_loss(g, on_scalar)
+        quantise_z(2, (on_vector, on_vector))
+        quantise_z(3, (on_vector, on_vector))
         pressure(0, (1, 1))
-        quantise_z(2, nc.vector.tensor_copy)
         pressure(1, (1, 1))
-        quantise_z(3, nc.vector.tensor_copy)
-        pressure(2, (1, 1, 2))
-        quantise_z(4, nc.vector.tensor_copy)
-        pressure(3, (2, 2), (1, 3))
-        pressure(4, (2, 2), (1, 3))
+        quantise_z(4, (on_vector, on_vector))
+        pressure(2, (1, 1, 1, 1))
+        pressure(3, (1, 1, 1, 1), (1, 3))
+        pressure(4, (1, 1, 1, 1), (1, 3))

@@ -362,16 +362,16 @@ def tile_list_particle_cell_pressure_kernel(
             loss(2, g, b)
 
         z_q = {}
-        word_banks = [4, 0, 6, 7, 5, 3, 2, 1]
-        out_banks = [4, 0, 6, 7, 5, 3, 4, 0, 2, 1, 6, 7, 5, 3, 4, 0]
-        spare = [("w_raw%d_%d_%d" % (t, a, m)) for t in (0, 2, 3) for a, m in BY_PASS] + ["old0", "old1", "old2", "sq3"]
+        word_banks = [4, 0, 6, 7] * 2
+        out_banks = [5, 3, 2, 1] * 3 + [4, 0, 6, 7]
+        spare = ["old0", "old1", "res_a", "res_b", "w_raw3_1_1", "w_raw3_1_0", "w_raw3_0_1", "w_raw3_0_0", "w_raw2_1_1", "w_raw2_1_0", "old2"]
 
-        def quantise_z(q, copies):
+        def quantise_z(q, copy):
             b0, nb = CHUNKS[q]
             words = z_t[q][:].rearrange("c cb u p e -> c (cb u p e)").bitcast(F32)
             z_bf = tile([P, nb * P, PACK], BF16, ("w_raw1_0_0", "w_raw1_0_1", "speed45", "w_first1", "neg_wgs")[q])
             z_words = z_bf[:].rearrange("p c i -> p (c i)").bitcast(F32)
-            for d, copy in enumerate(copies):
+            for d in range(nb // 2):
                 turned = bank(word_banks.pop(0))
                 for k in range(4):
                     w0 = d * BANK + k * P
@@ -414,21 +414,19 @@ def tile_list_particle_cell_pressure_kernel(
                 nc.sync.dma_start(rows.rearrange("(k p) c -> p k c", p=P), res[:])
                 n0 = n0 + banks * per_bank
 
-        def last_loss(g, copy):
+        for g in range(len(GROUPS)):
             turn_into(opened[g], pages[3], g, False)
-            round_loss(opened[g], 3, g, copy)
-
-        on_vector, on_scalar = nc.vector.tensor_copy, nc.scalar.copy
-        last_loss(0, on_vector)
-        quantise_z(0, (on_vector,))
-        quantise_z(1, (on_scalar,))
-        for g in range(1, len(GROUPS)):
-            last_loss(g, on_scalar)
-        quantise_z(2, (on_vector, on_vector))
-        quantise_z(3, (on_vector, on_vector))
+        round_loss(opened[0], 3, 0, nc.vector.tensor_copy)
+        round_loss(opened[1], 3, 1, nc.scalar.copy)
+        round_loss(opened[2], 3, 2, nc.scalar.copy)
+        round_loss(opened[3], 3, 3, nc.scalar.copy)
+        quantise_z(0, nc.vector.tensor_copy)
+        quantise_z(1, nc.vector.tensor_copy)
         pressure(0, (1, 1))
+        quantise_z(2, nc.vector.tensor_copy)
         pressure(1, (1, 1))
-        quantise_z(4, (on_vector, on_vector))
-        pressure(2, (1, 1, 1, 1))
-        pressure(3, (1, 1, 1, 1), (1, 3))
-        pressure(4, (1, 1, 1, 1), (1, 3))
+        quantise_z(3, nc.vector.tensor_copy)
+        pressure(2, (1, 1, 2))
+        quantise_z(4, nc.vector.tensor_copy)
+        pressure(3, (2, 2), (1, 3))
+        pressure(4, (2, 2), (1, 3))

@@ -98,7 +98,7 @@ def tile_list_particle_cell_pressure_kernel(
                 v_sc[QUADRANT * q : QUADRANT * q + both_planes, :].bitcast(I32),
                 picked_sc[both_planes * q : both_planes * (q + 1), :].bitcast(I32),
             )
-        pages = [keep.tile([P, T2], F32, name="page%d" % t) for t in range(2)]
+        pages = [keep.tile([P, T2], F32, name="page%d" % t) for t in range(SLICES)]
         ident = keep.tile([P, P], F32, name="ident")
         pools.append(ctx.enter_context(tc.tile_pool(name="late", bufs=1)))
         load_w(0, ((0, 0), (1, 0), (0, 1), (1, 1)))
@@ -106,8 +106,8 @@ def tile_list_particle_cell_pressure_kernel(
         load_w(1, BY_PASS)
         wgs_raw.append(load_wgs(1))
         load_w(2, BY_PASS)
-        load_old(0, 0, T2 // 2)
         load_w(3, BY_PASS)
+        load_old(0, 0, T2 // 2)
         load_old(0, T2 // 2, T2)
         load_old(1)
         load_old(3)
@@ -163,7 +163,7 @@ def tile_list_particle_cell_pressure_kernel(
             nc.vector.tensor_tensor(
                 pages[t][:].indirect(idx2[:, j0 // LIST_GROUP : (j0 + width) // LIST_GROUP]),
                 speed,
-                neg_wgs[:, j0 : j0 + width],
+                neg_wgs[h][:, c0 : c0 + width],
                 MULT,
             )
 
@@ -241,8 +241,8 @@ def tile_list_particle_cell_pressure_kernel(
 
         first_words = [gather_words(0, 0, S, "v0"), gather_words(1, 0, BANK, "v1_0")]
         gather_words(1, BANK, PIECE, "v1_2")
-        for page in pages:
-            nc.vector.memset(page[:], 0.0)
+        for t in range(SLICES):
+            (nc.vector if t < 2 else nc.gpsimd).memset(pages[t][:], 0.0)
         acc_a, acc_b = bank(6), [bank(0), bank(1)]
         for m in range(2):
             for a in range(PASSES):
@@ -261,9 +261,9 @@ def tile_list_particle_cell_pressure_kernel(
                         stop=(a == PASSES - 1),
                     )
         gather_words(1, BANK + PIECE, PIECE, "w_first3")
-        neg_wgs = tile([P, S], F32, "neg_wgs")
+        neg_wgs = [tile([P, BANK], F32, "neg_wgs")]
         sq_a = square(acc_a[:], "sq0")
-        nc.scalar.activation(neg_wgs[:, 0:BANK], wgs_raw[0][:], ACT.Copy, scale=-1.0)
+        nc.scalar.activation(neg_wgs[0][:], wgs_raw[0][:], ACT.Copy, scale=-1.0)
         sq_b = [square(acc_b[k][:, 0:PIECE], ("sq_b", "sq1")[k]) for k in range(2)]
 
         totals = []
@@ -315,61 +315,63 @@ def tile_list_particle_cell_pressure_kernel(
             round_w(rest[:, k], 1, a, m, nc.scalar.copy)
         quantise_w(1, 0, lone[:].rearrange("p c i -> p (c i)"))
         quantise_w(1, P, rest[:].rearrange("p k c i -> p (k c i)"))
-        pages.append(tile([P, T2], F32, "sq_b"))
-        nc.gpsimd.memset(pages[2][:], 0.0)
         root(first[1][:], totals[1][:])
         scatter(0, PIECE, first[1][:])
+        neg_wgs.append(tile([P, BANK], F32, "total1"))
+        nc.vector.tensor_scalar(neg_wgs[1][:], wgs_raw[1][:], -1.0, None, MULT)
         total = sums(squares(acc, ("sq2", "total0")), 4)
-        nc.scalar.activation(neg_wgs[:, BANK:S], wgs_raw[1][:], ACT.Copy, scale=-1.0)
         acc = both(1, 0, (3, 4))
         scatter(0, BANK, rooted(total, "speed1")[:])
 
-        total = sums(squares(acc, ("sq2", "sq3")), 5)
+        round_pieces(2, BY_PASS[:3], tag="w_first0")
+        sq = [square(acc[0][:], "sq2")]
+        round_pieces(2, BY_PASS[3:])
+        sq.append(square(acc[1][:], "sq3"))
+        halves = [bank(6), bank(7)]
+        for k in range(2):
+            summed(sq[k], halves[k][:, 0:PIECE])
         acc = both(1, 1, (3, 4))
-        round_pieces(2, BY_PASS, tag="w_first0")
         quantise_slice(2)
-        pages.append(tile([P, T2], F32, "w_first0"))
-        nc.gpsimd.memset(pages[3][:], 0.0)
-        scatter(1, 0, rooted(total, "speed2")[:])
+        speed = tile([P, BANK], F32, "speed2")
+        for k in range(2):
+            root(speed[:, k * PIECE : (k + 1) * PIECE], halves[k][:, 0:PIECE])
+        scatter(1, 0, speed[:])
 
-        total = sums(squares(acc, ("sq2", "sq3")), 2)
-        acc = both(2, 0, (0, 1)) + both(2, 1, (6, 7))
-        round_pieces(3, BY_PASS, tag="w_first1")
+        def finish(n, total):
+            t, h = divmod(n, 2)
+            scatter(t, h * BANK, rooted(total, "speed%d" % (n % 3))[:])
+
+        total = sums(squares(acc, ("sq2", "sq3")), 5)
+        acc = both(2, 0, (0, 1)) + both(2, 1, (3, 4))
+        round_pieces(3, BY_PASS, tag="total0")
         quantise_slice(3)
-        scatter(1, BANK, rooted(total, "speed3")[:])
-
-        sq = squares(acc[:2], ("sq3", "sq4")) + squares(acc[2:], ("sq5", "sq6"))
-        totals = [sums(sq[:2], 4), sums(sq[2:], 0)]
-        speed = tile([P, S], F32, "speed45")
-        for h in range(2):
-            root(speed[:, h * BANK : (h + 1) * BANK], totals[h][:])
-        scatter(2, 0, speed[:])
-        loss(0, 0, 5)
-        loss(0, 1, 3)
-        loss(0, 2, 2)
-        loss(0, 3, 1)
-        total = sums(squares(both(3, 0, (6, 7)), ("sq3", "sq4")), 4)
-        scatter(3, 0, rooted(total, "speed6")[:])
-        loss(1, 0, 0)
-        loss(1, 1, 6)
-        acc = both(3, 1, (0, 6))
-        loss(1, 2, 7)
-        loss(1, 3, 4)
-        total = sums(squares(acc, ("sq3", "sq4")), 7)
-        scatter(3, BANK, rooted(total, "speed7")[:])
-        opened = [open_loss(3, g, b) for g, b in enumerate((5, 3, 2, 1))]
-        for g, b in enumerate((4, 0, 6, 7)):
+        finish(3, total)
+        finish(4, sums(squares(acc[:2], ("sq4", "sq5")), 2))
+        total = sums(squares(acc[2:], ("sq2", "sq3")), 5)
+        acc = both(3, 0, (3, 4))
+        finish(5, total)
+        for g, b in enumerate((6, 7, 0, 1)):
+            loss(0, g, b)
+        finish(6, sums(squares(acc, ("sq4", "sq5")), 2))
+        loss(1, 0, 6)
+        loss(1, 1, 7)
+        acc = both(3, 1, (6, 7))
+        loss(1, 2, 5)
+        finish(7, sums(squares(acc, ("sq2", "sq3")), 3))
+        loss(1, 3, 2)
+        opened = [open_loss(3, g, b) for g, b in enumerate((0, 1, 4, 5))]
+        for g, b in enumerate((6, 7, 2, 3)):
             loss(2, g, b)
 
         z_q = {}
-        word_banks = [4, 0, 6, 7] * 2
-        out_banks = [5, 3, 2, 1] * 3 + [4, 0, 6, 7]
+        word_banks = [6, 7, 2, 3] * 2
+        out_banks = [0, 1, 4, 5] * 3 + [6, 7, 2, 3]
         spare = ["old0", "old1", "res_a", "res_b", "w_raw3_1_1", "w_raw3_1_0", "w_raw3_0_1", "w_raw3_0_0", "w_raw2_1_1", "w_raw2_1_0", "old2"]
 
         def quantise_z(q, copy):
             b0, nb = CHUNKS[q]
             words = z_t[q][:].rearrange("c cb u p e -> c (cb u p e)").bitcast(F32)
-            z_bf = tile([P, nb * P, PACK], BF16, ("w_raw1_0_0", "w_raw1_0_1", "speed45", "w_first1", "neg_wgs")[q])
+            z_bf = tile([P, nb * P, PACK], BF16, ("w_raw1_0_0", "w_raw1_0_1", "total0", "v0", "z_bf4")[q])
             z_words = z_bf[:].rearrange("p c i -> p (c i)").bitcast(F32)
             for d in range(nb // 2):
                 turned = bank(word_banks.pop(0))

@@ -234,10 +234,12 @@ def tile_list_particle_cell_pressure_kernel(
                 )
                 c0 = c0 + nb * P
 
-        def loss(t, g, b):
-            acc = open_loss(t, g, b)
+        def close_loss(acc, t, g):
             turn_into(acc, pages[t], g, False)
             round_loss(acc, t, g, nc.scalar.copy)
+
+        def loss(t, g, b):
+            close_loss(open_loss(t, g, b), t, g)
 
         first_words = [gather_words(0, 0, S, "v0"), gather_words(1, 0, BANK, "v1_0")]
         gather_words(1, BANK, PIECE, "v1_2")
@@ -261,6 +263,10 @@ def tile_list_particle_cell_pressure_kernel(
                         stop=(a == PASSES - 1),
                     )
         gather_words(1, BANK + PIECE, PIECE, "w_first3")
+        pair = tile([P, 2, P, PACK], BF16, "w_pair")
+        for m in range(2):
+            round_w(pair[:, m], 1, 0, m, nc.vector.tensor_copy)
+        quantise_w(1, 0, pair[:].rearrange("p m c i -> p (m c i)"))
         neg_wgs = [tile([P, BANK], F32, "neg_wgs")]
         sq_a = square(acc_a[:], "sq0")
         nc.scalar.activation(neg_wgs[0][:], wgs_raw[0][:], ACT.Copy, scale=-1.0)
@@ -308,13 +314,12 @@ def tile_list_particle_cell_pressure_kernel(
             return acc
 
         lone = tile([P, P, PACK], BF16, "sq1")
-        round_w(lone[:], 1, 0, 0, nc.vector.tensor_copy)
+        round_w(lone[:], 1, 1, 0, nc.vector.tensor_copy)
         scatter(0, 0, first[0][:])
-        rest = tile([P, 3, P, PACK], BF16, "sq_b")
-        for k, (a, m) in enumerate(BY_PASS[1:]):
-            round_w(rest[:, k], 1, a, m, nc.scalar.copy)
-        quantise_w(1, 0, lone[:].rearrange("p c i -> p (c i)"))
-        quantise_w(1, P, rest[:].rearrange("p k c i -> p (k c i)"))
+        rest = tile([P, P, PACK], BF16, "sq_b")
+        round_w(rest[:], 1, 1, 1, nc.scalar.copy)
+        quantise_w(1, 2 * P, lone[:].rearrange("p c i -> p (c i)"))
+        quantise_w(1, 3 * P, rest[:].rearrange("p c i -> p (c i)"))
         root(first[1][:], totals[1][:])
         scatter(0, PIECE, first[1][:])
         neg_wgs.append(tile([P, BANK], F32, "total1"))
@@ -339,33 +344,36 @@ def tile_list_particle_cell_pressure_kernel(
 
         def finish(n, total):
             t, h = divmod(n, 2)
-            scatter(t, h * BANK, rooted(total, "speed%d" % (n % 3))[:])
+            scatter(t, h * BANK, rooted(total, "speed%d" % (n % 4))[:])
 
         total = sums(squares(acc, ("sq2", "sq3")), 5)
+        waiting = [open_loss(0, g, 6 + g) for g in range(2)]
         acc = both(2, 0, (0, 1)) + both(2, 1, (3, 4))
         round_pieces(3, BY_PASS, tag="total0")
         quantise_slice(3)
         finish(3, total)
         finish(4, sums(squares(acc[:2], ("sq4", "sq5")), 2))
-        total = sums(squares(acc[2:], ("sq2", "sq3")), 5)
-        acc = both(3, 0, (3, 4))
-        finish(5, total)
-        for g, b in enumerate((6, 7, 0, 1)):
-            loss(0, g, b)
-        finish(6, sums(squares(acc, ("sq4", "sq5")), 2))
+        later = squares(acc[2:], ("sq2", "sq3"))
+        finish(6, sums(squares(both(3, 0, (3, 4)), ("sq4", "sq5")), 5))
+        for g in range(2):
+            close_loss(waiting[g], 0, g)
+        loss(0, 2, 0)
+        loss(0, 3, 1)
+        finish(5, sums(later, 5))
         loss(1, 0, 6)
         loss(1, 1, 7)
         acc = both(3, 1, (6, 7))
-        loss(1, 2, 5)
-        finish(7, sums(squares(acc, ("sq2", "sq3")), 3))
-        loss(1, 3, 2)
-        opened = [open_loss(3, g, b) for g, b in enumerate((0, 1, 4, 5))]
-        for g, b in enumerate((6, 7, 2, 3)):
-            loss(2, g, b)
+        loss(1, 2, 2)
+        finish(7, sums(squares(acc, ("sq4", "sq5")), 3))
+        loss(1, 3, 5)
+        opened = [open_loss(3, g, b) for g, b in enumerate((0, 1, 4, 2))]
+        waiting = [open_loss(2, g, b) for g, b in enumerate((6, 7, 5, 3))]
+        for g in range(len(GROUPS)):
+            close_loss(waiting[g], 2, g)
 
         z_q = {}
-        word_banks = [6, 7, 2, 3] * 2
-        out_banks = [0, 1, 4, 5] * 3 + [6, 7, 2, 3]
+        word_banks = [6, 7, 5, 3] * 2
+        out_banks = [0, 1, 4, 2] * 3 + [6, 7, 5, 3]
         spare = ["old0", "old1", "res_a", "res_b", "w_raw3_1_1", "w_raw3_1_0", "w_raw3_0_1", "w_raw3_0_0", "w_raw2_1_1", "w_raw2_1_0", "old2"]
 
         def quantise_z(q, copy):

@@ -371,6 +371,18 @@ def tile_list_particle_cell_pressure_kernel(
         for g in range(len(GROUPS)):
             close_loss(waiting[g], 2, g)
 
+        warm = bank(6)
+        for k in range(4):
+            nc.tensor.matmul_mx(
+                out=warm[:],
+                lhsT=wp_w[:, 0 : 2 * P].bitcast(FP4X4),
+                lhsT_scale=wp_sc[:, 0:P],
+                rhs=codes[3][:].bitcast(FP8X4),
+                rhs_scale=scales[3][:],
+                start=True,
+                stop=True,
+            )
+
         z_q = {}
         word_banks = [6, 7, 5, 3] * 2
         out_banks = [0, 1, 4, 2] * 3 + [6, 7, 5, 3]

@@ -106,11 +106,12 @@ def tile_list_particle_cell_pressure_kernel(
         load_w(1, BY_PASS)
         wgs_raw.append(load_wgs(1))
         load_w(2, BY_PASS)
+        load_old(3, 0, T2 // 2)
         load_w(3, BY_PASS)
         load_old(0, 0, T2 // 2)
         load_old(0, T2 // 2, T2)
         load_old(1)
-        load_old(3)
+        load_old(3, T2 // 2, T2)
         load_old(2)
 
         one = keep.tile([P, 8], F32, name="one")
@@ -342,50 +343,63 @@ def tile_list_particle_cell_pressure_kernel(
             root(speed[:, k * PIECE : (k + 1) * PIECE], halves[k][:, 0:PIECE])
         scatter(1, 0, speed[:])
 
+        def warm_up(b, passes):
+            warm = bank(b)
+            for k in range(passes):
+                nc.tensor.matmul_mx(
+                    out=warm[:],
+                    lhsT=wp_w[:, 0 : 2 * P].bitcast(FP4X4),
+                    lhsT_scale=wp_sc[:, 0:P],
+                    rhs=codes[3][:].bitcast(FP8X4),
+                    rhs_scale=scales[3][:],
+                    start=True,
+                    stop=True,
+                )
+
         def finish(n, total):
             t, h = divmod(n, 2)
             scatter(t, h * BANK, rooted(total, "speed%d" % (n % 4))[:])
 
         total = sums(squares(acc, ("sq2", "sq3")), 5)
         waiting = [open_loss(0, g, 6 + g) for g in range(2)]
-        acc = both(2, 0, (0, 1)) + both(2, 1, (3, 4))
+        opened = [open_loss(3, g, g) for g in range(2)]
+        acc = products(2, 0, bank(3))
         round_pieces(3, BY_PASS, tag="total0")
         quantise_slice(3)
         finish(3, total)
-        finish(4, sums(squares(acc[:2], ("sq4", "sq5")), 2))
-        later = squares(acc[2:], ("sq2", "sq3"))
-        finish(6, sums(squares(both(3, 0, (3, 4)), ("sq4", "sq5")), 5))
         for g in range(2):
-            close_loss(waiting[g], 0, g)
-        loss(0, 2, 0)
-        loss(0, 3, 1)
-        finish(5, sums(later, 5))
-        loss(1, 0, 6)
-        loss(1, 1, 7)
-        acc = both(3, 1, (6, 7))
-        loss(1, 2, 2)
-        finish(7, sums(squares(acc, ("sq4", "sq5")), 3))
-        loss(1, 3, 5)
-        opened = [open_loss(3, g, b) for g, b in enumerate((0, 1, 4, 2))]
-        waiting = [open_loss(2, g, b) for g, b in enumerate((6, 7, 5, 3))]
-        for g in range(len(GROUPS)):
+            turn_into(waiting[g], pages[0], g, False)
+        losses = [(0, 2), (0, 3), (1, 0), (1, 1), (1, 2), (1, 3)]
+        order = (4, 6, 5, 7)
+        for place, n in enumerate(order):
+            t, h = divmod(n, 2)
+            after = products(t, 2 * h + 1, bank(4))
+            total = bank((2, 5)[place % 2])
+            summed(square(acc[:], "sq4"), total[:, 0:PIECE])
+            if place == 0:
+                for g in range(2):
+                    round_loss(waiting[g], 0, g, nc.scalar.copy)
+            else:
+                loss(*losses.pop(0), 7)
+            if place + 1 < len(order):
+                following = order[place + 1]
+                acc = products(following // 2, 2 * (following % 2), bank(3))
+            summed(square(after[:], "sq5"), total[:, PIECE:BANK])
+            finish(n, total)
+            if losses:
+                loss(*losses.pop(0), 6)
+        opened = opened + [open_loss(3, 2, 2), open_loss(3, 3, 6)]
+        warm_up(3, 1)
+        waiting = [open_loss(2, g, b) for g, b in enumerate((3, 4, 7))]
+        warm_up(5, 1)
+        for g in range(3):
             close_loss(waiting[g], 2, g)
-
-        warm = bank(6)
-        for k in range(4):
-            nc.tensor.matmul_mx(
-                out=warm[:],
-                lhsT=wp_w[:, 0 : 2 * P].bitcast(FP4X4),
-                lhsT_scale=wp_sc[:, 0:P],
-                rhs=codes[3][:].bitcast(FP8X4),
-                rhs_scale=scales[3][:],
-                start=True,
-                stop=True,
-            )
+        loss(2, 3, 5)
+        warm_up(3, 2)
 
         z_q = {}
-        word_banks = [6, 7, 5, 3] * 2
-        out_banks = [0, 1, 4, 2] * 3 + [6, 7, 5, 3]
+        word_banks = [3, 4, 7, 5] * 2
+        out_banks = [0, 1, 2, 6] * 3 + [3, 4, 7, 5]
         spare = ["old0", "old1", "res_a", "res_b", "w_raw3_1_1", "w_raw3_1_0", "w_raw3_0_1", "w_raw3_0_0", "w_raw2_1_1", "w_raw2_1_0", "old2"]
 
         def quantise_z(q, copy):

@@ -106,9 +106,9 @@ def tile_list_particle_cell_pressure_kernel(
         load_w(1, BY_PASS)
         wgs_raw.append(load_wgs(1))
         load_w(2, BY_PASS)
+        load_old(0, 0, T2 // 2)
         load_old(3, 0, T2 // 2)
         load_w(3, BY_PASS)
-        load_old(0, 0, T2 // 2)
         load_old(0, T2 // 2, T2)
         load_old(1)
         load_old(3, T2 // 2, T2)

@@ -400,19 +400,19 @@ def tile_list_particle_cell_pressure_kernel(
         z_q = {}
         word_banks = [3, 4, 7, 5] * 2
         out_banks = [0, 1, 2, 6] * 3 + [3, 4, 7, 5]
-        spare = ["old0", "old1", "res_a", "res_b", "w_raw3_1_1", "w_raw3_1_0", "w_raw3_0_1", "w_raw3_0_0", "w_raw2_1_1", "w_raw2_1_0", "old2"]
+        spare = ["old0", "old1", "res_a", "sq4", "sq5", "sq3", "w_raw3_1_1", "w_raw3_1_0", "w_raw3_0_1", "w_raw3_0_0", "w_raw2_1_1", "w_raw2_1_0", "old2"]
 
-        def quantise_z(q, copy):
+        def quantise_z(q, *copies):
             b0, nb = CHUNKS[q]
             words = z_t[q][:].rearrange("c cb u p e -> c (cb u p e)").bitcast(F32)
-            z_bf = tile([P, nb * P, PACK], BF16, ("w_raw1_0_0", "w_raw1_0_1", "total0", "v0", "z_bf4")[q])
+            z_bf = tile([P, nb * P, PACK], BF16, ("total0", "w_raw1_0_1", "total0", "v0", "z_bf4")[q])
             z_words = z_bf[:].rearrange("p c i -> p (c i)").bitcast(F32)
             for d in range(nb // 2):
                 turned = bank(word_banks.pop(0))
                 for k in range(4):
                     w0 = d * BANK + k * P
                     nc.tensor.transpose(turned[:, k * P : (k + 1) * P], words[:, w0 : w0 + P], ident[:])
-                copy(
+                copies[d](
                     z_words[:, d * BANK : (d + 1) * BANK].rearrange("p (cb c u) -> p cb c u", cb=2, u=2),
                     turned[:].rearrange("p (cb u c) -> p cb c u", cb=2, u=2),
                 )
@@ -452,17 +452,18 @@ def tile_list_particle_cell_pressure_kernel(
 
         for g in range(len(GROUPS)):
             turn_into(opened[g], pages[3], g, False)
-        round_loss(opened[0], 3, 0, nc.vector.tensor_copy)
-        round_loss(opened[1], 3, 1, nc.scalar.copy)
-        round_loss(opened[2], 3, 2, nc.scalar.copy)
-        round_loss(opened[3], 3, 3, nc.scalar.copy)
-        quantise_z(0, nc.vector.tensor_copy)
-        quantise_z(1, nc.vector.tensor_copy)
+        on_vector, on_scalar = nc.vector.tensor_copy, nc.scalar.copy
+        round_loss(opened[0], 3, 0, on_vector)
+        round_loss(opened[1], 3, 1, on_scalar)
+        round_loss(opened[2], 3, 2, on_scalar)
+        quantise_z(0, on_vector)
+        quantise_z(1, on_scalar)
+        round_loss(opened[3], 3, 3, on_scalar)
+        quantise_z(2, on_vector, on_scalar)
         pressure(0, (1, 1))
-        quantise_z(2, nc.vector.tensor_copy)
         pressure(1, (1, 1))
-        quantise_z(3, nc.vector.tensor_copy)
-        pressure(2, (1, 1, 2))
-        quantise_z(4, nc.vector.tensor_copy)
-        pressure(3, (2, 2), (1, 3))
+        quantise_z(3, on_vector, on_vector)
+        pressure(2, (1, 1, 1, 1))
+        quantise_z(4, on_vector, on_vector)
+        pressure(3, (1, 1, 2), (2, 3))
         pressure(4, (2, 2), (1, 3))

from contextlib import ExitStack

import concourse.mybir as mybir
from concourse.masks import make_identity

K, T, S, H, T2, N, P = 1024, 4096, 1024, 512, 2048, 512, 128
FLOPS = 2 * (2 * K * H * S + H * N * T2)

F32 = mybir.dt.float32
BF16 = mybir.dt.bfloat16
I32 = mybir.dt.int32
U32 = mybir.dt.uint32
U16 = mybir.dt.uint16
U8 = mybir.dt.uint8
FP8X4 = mybir.dt.float8_e4m3fn_x4
FP4X4 = mybir.dt.float4_e2m1fn_x4
ACT = mybir.ActivationFunctionType
MULT = mybir.AluOpType.mult
ADD = mybir.AluOpType.add

PACK = 4
PASSES = K // (P * PACK)
SLICES = H // P
BANK = 512
PIECE = BANK // 2
QUADRANT = 32
PLANE_ROWS = 4
LIST_GROUP = 16
NEIGHBOURS = 4
CHUNKS = ((0, 2), (2, 2), (4, 4), (8, 4), (12, 4))
GROUPS = ((0, 1), (2,), (3,), (4,))


def tile_list_particle_cell_pressure_kernel(
    tc, tab_words, tab_scales, offs, wx, wy, wgs, offs2, old, wp_words, wp_scales, out
):
    nc = tc.nc
    with ExitStack() as ctx:
        keep = ctx.enter_context(tc.tile_pool(name="keep", bufs=1))
        psum = ctx.enter_context(tc.psum_pool(name="psum", bufs=1))

        def bank(b):
            return psum.tile([P, BANK], F32, name="bank%d" % b, tag="bank%d" % b)

        def tile(shape, dtype, tag):
            return pools[-1].tile(shape, dtype, name=tag, tag=tag, align_bytes=64)

        pools = [keep]

        idx = keep.tile([P, S // LIST_GROUP], U16, name="idx")
        idx2 = keep.tile([P, S // LIST_GROUP], U16, name="idx2")
        tab = [tile([P, T], I32, "tab%d" % a) for a in range(PASSES)]
        w_raw = {}
        old_sb = {}

        def load_table(a, c0, c1):
            words = tab_words[a].rearrange("p t i -> p (t i)").bitcast(I32)
            nc.sync.dma_start(tab[a][:, c0:c1], words[:, c0:c1])

        def load_w(t, order):
            for a, m in order:
                raw = tile([P, PACK, P], F32, "w_raw%d_%d_%d" % (t, a, m))
                rows = (wx, wy)[m][a * P * PACK : (a + 1) * P * PACK, t * P : (t + 1) * P]
                nc.sync.dma_start(raw[:], rows.rearrange("(p i) c -> p i c", i=PACK))
                w_raw[t, a, m] = raw

        def load_old(t, c0=0, c1=T2):
            if c0 == 0:
                old_sb[t] = tile([P, T2], F32, "old%d" % t)
            nc.sync.dma_start(old_sb[t][:, c0:c1], old[t * P : (t + 1) * P, c0:c1])

        def load_wgs(h):
            raw = tile([P, BANK], F32, "wgs%d" % h)
            nc.sync.dma_start(raw[:], wgs[:, h * BANK : (h + 1) * BANK])
            return raw

        BY_PASS = ((0, 0), (0, 1), (1, 0), (1, 1))
        picked_sc = tile([P, S], U8, "picked_sc")
        v_sc = tile([P, S], U8, "v_sc")
        both_planes = PASSES * PLANE_ROWS
        with tc.tile_pool(name="early", bufs=1) as early:
            tab_sc = early.tile([P, T], U8, name="tab_sc", align_bytes=64)
            nc.sync.dma_start(idx[:], offs)
            nc.sync.dma_start(idx2[:], offs2)
            for r in range(PLANE_ROWS):
                nc.sync.dma_start(
                    tab_sc[r:QUADRANT:PLANE_ROWS, :].bitcast(I32),
                    tab_scales.rearrange("a (q r) t -> r q a t", r=PLANE_ROWS)[r].bitcast(I32),
                )
            for a in range(PASSES):
                load_table(a, 0, T)
            nc.vector.memset(tab_sc[QUADRANT : P // 2, :].bitcast(I32), 0)
            nc.vector.memset(tab_sc[P // 2 : P, :].bitcast(I32), 0)
            nc.gpsimd.memset(v_sc[:].bitcast(I32), 0)
            nc.vector.tensor_copy(picked_sc[:], tab_sc[:].indirect(idx[:]))
        for q in range(P // QUADRANT):
            nc.sync.dma_start(
                v_sc[QUADRANT * q : QUADRANT * q + both_planes, :].bitcast(I32),
                picked_sc[both_planes * q : both_planes * (q + 1), :].bitcast(I32),
            )
        pages = [keep.tile([P, T2], F32, name="page%d" % t) for t in range(SLICES)]
        ident = keep.tile([P, P], F32, name="ident")
        pools.append(ctx.enter_context(tc.tile_pool(name="late", bufs=1)))
        load_w(0, ((0, 0), (1, 0), (0, 1), (1, 1)))
        wgs_raw = [load_wgs(0)]
        load_w(1, BY_PASS)
        wgs_raw.append(load_wgs(1))
        load_w(2, BY_PASS)
        load_old(0, 0, T2 // 2)
        load_old(3, 0, T2 // 2)
        load_w(3, BY_PASS)
        load_old(0, T2 // 2, T2)
        load_old(1)
        load_old(3, T2 // 2, T2)
        load_old(2)

        one = keep.tile([P, 8], F32, name="one")
        nc.gpsimd.memset(one[:], 1.0)
        preload = keep.tile([P, 8], F32, name="preload")
        nc.scalar.activation(preload[:], one[:], ACT.Sqrt)
        make_identity(nc, ident[:])
        wp_sc = tile([P, N], U8, "wp_sc")
        nc.gpsimd.memset(wp_sc[:].bitcast(I32), 0)
        wp_w = tile([P, 2 * N], U8, "wp_w")
        nc.sync.dma_start(wp_w[:].bitcast(I32), wp_words[0].bitcast(I32))
        for q in range(P // QUADRANT):
            nc.sync.dma_start(
                wp_sc[QUADRANT * q : QUADRANT * q + PLANE_ROWS, :].bitcast(I32),
                wp_scales[0, PLANE_ROWS * q : PLANE_ROWS * (q + 1), :].bitcast(I32),
            )


        v_w = {}

        def gather_words(a, j0, width, tag):
            words = tile([P, width], U32, tag)
            entries = idx[:, j0 // LIST_GROUP : (j0 + width) // LIST_GROUP]
            nc.vector.tensor_copy(words[:], tab[a][:].bitcast(U32).indirect(entries))
            for j in range(j0, j0 + width, PIECE):
                v_w[a, j // PIECE] = words[:, j - j0 : j - j0 + PIECE]
            return words

        def plane(a, j0, width):
            return v_sc[PLANE_ROWS * a : P, j0 : j0 + width]

        codes = [tile([P, PASSES * 2 * P], U32, "w_codes%d" % t) for t in range(SLICES)]
        scales = [tile([P, PASSES * 2 * P], U8, "w_scales%d" % t) for t in range(SLICES)]

        def round_w(dst, t, a, m, copy):
            copy(
                dst.rearrange("p (g c) i -> p g i c", c=NEIGHBOURS),
                w_raw[t, a, m][:].rearrange("p i (g c) -> p g i c", c=NEIGHBOURS),
            )

        def quantise_w(t, c0, src):
            width = src.shape[1] // PACK
            nc.vector.quantize_mx(
                out=codes[t][:, c0 : c0 + width].bitcast(FP8X4), scales=scales[t][:, c0 : c0 + width], in_=src
            )

        def scatter(t, j0, speed):
            width = speed.shape[1]
            h, c0 = divmod(j0, BANK)
            nc.vector.tensor_tensor(
                pages[t][:].indirect(idx2[:, j0 // LIST_GROUP : (j0 + width) // LIST_GROUP]),
                speed,
                neg_wgs[h][:, c0 : c0 + width],
                MULT,
            )

        def products(t, k, acc, passes=range(PASSES)):
            for a in passes:
                cols = slice(a * 2 * P, (a + 1) * 2 * P)
                for e in range(2):
                    j0 = k * PIECE + e * P
                    nc.tensor.matmul_mx(
                        out=acc[:, e * 2 * P : (e + 1) * 2 * P],
                        lhsT=v_w[a, k][:, e * P : (e + 1) * P].bitcast(FP8X4),
                        lhsT_scale=plane(a, j0, P),
                        rhs=codes[t][:, cols].bitcast(FP8X4),
                        rhs_scale=scales[t][:, cols],
                        start=(a == 0 and e == 0),
                        stop=(a == PASSES - 1 and e == 1),
                    )
            return acc

        def square(acc, tag):
            sq = tile([P, acc.shape[1]], F32, tag)
            nc.scalar.activation(sq[:], acc, ACT.Square)
            return sq

        def summed(sq, total):
            for e in range(2):
                for m in range(2):
                    c0 = (2 * e + m) * P
                    nc.tensor.matmul(
                        total[:, e * P : (e + 1) * P],
                        sq[:, c0 : c0 + P],
                        ident[:],
                        start=(m == 0),
                        stop=(m == 1),
                        is_transpose=True,
                    )

        def root(dst, total):
            nc.scalar.activation(dst, total, ACT.Sqrt)

        z_t = [keep.tile([P, nb, 2, P, 2], BF16, name="z_t%d" % q) for q, (b0, nb) in enumerate(CHUNKS)]

        def turn_into(acc, src, g, first):
            blocks = [b for q in GROUPS[g] for b in range(CHUNKS[q][0], CHUNKS[q][0] + CHUNKS[q][1])]
            for k, b in enumerate(blocks):
                nc.tensor.matmul(
                    acc[:, k * P : (k + 1) * P],
                    src[:, b * P : (b + 1) * P],
                    ident[:],
                    start=(first and k == 0),
                    stop=(not first and k == len(blocks) - 1),
                    is_transpose=True,
                )

        def open_loss(t, g, b):
            acc = bank(b)
            turn_into(acc, old_sb[t], g, True)
            return acc

        def round_loss(acc, t, g, copy):
            words = P // PACK
            c0 = 0
            for q in GROUPS[g]:
                nb = CHUNKS[q][1]
                copy(
                    z_t[q][:, :, :, words * t : words * (t + 1), :],
                    acc[:, c0 : c0 + nb * P].rearrange("c (cb p u e) -> c cb u p e", cb=nb, u=2, e=2),
                )
                c0 = c0 + nb * P

        def close_loss(acc, t, g):
            turn_into(acc, pages[t], g, False)
            round_loss(acc, t, g, nc.scalar.copy)

        def loss(t, g, b):
            close_loss(open_loss(t, g, b), t, g)

        first_words = [gather_words(0, 0, S, "v0"), gather_words(1, 0, BANK, "v1_0")]
        gather_words(1, BANK, PIECE, "v1_2")
        for t in range(SLICES):
            (nc.vector if t < 2 else nc.gpsimd).memset(pages[t][:], 0.0)
        acc_a, acc_b = bank(6), [bank(0), bank(1)]
        for m in range(2):
            for a in range(PASSES):
                wb = tile([P, P, PACK], BF16, "w_first%d" % (2 * m + a))
                round_w(wb[:], 0, a, m, nc.vector.tensor_copy if (a, m) == (1, 1) else nc.scalar.copy)
                cols = slice((2 * a + m) * P, (2 * a + m + 1) * P)
                quantise_w(0, cols.start, wb[:].rearrange("p c i -> p (c i)"))
                for j0, width, dst in ((0, BANK, acc_a),) if m == 0 else ((0, PIECE, acc_b[0]), (PIECE, PIECE, acc_b[1])):
                    nc.tensor.matmul_mx(
                        out=dst[:, 0:width],
                        lhsT=codes[0][:, cols].bitcast(FP8X4),
                        lhsT_scale=scales[0][:, cols],
                        rhs=first_words[a][:, j0 : j0 + width].bitcast(FP8X4),
                        rhs_scale=plane(a, j0, width),
                        start=(a == 0),
                        stop=(a == PASSES - 1),
                    )
        gather_words(1, BANK + PIECE, PIECE, "w_first3")
        pair = tile([P, 2, P, PACK], BF16, "w_pair")
        for m in range(2):
            round_w(pair[:, m], 1, 0, m, nc.vector.tensor_copy)
        quantise_w(1, 0, pair[:].rearrange("p m c i -> p (m c i)"))
        neg_wgs = [tile([P, BANK], F32, "neg_wgs")]
        sq_a = square(acc_a[:], "sq0")
        nc.scalar.activation(neg_wgs[0][:], wgs_raw[0][:], ACT.Copy, scale=-1.0)
        sq_b = [square(acc_b[k][:, 0:PIECE], ("sq_b", "sq1")[k]) for k in range(2)]

        totals = []
        for k in range(2):
            totals.append(tile([P, PIECE], F32, "total%d" % k))
            nc.vector.tensor_tensor(totals[k][:], sq_a[:, k * PIECE : (k + 1) * PIECE], sq_b[k][:], ADD)
        acc = [products(0, 2, bank(2)), products(0, 3, bank(3))]
        first = [tile([P, PIECE], F32, "first%d" % k) for k in range(2)]
        root(first[0][:], totals[0][:])

        w_bf = {}

        def round_pieces(t, pieces, copy=nc.scalar.copy, tag=None):
            if tag:
                w_bf[t] = tile([P, PASSES, 2, P, PACK], BF16, tag)
            for a, m in pieces:
                round_w(w_bf[t][:, a, m], t, a, m, copy)

        def quantise_slice(t):
            quantise_w(t, 0, w_bf[t][:].rearrange("p a m c i -> p (a m c i)"))

        def squares(acc, tags):
            return [square(acc[k][:], tags[k]) for k in range(2)]

        def sums(sq, b):
            total = bank(b)
            for k in range(2):
                summed(sq[k], total[:, k * PIECE : (k + 1) * PIECE])
            return total

        def rooted(total, tag):
            speed = tile([P, BANK], F32, tag)
            root(speed[:], total[:])
            return speed

        def both(t, h, banks):
            return [products(t, 2 * h + k, bank(banks[k])) for k in range(2)]

        def closed(t, g, b):
            acc = open_loss(t, g, b)
            turn_into(acc, pages[t], g, False)
            return acc

        lone = tile([P, P, PACK], BF16, "sq1")
        round_w(lone[:], 1, 1, 0, nc.vector.tensor_copy)
        scatter(0, 0, first[0][:])
        rest = tile([P, P, PACK], BF16, "sq_b")
        round_w(rest[:], 1, 1, 1, nc.scalar.copy)
        quantise_w(1, 2 * P, lone[:].rearrange("p c i -> p (c i)"))
        quantise_w(1, 3 * P, rest[:].rearrange("p c i -> p (c i)"))
        root(first[1][:], totals[1][:])
        scatter(0, PIECE, first[1][:])
        neg_wgs.append(tile([P, BANK], F32, "total1"))
        nc.vector.tensor_scalar(neg_wgs[1][:], wgs_raw[1][:], -1.0, None, MULT)
        total = sums(squares(acc, ("sq2", "total0")), 4)
        acc = both(1, 0, (3, 4))
        scatter(0, BANK, rooted(total, "speed1")[:])

        round_pieces(2, BY_PASS[:3], tag="w_first0")
        sq = [square(acc[0][:], "sq2")]
        round_pieces(2, BY_PASS[3:])
        sq.append(square(acc[1][:], "sq3"))
        halves = [bank(6), bank(7)]
        for k in range(2):
            summed(sq[k], halves[k][:, 0:PIECE])
        acc = both(1, 1, (3, 4))
        quantise_slice(2)
        speed = tile([P, BANK], F32, "speed2")
        for k in range(2):
            root(speed[:, k * PIECE : (k + 1) * PIECE], halves[k][:, 0:PIECE])
        scatter(1, 0, speed[:])

        def warm_up(b, passes):
            warm = bank(b)
            for k in range(passes):
                nc.tensor.matmul_mx(
                    out=warm[:],
                    lhsT=wp_w[:, 0 : 2 * P].bitcast(FP4X4),
                    lhsT_scale=wp_sc[:, 0:P],
                    rhs=codes[3][:].bitcast(FP8X4),
                    rhs_scale=scales[3][:],
                    start=True,
                    stop=True,
                )

        def finish(n, total):
            t, h = divmod(n, 2)
            scatter(t, h * BANK, rooted(total, "speed%d" % (n % 4))[:])

        total = sums(squares(acc, ("sq2", "sq3")), 5)
        waiting = [open_loss(0, g, 6 + g) for g in range(2)]
        opened = [open_loss(3, g, g) for g in range(2)]
        acc = products(2, 0, bank(3))
        round_pieces(3, BY_PASS, tag="total0")
        quantise_slice(3)
        finish(3, total)
        for g in range(2):
            turn_into(waiting[g], pages[0], g, False)
        losses = [(0, 2), (0, 3), (1, 0), (1, 1), (1, 2), (1, 3)]
        order = (4, 6, 5, 7)
        for place, n in enumerate(order):
            t, h = divmod(n, 2)
            after = products(t, 2 * h + 1, bank(4))
            total = bank((2, 5)[place % 2])
            summed(square(acc[:], "sq4"), total[:, 0:PIECE])
            if place == 0:
                for g in range(2):
                    round_loss(waiting[g], 0, g, nc.scalar.copy)
            else:
                loss(*losses.pop(0), 7)
            if place + 1 < len(order):
                following = order[place + 1]
                acc = products(following // 2, 2 * (following % 2), bank(3))
            summed(square(after[:], "sq5"), total[:, PIECE:BANK])
            finish(n, total)
            if losses:
                loss(*losses.pop(0), 6)
        opened = opened + [open_loss(3, 2, 2), open_loss(3, 3, 6)]
        warm_up(3, 1)
        waiting = [open_loss(2, g, b) for g, b in enumerate((3, 4, 7))]
        warm_up(5, 1)
        for g in range(3):
            close_loss(waiting[g], 2, g)
        loss(2, 3, 5)
        warm_up(3, 2)

        z_q = {}
        word_banks = [3, 4, 7, 5] * 2
        out_banks = [0, 1, 2, 6] * 3 + [3, 4, 7, 5]
        spare = ["old0", "old1", "res_a", "sq4", "sq5", "sq3", "w_raw3_1_1", "w_raw3_1_0", "w_raw3_0_1", "w_raw3_0_0", "w_raw2_1_1", "w_raw2_1_0", "old2"]

        def quantise_z(q, *copies):
            b0, nb = CHUNKS[q]
            words = z_t[q][:].rearrange("c cb u p e -> c (cb u p e)").bitcast(F32)
            z_bf = tile([P, nb * P, PACK], BF16, ("total0", "w_raw1_0_1", "total0", "v0", "z_bf4")[q])
            z_words = z_bf[:].rearrange("p c i -> p (c i)").bitcast(F32)
            for d in range(nb // 2):
                turned = bank(word_banks.pop(0))
                for k in range(4):
                    w0 = d * BANK + k * P
                    nc.tensor.transpose(turned[:, k * P : (k + 1) * P], words[:, w0 : w0 + P], ident[:])
                copies[d](
                    z_words[:, d * BANK : (d + 1) * BANK].rearrange("p (cb c u) -> p cb c u", cb=2, u=2),
                    turned[:].rearrange("p (cb u c) -> p cb c u", cb=2, u=2),
                )
            z_codes = tile([P, nb * P], U32, "z_codes%d" % q)
            z_scales = tile([P, nb * P], U8, "z_scales%d" % q)
            nc.vector.quantize_mx(
                out=z_codes[:].bitcast(FP8X4), scales=z_scales[:], in_=z_bf[:].rearrange("p c i -> p (c i)")
            )
            z_q[q] = (z_codes, z_scales)

        def pressure(q, stores, on_vector=()):
            b0, nb = CHUNKS[q]
            width = nb * P
            per_bank = BANK // width
            z_codes, z_scales = z_q[q]
            n0 = 0
            for banks in stores:
                res = tile([P, banks * per_bank, width], F32, spare.pop())
                for s in range(banks):
                    acc = bank(out_banks.pop(0))
                    for k in range(per_bank):
                        n = n0 + s * per_bank + k
                        nc.tensor.matmul_mx(
                            out=acc[:, k * width : (k + 1) * width],
                            lhsT=wp_w[:, 2 * n * P : 2 * (n + 1) * P].bitcast(FP4X4),
                            lhsT_scale=wp_sc[:, n * P : (n + 1) * P],
                            rhs=z_codes[:].bitcast(FP8X4),
                            rhs_scale=z_scales[:],
                            start=True,
                            stop=True,
                        )
                    copy = nc.vector.tensor_copy if n0 + s in on_vector else nc.scalar.copy
                    copy(res[:, s * per_bank : (s + 1) * per_bank, :].rearrange("p k c -> p (k c)"), acc[:])
                rows = out[n0 * P : (n0 + banks * per_bank) * P, b0 * P : b0 * P + width]
                nc.sync.dma_start(rows.rearrange("(k p) c -> p k c", p=P), res[:])
                n0 = n0 + banks * per_bank

        for g in range(len(GROUPS)):
            turn_into(opened[g], pages[3], g, False)
        on_vector, on_scalar = nc.vector.tensor_copy, nc.scalar.copy
        round_loss(opened[0], 3, 0, on_vector)
        round_loss(opened[1], 3, 1, on_scalar)
        round_loss(opened[2], 3, 2, on_scalar)
        quantise_z(0, on_vector)
        quantise_z(1, on_scalar)
        round_loss(opened[3], 3, 3, on_scalar)
        quantise_z(2, on_vector, on_scalar)
        pressure(0, (1, 1))
        pressure(1, (1, 1))
        quantise_z(3, on_vector, on_vector)
        pressure(2, (1, 1, 1, 1))
        quantise_z(4, on_vector, on_vector)
        pressure(3, (1, 1, 2), (2, 3))
        pressure(4, (2, 2), (1, 3))
